import numpy as np
import ml_dtypes


def mxq(x, axis, fmt="e4m3"):
    dtype, down = {"e4m3": (ml_dtypes.float8_e4m3fn, 7), "e5m2": (ml_dtypes.float8_e5m2, 14)}[fmt]
    v = np.moveaxis(np.asarray(x, np.float32).astype(ml_dtypes.bfloat16).astype(np.float64), axis, -1)
    blocks = v.reshape(v.shape[:-1] + (-1, 32))
    amax = np.abs(blocks).max(-1, keepdims=True)
    byte = np.maximum(np.where(amax > 0, np.frexp(amax)[1] - 1 + 127, 0) - down, 1)
    scale = np.exp2(byte - 127.0)
    codes = (blocks / scale).astype(np.float32).astype(dtype).astype(np.float64)
    return np.moveaxis((codes * scale).reshape(v.shape), -1, axis)


WIDE = False


def mx_kscale(k):
    if not WIDE:
        return np.ones(k)
    levels = np.array([10, -10, 5, -5, 0])
    if k % 512:
        return np.exp2(np.random.permutation(np.resize(levels, k // 32))).repeat(32)
    a = np.empty((k // 512, 16))
    for p in range(k // 512):
        a[p, :8] = np.random.permutation(np.resize(levels, 8))
        for g in range(8):
            far = levels[np.abs(levels - a[p, g]) >= 10]
            a[p, g + 8] = far[np.random.randint(len(far))]
    return np.exp2(a.ravel()).repeat(32)


BF16 = ml_dtypes.bfloat16


def bf(x):
    return np.asarray(x, np.float32).astype(BF16)


def f64(x):
    return np.asarray(x).astype(np.float64)


V, H, B = 1024, 2048, 1024


def draw0():
    s, t = mx_kscale(V), mx_kscale(H)
    v = np.random.standard_normal((V, B)) * s[:, None]
    w = np.random.standard_normal((H, V)) / np.sqrt(V) / s * t[:, None]
    beta = (1 + 0.1 * np.random.standard_normal((H, 1))) / t[:, None]
    return {"v": bf(v), "w": bf(w), "beta": bf(beta)}


def core(v, w, beta):
    weights = f64(w)
    scale = f64(beta)
    a = mxq(weights, 1, "e4m3") @ mxq(f64(v), 0, "e4m3")
    h = scale * (1.0 / (1.0 + np.exp(-scale * a)))
    recon = mxq(weights, 0, "e4m3").T @ mxq(h, 0, "e4m3")
    return recon


def e4m3fn_bytes(y):
    return np.clip(np.asarray(y, np.float64), -448.0, 448.0).astype(np.float32).astype(ml_dtypes.float8_e4m3fn).view(np.uint8)


def e4m3fn_values(b):
    return np.asarray(b, np.uint8).view(ml_dtypes.float8_e4m3fn).astype(np.float64)


def setup_inputs():
    d = draw0()
    x0 = np.asarray(d['v']).astype(np.float64)
    s = (np.max(np.abs(x0), axis=(1,), keepdims=True) / 448.0).astype(np.float32)
    out = {}
    for k, v in d.items():
        if k == 'v':
            out['v_bytes'] = e4m3fn_bytes(x0 / s.astype(np.float64))
            out['v_scale'] = s
        else:
            out[k] = v
    return out


def reference(v_bytes, v_scale, w, beta):
    return core(e4m3fn_values(v_bytes) * v_scale.astype(np.float64), w, beta)

@@ -1,0 +1,226 @@
+from contextlib import ExitStack
+
+import concourse.mybir as mybir
+from concourse.masks import make_identity
+
+V, H, B = 1024, 2048, 1024
+FLOPS = 2 * 2 * H * V * B
+
+F32 = mybir.dt.float32
+BF16 = mybir.dt.bfloat16
+U32 = mybir.dt.uint32
+U8 = mybir.dt.uint8
+FP8 = mybir.dt.float8_e4m3fn
+FP8X4 = mybir.dt.float8_e4m3fn_x4
+ACT = mybir.ActivationFunctionType
+ALU = mybir.AluOpType
+
+P = 128
+T = 4
+KP = P * T
+NV = V // KP
+NH = H // KP
+HALF = 512
+NB = B // HALF
+NM = V // P
+
+ORDER = (
+    "T000P wid000S wid001S wid002S wid003S wid110S wid111S wid112S "
+    "wid113S wid010V wid011V wid012V wid013V vi01V vi00V wid100V "
+    "wid101V wid102V wid103V d00V vi11V vq00V T001P T010P "
+    "E010S T011P E011S E000S E001S d01S q101V d10V "
+    "q200V d21V vi10V T100P T101P T200P T201P T110P "
+    "E110S T111P E111S E200S E201S q120V vq10V T310P "
+    "T311P T300P E300S T301P E301S E100S E101S d11S "
+    "E310S E311S q130V q111V vq01V vq11V q110V d30V "
+    "q131V q210V q100V d20V q221V T210P E210S T211P "
+    "E211S q121V q201V M010P F010S M011P F011S M012P "
+    "F012S M013P F013S X01V M030P F030S M031P F031S "
+    "M032P F032S M033P F033S X03V M000P F000S M001P "
+    "F001S M002P F002S M003P F003S X00V q211V M020P "
+    "F020S M021P F021S M022P F022S M023P F023S X02V "
+    "hq01V hq00V hq03V M110P F110S M111P F111S M112P "
+    "F112S M113P F113S d31S q231V hq02V q230V q220V "
+    "M100P F100S M101P F101S M102P F102S M103P F103S "
+    "X10V X11V hq10V M120P M121P M122P M123P M130P "
+    "F130S M131P F131S M132P F132S M133P F133S F120S "
+    "F121S F122S F123S G120S G121S G122S G123S X12V "
+    "hq11V hq12V X13V hq13V N060P N061P N062P N063P "
+    "N050P N051P N052P N053P J05S J06S N000P N001P "
+    "N002P N003P N010P N011P N012P N013P J01S N040P "
+    "N041P N042P N043P N020P N021P N022P N023P N030P "
+    "N031P N032P N033P N070P N071P N072P N073P J07S "
+    "J02S J03S J04S N100P N101P N102P N170P N171P "
+    "N172P N140P N141P N142P N160P N161P N162P N130P "
+    "N131P N132P N133P J13S N143P J14S N173P J17S "
+    "N163P J16S N103P J10S J00S N120P N121P N122P "
+    "N150P N151P N152P N123P J12S N153P J15V N110P "
+    "N111P N112P N113P J11S "
+)
+
+
+def tile_rbm_mean_field_reconstruction_s7_kernel(tc, v_bytes, v_scale, w, beta, out):
+    nc = tc.nc
+    with ExitStack() as ctx:
+        keep = ctx.enter_context(tc.tile_pool(name="keep", bufs=1))
+        rot = ctx.enter_context(tc.tile_pool(name="rot", bufs=3))
+        psum = ctx.enter_context(tc.psum_pool(name="psum", bufs=8))
+
+        v_raw = [keep.tile([P, T, B], U8, name="v_raw%d" % c, align_bytes=64) for c in range(NV)]
+        w_sb = [keep.tile([P, T, V], BF16, name="w_sb%d" % g, align_bytes=64) for g in range(NH)]
+        vs = keep.tile([P, NV, T], F32, name="vs")
+        beta_bf = keep.tile([P, NH, T], BF16, name="beta_bf")
+        beta32 = keep.tile([P, NH, T], F32, name="beta32")
+        w_view = w.rearrange("(g p t) v -> g p t v", p=P, t=T)
+        v_view = v_bytes.rearrange("(c p t) n -> c p t n", p=P, t=T)
+
+        def load_w(g, a):
+            nc.sync.dma_start(out=w_sb[g][:, 2 * a : 2 * a + 2, :], in_=w_view[g][:, 2 * a : 2 * a + 2, :])
+
+        nc.scalar.dma_start(out=vs[:], in_=v_scale.rearrange("(c p t) o -> p c (t o)", p=P, t=T))
+        nc.sync.dma_start(out=v_raw[0][:, 0:2, :], in_=v_view[0][:, 0:2, :])
+        nc.sync.dma_start(out=v_raw[0][:, 2:4, :], in_=v_view[0][:, 2:4, :])
+        load_w(0, 0)
+        nc.sync.dma_start(out=v_raw[1][:], in_=v_view[1])
+        load_w(0, 1)
+        load_w(1, 0)
+        load_w(1, 1)
+        nc.sync.dma_start(out=beta_bf[:], in_=beta.rearrange("(g p t) o -> p g (t o)", p=P, t=T))
+        load_w(2, 0)
+        load_w(2, 1)
+        load_w(3, 0)
+        load_w(3, 1)
+
+        ident = keep.tile([P, P], F32, name="ident")
+        make_identity(nc, ident[:])
+        dummy = keep.tile([P, 1], F32, name="dummy")
+        nc.vector.memset(dummy[:], 0.0)
+        nc.scalar.activation(out=dummy[:], in_=dummy[:], func=ACT.Sigmoid)
+        nc.gpsimd.tensor_copy(out=beta32[:], in_=beta_bf[:])
+
+        v_codes = keep.tile([P, NV, B], U32, name="v_codes", align_bytes=64)
+        v_sc = keep.tile([P, NV, B], U8, name="v_sc", align_bytes=64)
+        wt_codes = keep.tile([P, NV, H], U32, name="wt_codes", align_bytes=64)
+        wt_sc = keep.tile([P, NV, H], U8, name="wt_sc", align_bytes=64)
+        w2_codes = keep.tile([P, NH, V], U32, name="w2_codes", align_bytes=64)
+        w2_sc = keep.tile([P, NH, V], U8, name="w2_sc", align_bytes=64)
+        h_codes = keep.tile([P, NH, B], U32, name="h_codes", align_bytes=64)
+        h_sc = keep.tile([P, NH, B], U8, name="h_sc", align_bytes=64)
+
+        def interleave(eng, dst, src):
+            o = dst.rearrange("p (c i) t -> p c t i", i=4)
+            s = src.rearrange("p t (c i) -> p c t i", i=4)
+            eng(out=o, in_=s)
+
+        live = {}
+
+        def cols_of(n):
+            return slice(n * HALF, (n + 1) * HALF)
+
+        def step(name, e):
+            k = name[0]
+            if name[:3] == "wid":
+                c, n, t = int(name[3]), int(name[4]), int(name[5])
+                if ("vf", c, n) not in live:
+                    v_flat = rot.tile([P, T, HALF], BF16, name="v_flat", tag="stage", align_bytes=64, bufs=14)
+                    live["vf", c, n] = v_flat
+                flat = live["vf", c, n]
+                src = v_raw[c][:, t, cols_of(n)].bitcast(FP8)
+                if e == "V":
+                    nc.vector.tensor_scalar(out=flat[:, t, :], in0=src, scalar1=vs[:, c, t : t + 1], scalar2=None, op0=ALU.mult)
+                else:
+                    nc.scalar.activation(out=flat[:, t, :], in_=src, func=ACT.Copy, scale=vs[:, c, t : t + 1])
+            elif name[:2] == "vi":
+                c, n = int(name[2]), int(name[3])
+                v_grp = rot.tile([P, HALF, T], BF16, name="v_grp", tag="stage", align_bytes=64, bufs=14)
+                live["vg", c, n] = v_grp
+                interleave(nc.vector.tensor_copy, v_grp[:], live["vf", c, n][:])
+            elif name[:2] == "vq":
+                c, n = int(name[2]), int(name[3])
+                nc.vector.quantize_mx(out=v_codes[:, c, cols_of(n)].bitcast(FP8X4), scales=v_sc[:, c, cols_of(n)], in_=live["vg", c, n][:].rearrange("p n t -> p (n t)"))
+            elif k == "T":
+                g, c, a = int(name[1]), int(name[2]), int(name[3])
+                bank = psum.tile([P, 512], F32, name="bank")
+                live["tb", g, c, a] = bank
+                for b in range(2):
+                    row = w_sb[g][:, 2 * a + b, :].bitcast(F32)
+                    for u in range(2):
+                        j = (2 * b + u) * P
+                        nc.tensor.transpose(bank[:, j : j + P], row[:, 256 * c + u : 256 * (c + 1) : 2], ident[:])
+            elif k == "E":
+                g, c, a = int(name[1]), int(name[2]), int(name[3])
+                if ("wt", g, c) not in live:
+                    wt_grp = rot.tile([P, KP, T], BF16, name="wt_grp", tag="stage", align_bytes=64, bufs=14)
+                    live["wt", g, c] = wt_grp
+                words = live["wt", g, c][:].rearrange("p m t -> p (m t)").bitcast(F32).rearrange("p (t m u) -> p t m u", t=T, u=2)
+                eng = nc.vector.tensor_copy if e == "V" else nc.scalar.copy
+                eng(out=words[:, 2 * a : 2 * a + 2], in_=live["tb", g, c, a][:].rearrange("p (t u m) -> p t m u", t=2, u=2))
+            elif name[:2] == "q1":
+                g, c = int(name[2]), int(name[3])
+                cols = slice(g * KP, (g + 1) * KP)
+                nc.vector.quantize_mx(out=wt_codes[:, c, cols].bitcast(FP8X4), scales=wt_sc[:, c, cols], in_=live["wt", g, c][:].rearrange("p m t -> p (m t)"))
+            elif k == "d":
+                g, a = int(name[1]), int(name[2])
+                w2_grp = rot.tile([P, HALF, T], BF16, name="w2_grp", tag="stage", align_bytes=64, bufs=14)
+                live["w2", g, a] = w2_grp
+                interleave(nc.scalar.copy if e == "S" else nc.vector.tensor_copy, w2_grp[:], w_sb[g][:, :, cols_of(a)])
+            elif name[:2] == "q2":
+                g, a = int(name[2]), int(name[3])
+                nc.vector.quantize_mx(out=w2_codes[:, g, cols_of(a)].bitcast(FP8X4), scales=w2_sc[:, g, cols_of(a)], in_=live["w2", g, a][:].rearrange("p m t -> p (m t)"))
+            elif k == "M":
+                n, g, t = int(name[1]), int(name[2]), int(name[3])
+                bank = psum.tile([P, 512], F32, name="bank")
+                live["mb", n, g, t] = bank
+                m = slice(g * KP + t * P, g * KP + (t + 1) * P)
+                for c in range(NV):
+                    nc.tensor.matmul_mx(out=bank[:], lhsT=wt_codes[:, c, m].bitcast(FP8X4), lhsT_scale=wt_sc[:, c, m],
+                                        rhs=v_codes[:, c, cols_of(n)].bitcast(FP8X4), rhs_scale=v_sc[:, c, cols_of(n)],
+                                        start=(c == 0), stop=(c == NV - 1))
+            elif k == "F":
+                n, g, t = int(name[1]), int(name[2]), int(name[3])
+                if ("sig", n, g) not in live:
+                    sig = rot.tile([P, T, HALF], F32, name="sig", align_bytes=64, bufs=5)
+                    live["sig", n, g] = sig
+                nc.scalar.activation(out=live["sig", n, g][:, t, :], in_=live["mb", n, g, t][:], func=ACT.Sigmoid, scale=beta32[:, g, t : t + 1])
+            elif k == "G":
+                n, g, t = int(name[1]), int(name[2]), int(name[3])
+                if ("hf", n, g) not in live:
+                    h_flat = rot.tile([P, T, HALF], BF16, name="h_flat", tag="stage", align_bytes=64, bufs=14)
+                    live["hf", n, g] = h_flat
+                nc.scalar.activation(out=live["hf", n, g][:, t, :], in_=live["sig", n, g][:, t, :], func=ACT.Copy, scale=beta32[:, g, t : t + 1])
+            elif k == "X" and ("hf", int(name[1]), int(name[2])) in live:
+                n, g = int(name[1]), int(name[2])
+                h_grp = rot.tile([P, HALF, T], BF16, name="h_grp", tag="stage", align_bytes=64, bufs=14)
+                live["h", n, g] = h_grp
+                interleave(nc.vector.tensor_copy, h_grp[:], live["hf", n, g][:])
+            elif k == "X":
+                n, g = int(name[1]), int(name[2])
+                h_grp = rot.tile([P, HALF, T], BF16, name="h_grp", tag="stage", align_bytes=64, bufs=14)
+                live["h", n, g] = h_grp
+                nc.vector.tensor_tensor(
+                    out=h_grp[:].rearrange("p (c i) t -> p c t i", i=4),
+                    in0=live["sig", n, g][:].rearrange("p t (c i) -> p c t i", i=4),
+                    in1=beta32[:, g, :].unsqueeze(1).unsqueeze(3).to_broadcast([P, HALF // 4, T, 4]),
+                    op=ALU.mult)
+            elif name[:2] == "hq":
+                n, g = int(name[2]), int(name[3])
+                nc.vector.quantize_mx(out=h_codes[:, g, cols_of(n)].bitcast(FP8X4), scales=h_sc[:, g, cols_of(n)], in_=live["h", n, g][:].rearrange("p n t -> p (n t)"))
+            elif k == "N":
+                n, m, g = int(name[1]), int(name[2]), int(name[3])
+                if g == 0:
+                    bank = psum.tile([P, 512], F32, name="bank")
+                    live["nb", n, m] = bank
+                mc = slice(m * P, (m + 1) * P)
+                nc.tensor.matmul_mx(out=live["nb", n, m][:], lhsT=w2_codes[:, g, mc].bitcast(FP8X4), lhsT_scale=w2_sc[:, g, mc],
+                                    rhs=h_codes[:, g, cols_of(n)].bitcast(FP8X4), rhs_scale=h_sc[:, g, cols_of(n)],
+                                    start=(g == 0), stop=(g == NH - 1))
+            elif k == "J":
+                n, m = int(name[1]), int(name[2])
+                res = rot.tile([P, HALF], F32, name="res", bufs=8)
+                eng = nc.vector.tensor_copy if e == "V" else nc.scalar.copy
+                eng(out=res[:], in_=live["nb", n, m][:])
+                nc.sync.dma_start(out=out[m * P : (m + 1) * P, cols_of(n)], in_=res[:])
+
+        with tc.manual_schedule():
+            for item in ORDER.split():
+                step(item[:-1], item[-1])

@@ -20,84 +20,28 @@ T = 4
 KP = P * T
 NV = V // KP
 NH = H // KP
-HALF = 512
-NB = B // HALF
-NM = V // P
+BANK = 512
+NBANKS = 8
 
-ORDER = (
-    "T000P wid000S wid001S wid002S wid003S wid110S wid111S wid112S "
-    "wid113S wid010V wid011V wid012V wid013V vi01V vi00V wid100V "
-    "wid101V wid102V wid103V d00V vi11V vq00V T001P T010P "
-    "E010S T011P E011S E000S E001S d01S q101V d10V "
-    "q200V d21V vi10V T100P T101P T200P T201P T110P "
-    "E110S T111P E111S E200S E201S q120V vq10V T310P "
-    "T311P T300P E300S T301P E301S E100S E101S d11S "
-    "E310S E311S q130V q111V vq01V vq11V q110V d30V "
-    "q131V q210V q100V d20V q221V T210P E210S T211P "
-    "E211S q121V q201V M010P F010S M011P F011S M012P "
-    "F012S M013P F013S X01V M030P F030S M031P F031S "
-    "M032P F032S M033P F033S X03V M000P F000S M001P "
-    "F001S M002P F002S M003P F003S X00V q211V M020P "
-    "F020S M021P F021S M022P F022S M023P F023S X02V "
-    "hq01V hq00V hq03V M110P F110S M111P F111S M112P "
-    "F112S M113P F113S d31S q231V hq02V q230V q220V "
-    "M100P F100S M101P F101S M102P F102S M103P F103S "
-    "X10V X11V hq10V M120P M121P M122P M123P M130P "
-    "F130S M131P F131S M132P F132S M133P F133S F120S "
-    "F121S F122S F123S G120S G121S G122S G123S X12V "
-    "hq11V hq12V X13V hq13V N060P N061P N062P N063P "
-    "N050P N051P N052P N053P J05S J06S N000P N001P "
-    "N002P N003P N010P N011P N012P N013P J01S N040P "
-    "N041P N042P N043P N020P N021P N022P N023P N030P "
-    "N031P N032P N033P N070P N071P N072P N073P J07S "
-    "J02S J03S J04S N100P N101P N102P N170P N171P "
-    "N172P N140P N141P N142P N160P N161P N162P N130P "
-    "N131P N132P N133P J13S N143P J14S N173P J17S "
-    "N163P J16S N103P J10S J00S N120P N121P N122P "
-    "N150P N151P N152P N123P J12S N153P J15V N110P "
-    "N111P N112P N113P J11S "
-)
+CHUNKS = [(0, 512), (512, 512)]
+BUFS = {"vflat": 2, "vgrp": 2, "wtgrp": 3, "w2grp": 3, "gate_a": 1, "gate_b": 1, "hgrp": 3, "sig": 6, "res": 6}
+RUN = 4
+XRUN = 4
 
 
 def tile_rbm_mean_field_reconstruction_s7_kernel(tc, v_bytes, v_scale, w, beta, out):
     nc = tc.nc
     with ExitStack() as ctx:
         keep = ctx.enter_context(tc.tile_pool(name="keep", bufs=1))
-        rot = ctx.enter_context(tc.tile_pool(name="rot", bufs=3))
-        psum = ctx.enter_context(tc.psum_pool(name="psum", bufs=8))
+        rot = ctx.enter_context(tc.tile_pool(name="rot", bufs=1))
+        psum = ctx.enter_context(tc.psum_pool(name="psum", bufs=1))
 
-        v_raw = [keep.tile([P, T, B], U8, name="v_raw%d" % c, align_bytes=64) for c in range(NV)]
-        w_sb = [keep.tile([P, T, V], BF16, name="w_sb%d" % g, align_bytes=64) for g in range(NH)]
+        w_view = w.rearrange("(g p t) v -> g p t v", p=P, t=T)
+        v_view = v_bytes.rearrange("(c p t) n -> c p t n", p=P, t=T)
         vs = keep.tile([P, NV, T], F32, name="vs")
         beta_bf = keep.tile([P, NH, T], BF16, name="beta_bf")
         beta32 = keep.tile([P, NH, T], F32, name="beta32")
-        w_view = w.rearrange("(g p t) v -> g p t v", p=P, t=T)
-        v_view = v_bytes.rearrange("(c p t) n -> c p t n", p=P, t=T)
-
-        def load_w(g, a):
-            nc.sync.dma_start(out=w_sb[g][:, 2 * a : 2 * a + 2, :], in_=w_view[g][:, 2 * a : 2 * a + 2, :])
-
-        nc.scalar.dma_start(out=vs[:], in_=v_scale.rearrange("(c p t) o -> p c (t o)", p=P, t=T))
-        nc.sync.dma_start(out=v_raw[0][:, 0:2, :], in_=v_view[0][:, 0:2, :])
-        nc.sync.dma_start(out=v_raw[0][:, 2:4, :], in_=v_view[0][:, 2:4, :])
-        load_w(0, 0)
-        nc.sync.dma_start(out=v_raw[1][:], in_=v_view[1])
-        load_w(0, 1)
-        load_w(1, 0)
-        load_w(1, 1)
-        nc.sync.dma_start(out=beta_bf[:], in_=beta.rearrange("(g p t) o -> p g (t o)", p=P, t=T))
-        load_w(2, 0)
-        load_w(2, 1)
-        load_w(3, 0)
-        load_w(3, 1)
-
         ident = keep.tile([P, P], F32, name="ident")
-        make_identity(nc, ident[:])
-        dummy = keep.tile([P, 1], F32, name="dummy")
-        nc.vector.memset(dummy[:], 0.0)
-        nc.scalar.activation(out=dummy[:], in_=dummy[:], func=ACT.Sigmoid)
-        nc.gpsimd.tensor_copy(out=beta32[:], in_=beta_bf[:])
-
         v_codes = keep.tile([P, NV, B], U32, name="v_codes", align_bytes=64)
         v_sc = keep.tile([P, NV, B], U8, name="v_sc", align_bytes=64)
         wt_codes = keep.tile([P, NV, H], U32, name="wt_codes", align_bytes=64)
@@ -107,120 +51,245 @@ def tile_rbm_mean_field_reconstruction_s7_kernel(tc, v_bytes, v_scale, w, beta, 
         h_codes = keep.tile([P, NH, B], U32, name="h_codes", align_bytes=64)
         h_sc = keep.tile([P, NH, B], U8, name="h_sc", align_bytes=64)
 
-        def interleave(eng, dst, src):
-            o = dst.rearrange("p (c i) t -> p c t i", i=4)
-            s = src.rearrange("p t (c i) -> p c t i", i=4)
-            eng(out=o, in_=s)
-
         live = {}
+        copy_on = {"V": nc.vector.tensor_copy, "S": nc.scalar.copy}
 
-        def cols_of(n):
-            return slice(n * HALF, (n + 1) * HALF)
+        def samples(n):
+            return slice(CHUNKS[n][0], CHUNKS[n][0] + CHUNKS[n][1])
 
-        def step(name, e):
-            k = name[0]
-            if name[:3] == "wid":
-                c, n, t = int(name[3]), int(name[4]), int(name[5])
-                if ("vf", c, n) not in live:
-                    v_flat = rot.tile([P, T, HALF], BF16, name="v_flat", tag="stage", align_bytes=64, bufs=14)
-                    live["vf", c, n] = v_flat
-                flat = live["vf", c, n]
-                src = v_raw[c][:, t, cols_of(n)].bitcast(FP8)
-                if e == "V":
-                    nc.vector.tensor_scalar(out=flat[:, t, :], in0=src, scalar1=vs[:, c, t : t + 1], scalar2=None, op0=ALU.mult)
-                else:
-                    nc.scalar.activation(out=flat[:, t, :], in_=src, func=ACT.Copy, scale=vs[:, c, t : t + 1])
-            elif name[:2] == "vi":
-                c, n = int(name[2]), int(name[3])
-                v_grp = rot.tile([P, HALF, T], BF16, name="v_grp", tag="stage", align_bytes=64, bufs=14)
-                live["vg", c, n] = v_grp
-                interleave(nc.vector.tensor_copy, v_grp[:], live["vf", c, n][:])
-            elif name[:2] == "vq":
-                c, n = int(name[2]), int(name[3])
-                nc.vector.quantize_mx(out=v_codes[:, c, cols_of(n)].bitcast(FP8X4), scales=v_sc[:, c, cols_of(n)], in_=live["vg", c, n][:].rearrange("p n t -> p (n t)"))
-            elif k == "T":
-                g, c, a = int(name[1]), int(name[2]), int(name[3])
-                bank = psum.tile([P, 512], F32, name="bank")
-                live["tb", g, c, a] = bank
-                for b in range(2):
-                    row = w_sb[g][:, 2 * a + b, :].bitcast(F32)
-                    for u in range(2):
-                        j = (2 * b + u) * P
-                        nc.tensor.transpose(bank[:, j : j + P], row[:, 256 * c + u : 256 * (c + 1) : 2], ident[:])
-            elif k == "E":
-                g, c, a = int(name[1]), int(name[2]), int(name[3])
-                if ("wt", g, c) not in live:
-                    wt_grp = rot.tile([P, KP, T], BF16, name="wt_grp", tag="stage", align_bytes=64, bufs=14)
-                    live["wt", g, c] = wt_grp
-                words = live["wt", g, c][:].rearrange("p m t -> p (m t)").bitcast(F32).rearrange("p (t m u) -> p t m u", t=T, u=2)
-                eng = nc.vector.tensor_copy if e == "V" else nc.scalar.copy
-                eng(out=words[:, 2 * a : 2 * a + 2], in_=live["tb", g, c, a][:].rearrange("p (t u m) -> p t m u", t=2, u=2))
-            elif name[:2] == "q1":
-                g, c = int(name[2]), int(name[3])
-                cols = slice(g * KP, (g + 1) * KP)
-                nc.vector.quantize_mx(out=wt_codes[:, c, cols].bitcast(FP8X4), scales=wt_sc[:, c, cols], in_=live["wt", g, c][:].rearrange("p m t -> p (m t)"))
-            elif k == "d":
-                g, a = int(name[1]), int(name[2])
-                w2_grp = rot.tile([P, HALF, T], BF16, name="w2_grp", tag="stage", align_bytes=64, bufs=14)
-                live["w2", g, a] = w2_grp
-                interleave(nc.scalar.copy if e == "S" else nc.vector.tensor_copy, w2_grp[:], w_sb[g][:, :, cols_of(a)])
-            elif name[:2] == "q2":
-                g, a = int(name[2]), int(name[3])
-                nc.vector.quantize_mx(out=w2_codes[:, g, cols_of(a)].bitcast(FP8X4), scales=w2_sc[:, g, cols_of(a)], in_=live["w2", g, a][:].rearrange("p m t -> p (m t)"))
-            elif k == "M":
-                n, g, t = int(name[1]), int(name[2]), int(name[3])
-                bank = psum.tile([P, 512], F32, name="bank")
-                live["mb", n, g, t] = bank
-                m = slice(g * KP + t * P, g * KP + (t + 1) * P)
-                for c in range(NV):
-                    nc.tensor.matmul_mx(out=bank[:], lhsT=wt_codes[:, c, m].bitcast(FP8X4), lhsT_scale=wt_sc[:, c, m],
-                                        rhs=v_codes[:, c, cols_of(n)].bitcast(FP8X4), rhs_scale=v_sc[:, c, cols_of(n)],
-                                        start=(c == 0), stop=(c == NV - 1))
-            elif k == "F":
-                n, g, t = int(name[1]), int(name[2]), int(name[3])
-                if ("sig", n, g) not in live:
-                    sig = rot.tile([P, T, HALF], F32, name="sig", align_bytes=64, bufs=5)
-                    live["sig", n, g] = sig
-                nc.scalar.activation(out=live["sig", n, g][:, t, :], in_=live["mb", n, g, t][:], func=ACT.Sigmoid, scale=beta32[:, g, t : t + 1])
-            elif k == "G":
-                n, g, t = int(name[1]), int(name[2]), int(name[3])
-                if ("hf", n, g) not in live:
-                    h_flat = rot.tile([P, T, HALF], BF16, name="h_flat", tag="stage", align_bytes=64, bufs=14)
-                    live["hf", n, g] = h_flat
-                nc.scalar.activation(out=live["hf", n, g][:, t, :], in_=live["sig", n, g][:, t, :], func=ACT.Copy, scale=beta32[:, g, t : t + 1])
-            elif k == "X" and ("hf", int(name[1]), int(name[2])) in live:
-                n, g = int(name[1]), int(name[2])
-                h_grp = rot.tile([P, HALF, T], BF16, name="h_grp", tag="stage", align_bytes=64, bufs=14)
-                live["h", n, g] = h_grp
-                interleave(nc.vector.tensor_copy, h_grp[:], live["hf", n, g][:])
-            elif k == "X":
-                n, g = int(name[1]), int(name[2])
-                h_grp = rot.tile([P, HALF, T], BF16, name="h_grp", tag="stage", align_bytes=64, bufs=14)
-                live["h", n, g] = h_grp
-                nc.vector.tensor_tensor(
-                    out=h_grp[:].rearrange("p (c i) t -> p c t i", i=4),
-                    in0=live["sig", n, g][:].rearrange("p t (c i) -> p c t i", i=4),
-                    in1=beta32[:, g, :].unsqueeze(1).unsqueeze(3).to_broadcast([P, HALF // 4, T, 4]),
-                    op=ALU.mult)
-            elif name[:2] == "hq":
-                n, g = int(name[2]), int(name[3])
-                nc.vector.quantize_mx(out=h_codes[:, g, cols_of(n)].bitcast(FP8X4), scales=h_sc[:, g, cols_of(n)], in_=live["h", n, g][:].rearrange("p n t -> p (n t)"))
-            elif k == "N":
-                n, m, g = int(name[1]), int(name[2]), int(name[3])
-                if g == 0:
-                    bank = psum.tile([P, 512], F32, name="bank")
-                    live["nb", n, m] = bank
-                mc = slice(m * P, (m + 1) * P)
-                nc.tensor.matmul_mx(out=live["nb", n, m][:], lhsT=w2_codes[:, g, mc].bitcast(FP8X4), lhsT_scale=w2_sc[:, g, mc],
-                                    rhs=h_codes[:, g, cols_of(n)].bitcast(FP8X4), rhs_scale=h_sc[:, g, cols_of(n)],
-                                    start=(g == 0), stop=(g == NH - 1))
-            elif k == "J":
-                n, m = int(name[1]), int(name[2])
-                res = rot.tile([P, HALF], F32, name="res", bufs=8)
-                eng = nc.vector.tensor_copy if e == "V" else nc.scalar.copy
-                eng(out=res[:], in_=live["nb", n, m][:])
-                nc.sync.dma_start(out=out[m * P : (m + 1) * P, cols_of(n)], in_=res[:])
+        def staged(tag, key, shape, dtype):
+            if (tag, key) not in live:
+                live[tag, key] = rot.tile(shape, dtype, name=tag, align_bytes=64, bufs=BUFS[tag])
+            return live[tag, key]
+
+        def weave(e, dst, src):
+            o = dst.rearrange("p (c i) t -> p c t i", i=RUN)
+            s = src.rearrange("p t (c i) -> p c t i", i=RUN)
+            if e == "G":
+                nc.gpsimd.tensor_scalar(out=dst, in0=src.rearrange("p t n -> p n t"), scalar1=1.0, scalar2=0.0, op0=ALU.mult, op1=ALU.add)
+            else:
+                copy_on[e](out=o, in_=s)
+
+        def quantise(codes, scales, grouped):
+            nc.vector.quantize_mx(out=codes.bitcast(FP8X4), scales=scales, in_=grouped.rearrange("p n t -> p (n t)"))
+
+        def small_loads():
+            nc.scalar.dma_start(out=vs[:], in_=v_scale.rearrange("(c p t) o -> p c (t o)", p=P, t=T))
+            nc.scalar.dma_start(out=beta_bf[:], in_=beta.rearrange("(g p t) o -> p g (t o)", p=P, t=T))
+            make_identity(nc, ident[:])
+            dummy = keep.tile([P, 1], F32, name="dummy")
+            nc.vector.memset(dummy[:], 0.0)
+            nc.scalar.activation(out=dummy[:], in_=dummy[:], func=ACT.Sigmoid)
+            nc.gpsimd.tensor_copy(out=beta32[:], in_=beta_bf[:])
+
+        def load_v(c, lo, hi):
+            first, last = CHUNKS[lo][0], CHUNKS[hi - 1][0] + CHUNKS[hi - 1][1]
+            raw = keep.tile([P, T, last - first], U8, name="v_raw%d_%d" % (c, lo), align_bytes=64)
+            nc.sync.dma_start(out=raw[:], in_=v_view[c][:, :, first:last])
+            for n in range(lo, hi):
+                live["vraw", c, n] = raw[:, :, CHUNKS[n][0] - first : CHUNKS[n][0] - first + CHUNKS[n][1]]
+
+        def load_w(g, c):
+            rows = keep.tile([P, T, KP], BF16, name="w_rows%d_%d" % (g, c), align_bytes=64)
+            nc.sync.dma_start(out=rows[:], in_=w_view[g][:, :, c * KP : (c + 1) * KP])
+            live["w", g, c] = rows
+
+        def widen(c, n, t, e):
+            flat = staged("vflat", (c, n), [P, T, CHUNKS[n][1]], BF16)
+            src = live["vraw", c, n][:, t, :].bitcast(FP8)
+            if e == "V":
+                nc.vector.tensor_scalar(out=flat[:, t, :], in0=src, scalar1=vs[:, c, t : t + 1], scalar2=None, op0=ALU.mult)
+            else:
+                nc.scalar.activation(out=flat[:, t, :], in_=src, func=ACT.Copy, scale=vs[:, c, t : t + 1])
+
+        def weave_v(c, n, e):
+            weave(e, staged("vgrp", (c, n), [P, CHUNKS[n][1], T], BF16)[:], live["vflat", (c, n)][:])
+
+        def quant_v(c, n):
+            quantise(v_codes[:, c, samples(n)], v_sc[:, c, samples(n)], live["vgrp", (c, n)][:])
+
+        def turn(g, c, a, b):
+            bank = psum.tile([P, BANK], F32, name="bank%d" % b)
+            live["tb", g, c, a] = bank
+            for i in range(2):
+                words = live["w", g, c][:, 2 * a + i, :].bitcast(F32)
+                for u in range(2):
+                    j = (2 * i + u) * P
+                    nc.tensor.transpose(bank[:, j : j + P], words[:, u : 2 * P : 2], ident[:])
+
+        def empty_turn(g, c, a, e):
+            grp = staged("wtgrp", (g, c), [P, KP, T], BF16)
+            words = grp[:].rearrange("p m t -> p (m t)").bitcast(F32).rearrange("p (t m u) -> p t m u", t=T, u=2)
+            copy_on[e](out=words[:, 2 * a : 2 * a + 2], in_=live["tb", g, c, a][:].rearrange("p (t u m) -> p t m u", t=2, u=2))
+
+        def quant_up(g, c):
+            cols = slice(g * KP, (g + 1) * KP)
+            quantise(wt_codes[:, c, cols], wt_sc[:, c, cols], live["wtgrp", (g, c)][:])
+
+        def weave_w(g, c, e, tag="w2grp"):
+            live["w2", g, c] = staged(tag, (g, c), [P, KP, T], BF16)
+            weave(e, live["w2", g, c][:], live["w", g, c][:])
+
+        def quant_down(g, c):
+            cols = slice(c * KP, (c + 1) * KP)
+            quantise(w2_codes[:, g, cols], w2_sc[:, g, cols], live["w2", g, c][:])
+
+        def beta_to_bank(b):
+            bank = psum.tile([P, BANK], F32, name="bank%d" % b)
+            nc.tensor.matmul(out=bank[:, 0 : NH * T], lhsT=ident[:], rhs=beta32[:].rearrange("p g t -> p (g t)"), start=True, stop=True)
+            live["beta"] = bank[:, 0 : NH * T].rearrange("p (g t) -> p g t", t=T)
+
+        def up(n, g, t, b):
+            bank = psum.tile([P, BANK], F32, name="bank%d" % b)
+            live["mb", n, g, t] = bank
+            m = slice(g * KP + t * P, g * KP + (t + 1) * P)
+            for c in range(NV):
+                nc.tensor.matmul_mx(out=bank[:, 0 : CHUNKS[n][1]], lhsT=wt_codes[:, c, m].bitcast(FP8X4), lhsT_scale=wt_sc[:, c, m],
+                                    rhs=v_codes[:, c, samples(n)].bitcast(FP8X4), rhs_scale=v_sc[:, c, samples(n)],
+                                    start=(c == 0), stop=(c == NV - 1))
+
+        def sigmoid(n, g, t):
+            sig = staged("sig", (n, g), [P, T, CHUNKS[n][1]], F32)
+            nc.scalar.activation(out=sig[:, t, :], in_=live["mb", n, g, t][:, 0 : CHUNKS[n][1]], func=ACT.Sigmoid, scale=beta32[:, g, t : t + 1])
+
+        def scale_weave(n, g, from_bank):
+            width = CHUNKS[n][1]
+            factors = live["beta"] if from_bank else beta32[:]
+            nc.vector.tensor_tensor(
+                out=staged("hgrp", (n, g), [P, width, T], BF16)[:].rearrange("p (c i) t -> p c t i", i=XRUN),
+                in0=live["sig", (n, g)][:].rearrange("p t (c i) -> p c t i", i=XRUN),
+                in1=factors[:, g, :].unsqueeze(1).unsqueeze(3).to_broadcast([P, width // XRUN, T, XRUN]),
+                op=ALU.mult)
+
+        def quant_h(n, g):
+            quantise(h_codes[:, g, samples(n)], h_sc[:, g, samples(n)], live["hgrp", (n, g)][:])
+
+        def down(n, j, g, b, first, last):
+            width = CHUNKS[n][1]
+            per = BANK // width
+            if first:
+                live["nb", n, j] = psum.tile([P, BANK], F32, name="bank%d" % b)
+            for i in range(per):
+                mc = slice((j * per + i) * P, (j * per + i + 1) * P)
+                nc.tensor.matmul_mx(out=live["nb", n, j][:, i * width : (i + 1) * width],
+                                    lhsT=w2_codes[:, g, mc].bitcast(FP8X4), lhsT_scale=w2_sc[:, g, mc],
+                                    rhs=h_codes[:, g, samples(n)].bitcast(FP8X4), rhs_scale=h_sc[:, g, samples(n)],
+                                    start=(first and i == 0), stop=(last and i == per - 1))
+
+        def finish(n, j, e):
+            width = CHUNKS[n][1]
+            per = BANK // width
+            res = staged("res", (n, j), [P, BANK], F32)
+            copy_on[e](out=res[:], in_=live["nb", n, j][:])
+            rows = out.rearrange("(j i p) n -> j p i n", i=per, p=P)[j]
+            nc.sync.dma_start(out=rows[:, :, samples(n)], in_=res[:].rearrange("p (i n) -> p i n", i=per))
 
         with tc.manual_schedule():
-            for item in ORDER.split():
-                step(item[:-1], item[-1])
+            small_loads()
+            load_v(0, 0, 1)
+            load_v(1, 0, 1)
+            for g in range(NH):
+                load_w(g, 0)
+                load_w(g, 1)
+                if g == 2:
+                    load_v(0, 1, 2)
+                    load_v(1, 1, 2)
+            nb = [0]
+
+            def bank():
+                nb.append(nb[-1] + 1)
+                return nb[-2] % (NBANKS - 1)
+
+            def turn_group(g, on="SSSS"):
+                for c in range(NV):
+                    for a in range(2):
+                        turn(g, c, a, bank())
+                        if on[2 * c + a] == "S":
+                            empty_turn(g, c, a, "S")
+
+            def up_group(n, g):
+                for t in range(T):
+                    up(n, g, t, bank())
+                    sigmoid(n, g, t)
+
+            def down_pass(n, js, g, banks=None):
+                for j in js:
+                    down(n, j, g, (banks[j % 4] if banks else bank()) if g == 0 else 0, g == 0, g == NH - 1)
+
+            for t in range(T):
+                widen(0, 0, t, "V")
+                widen(1, 0, t, "S")
+            turn_group(0)
+            weave_v(0, 0, "V")
+            weave_v(1, 0, "V")
+            quant_v(0, 0)
+            quant_up(0, 0)
+            quant_v(1, 0)
+            quant_up(0, 1)
+            turn_group(1)
+            beta_to_bank(7)
+            up_group(0, 0)
+            weave_w(0, 0, "V", "gate_a")
+            quant_up(1, 0)
+            quant_up(1, 1)
+            turn_group(2)
+            quant_down(0, 0)
+            weave_w(1, 0, "G", "gate_a")
+            scale_weave(0, 0, True)
+            up_group(0, 1)
+            quant_up(2, 0)
+            quant_up(2, 1)
+            for c in range(NV):
+                for t in range(T):
+                    widen(c, 1, t, "V")
+            turn_group(3)
+            up_group(0, 2)
+            weave_v(0, 1, "V")
+            quant_up(3, 0)
+            quant_up(3, 1)
+            weave_v(1, 1, "V")
+            quant_v(0, 1)
+            quant_h(0, 0)
+            quant_v(1, 1)
+            up_group(0, 3)
+            quant_down(1, 0)
+            weave_w(2, 0, "G", "gate_a")
+            weave_w(3, 0, "G", "gate_b")
+            for g in range(1, NH):
+                scale_weave(0, g, True)
+            for g in range(NH):
+                up_group(1, g)
+            for g in range(1, NH):
+                quant_h(0, g)
+            quant_down(3, 0)
+            quant_down(2, 0)
+            weave_w(0, 1, "G", "gate_a")
+            weave_w(1, 1, "S")
+            weave_w(2, 1, "S")
+            weave_w(3, 1, "S")
+            scale_weave(1, 0, True)
+            scale_weave(1, 1, True)
+            for g in range(NH):
+                down_pass(0, range(4), g, [0, 1, 2, 3])
+            for g in range(2):
+                quant_h(1, g)
+                down_pass(1, range(4), g, [4, 5, 6, 7])
+            for j in range(4):
+                finish(0, j, "S")
+            for g in range(NH):
+                quant_down(g, 1)
+            scale_weave(1, 2, False)
+            scale_weave(1, 3, False)
+            for j in range(4, 8):
+                for g in range(NH):
+                    down_pass(0, [j], g, [0, 1, 2, 3])
+                finish(0, j, "S")
+            for g in range(2, NH):
+                quant_h(1, g)
+                down_pass(1, range(4), g)
+            for j in range(4):
+                finish(1, j, "VS"[j % 2])
+            for j in range(4, 8):
+                for g in range(NH):
+                    down_pass(1, [j], g, [0, 1, 2, 3])
+                finish(1, j, "VS"[j % 2])

@@ -24,7 +24,8 @@ BANK = 512
 NBANKS = 8
 
 CHUNKS = [(0, 512), (512, 512)]
-BUFS = {"vflat": 2, "vgrp": 2, "wtgrp": 3, "w2grp": 3, "gate_a": 1, "gate_b": 1, "hgrp": 3, "sig": 6, "res": 6}
+PARTS = [(0, 512), (512, 256), (768, 256)]
+BUFS = {"vflat": 2, "vgrp": 2, "wtgrp": 3, "w2grp": 2, "gate_a": 1, "gate_b": 2, "hgrp": 5, "sig": 6, "res": 6}
 RUN = 4
 XRUN = 4
 
@@ -117,14 +118,15 @@ def tile_rbm_mean_field_reconstruction_s7_kernel(tc, v_bytes, v_scale, w, beta, 
                     j = (2 * i + u) * P
                     nc.tensor.transpose(bank[:, j : j + P], words[:, u : 2 * P : 2], ident[:])
 
-        def empty_turn(g, c, a, e):
-            grp = staged("wtgrp", (g, c), [P, KP, T], BF16)
+        def empty_turn(g, c, a, e, tag="wtgrp"):
+            grp = staged(tag, ("up", g, c), [P, KP, T], BF16)
+            live["wt", g, c] = grp
             words = grp[:].rearrange("p m t -> p (m t)").bitcast(F32).rearrange("p (t m u) -> p t m u", t=T, u=2)
             copy_on[e](out=words[:, 2 * a : 2 * a + 2], in_=live["tb", g, c, a][:].rearrange("p (t u m) -> p t m u", t=2, u=2))
 
         def quant_up(g, c):
             cols = slice(g * KP, (g + 1) * KP)
-            quantise(wt_codes[:, c, cols], wt_sc[:, c, cols], live["wtgrp", (g, c)][:])
+            quantise(wt_codes[:, c, cols], wt_sc[:, c, cols], live["wt", g, c][:])
 
         def weave_w(g, c, e, tag="w2grp"):
             live["w2", g, c] = staged(tag, (g, c), [P, KP, T], BF16)
@@ -152,37 +154,42 @@ def tile_rbm_mean_field_reconstruction_s7_kernel(tc, v_bytes, v_scale, w, beta, 
             sig = staged("sig", (n, g), [P, T, CHUNKS[n][1]], F32)
             nc.scalar.activation(out=sig[:, t, :], in_=live["mb", n, g, t][:, 0 : CHUNKS[n][1]], func=ACT.Sigmoid, scale=beta32[:, g, t : t + 1])
 
-        def scale_weave(n, g, from_bank):
-            width = CHUNKS[n][1]
+        def part_samples(d):
+            return slice(PARTS[d][0], PARTS[d][0] + PARTS[d][1])
+
+        def scale_weave(d, g, from_bank, tag="hgrp"):
+            first, width = PARTS[d]
+            n = first // BANK
             factors = live["beta"] if from_bank else beta32[:]
+            live["h", d, g] = staged(tag, ("h", d, g), [P, width, T], BF16)
             nc.vector.tensor_tensor(
-                out=staged("hgrp", (n, g), [P, width, T], BF16)[:].rearrange("p (c i) t -> p c t i", i=XRUN),
-                in0=live["sig", (n, g)][:].rearrange("p t (c i) -> p c t i", i=XRUN),
+                out=live["h", d, g][:].rearrange("p (c i) t -> p c t i", i=XRUN),
+                in0=live["sig", (n, g)][:, :, first - n * BANK : first - n * BANK + width].rearrange("p t (c i) -> p c t i", i=XRUN),
                 in1=factors[:, g, :].unsqueeze(1).unsqueeze(3).to_broadcast([P, width // XRUN, T, XRUN]),
                 op=ALU.mult)
 
-        def quant_h(n, g):
-            quantise(h_codes[:, g, samples(n)], h_sc[:, g, samples(n)], live["hgrp", (n, g)][:])
+        def quant_h(d, g):
+            quantise(h_codes[:, g, part_samples(d)], h_sc[:, g, part_samples(d)], live["h", d, g][:])
 
-        def down(n, j, g, b, first, last):
-            width = CHUNKS[n][1]
+        def down(d, j, g, b, first, last):
+            width = PARTS[d][1]
             per = BANK // width
             if first:
-                live["nb", n, j] = psum.tile([P, BANK], F32, name="bank%d" % b)
+                live["nb", d, j] = psum.tile([P, BANK], F32, name="bank%d" % b)
             for i in range(per):
                 mc = slice((j * per + i) * P, (j * per + i + 1) * P)
-                nc.tensor.matmul_mx(out=live["nb", n, j][:, i * width : (i + 1) * width],
+                nc.tensor.matmul_mx(out=live["nb", d, j][:, i * width : (i + 1) * width],
                                     lhsT=w2_codes[:, g, mc].bitcast(FP8X4), lhsT_scale=w2_sc[:, g, mc],
-                                    rhs=h_codes[:, g, samples(n)].bitcast(FP8X4), rhs_scale=h_sc[:, g, samples(n)],
+                                    rhs=h_codes[:, g, part_samples(d)].bitcast(FP8X4), rhs_scale=h_sc[:, g, part_samples(d)],
                                     start=(first and i == 0), stop=(last and i == per - 1))
 
-        def finish(n, j, e):
-            width = CHUNKS[n][1]
+        def finish(d, j, e):
+            width = PARTS[d][1]
             per = BANK // width
-            res = staged("res", (n, j), [P, BANK], F32)
-            copy_on[e](out=res[:], in_=live["nb", n, j][:])
+            res = staged("res", (d, j), [P, BANK], F32)
+            copy_on[e](out=res[:], in_=live["nb", d, j][:])
             rows = out.rearrange("(j i p) n -> j p i n", i=per, p=P)[j]
-            nc.sync.dma_start(out=rows[:, :, samples(n)], in_=res[:].rearrange("p (i n) -> p i n", i=per))
+            nc.sync.dma_start(out=rows[:, :, part_samples(d)], in_=res[:].rearrange("p (i n) -> p i n", i=per))
 
         with tc.manual_schedule():
             small_loads()
@@ -191,7 +198,7 @@ def tile_rbm_mean_field_reconstruction_s7_kernel(tc, v_bytes, v_scale, w, beta, 
             for g in range(NH):
                 load_w(g, 0)
                 load_w(g, 1)
-                if g == 2:
+                if g == 1:
                     load_v(0, 1, 2)
                     load_v(1, 1, 2)
             nb = [0]
@@ -200,12 +207,11 @@ def tile_rbm_mean_field_reconstruction_s7_kernel(tc, v_bytes, v_scale, w, beta, 
                 nb.append(nb[-1] + 1)
                 return nb[-2] % (NBANKS - 1)
 
-            def turn_group(g, on="SSSS"):
+            def turn_group(g, tag="wtgrp"):
                 for c in range(NV):
                     for a in range(2):
                         turn(g, c, a, bank())
-                        if on[2 * c + a] == "S":
-                            empty_turn(g, c, a, "S")
+                        empty_turn(g, c, a, "S", tag if c == 1 else "wtgrp")
 
             def up_group(n, g):
                 for t in range(T):
@@ -226,70 +232,80 @@ def tile_rbm_mean_field_reconstruction_s7_kernel(tc, v_bytes, v_scale, w, beta, 
             quant_up(0, 0)
             quant_v(1, 0)
             quant_up(0, 1)
-            turn_group(1)
+            turn_group(1, "gate_a")
             beta_to_bank(7)
             up_group(0, 0)
-            weave_w(0, 0, "V", "gate_a")
-            quant_up(1, 0)
-            quant_up(1, 1)
-            turn_group(2)
-            quant_down(0, 0)
-            weave_w(1, 0, "G", "gate_a")
-            scale_weave(0, 0, True)
-            up_group(0, 1)
-            quant_up(2, 0)
-            quant_up(2, 1)
             for c in range(NV):
                 for t in range(T):
                     widen(c, 1, t, "V")
+                quant_up(1, c)
+            turn_group(2)
+            weave_w(0, 0, "G", "gate_a")
+            scale_weave(0, 0, True)
+            up_group(0, 1)
+            weave_v(0, 1, "V")
+            quant_up(2, 0)
+            quant_up(2, 1)
             turn_group(3)
             up_group(0, 2)
-            weave_v(0, 1, "V")
+            weave_v(1, 1, "V")
             quant_up(3, 0)
             quant_up(3, 1)
-            weave_v(1, 1, "V")
             quant_v(0, 1)
-            quant_h(0, 0)
             quant_v(1, 1)
+            quant_h(0, 0)
             up_group(0, 3)
-            quant_down(1, 0)
-            weave_w(2, 0, "G", "gate_a")
+            quant_down(0, 0)
+            weave_w(1, 0, "G", "gate_a")
+            weave_w(2, 0, "G", "gate_b")
             weave_w(3, 0, "G", "gate_b")
             for g in range(1, NH):
                 scale_weave(0, g, True)
             for g in range(NH):
                 up_group(1, g)
-            for g in range(1, NH):
-                quant_h(0, g)
-            quant_down(3, 0)
-            quant_down(2, 0)
-            weave_w(0, 1, "G", "gate_a")
-            weave_w(1, 1, "S")
-            weave_w(2, 1, "S")
-            weave_w(3, 1, "S")
             scale_weave(1, 0, True)
             scale_weave(1, 1, True)
+
+            weave_w(0, 1, "S")
+            weave_w(1, 1, "S")
+            lo, hi = [0, 1, 2, 3], [4, 5, 6, 7]
             for g in range(NH):
-                down_pass(0, range(4), g, [0, 1, 2, 3])
+                if g > 0:
+                    quant_h(0, g)
+                    quant_down(g, 0)
+                down_pass(0, range(4), g, lo)
             for g in range(2):
                 quant_h(1, g)
-                down_pass(1, range(4), g, [4, 5, 6, 7])
+                down_pass(1, range(2), g, hi)
+            quant_down(0, 1)
+            down_pass(1, range(2, 4), 0, hi)
+            weave_w(2, 1, "V")
             for j in range(4):
                 finish(0, j, "S")
-            for g in range(NH):
-                quant_down(g, 1)
+            quant_down(1, 1)
+            weave_w(3, 1, "S")
+            down_pass(1, range(2, 4), 1)
+            for g in range(2):
+                down_pass(0, range(4, 8), g, lo)
             scale_weave(1, 2, False)
+            quant_down(2, 1)
             scale_weave(1, 3, False)
+            quant_h(1, 2)
+            down_pass(0, range(4, 8), 2)
+            down_pass(1, range(4), 2)
+            scale_weave(2, 0, False)
+            quant_h(1, 3)
+            quant_down(3, 1)
+            down_pass(0, range(4, 8), 3)
             for j in range(4, 8):
-                for g in range(NH):
-                    down_pass(0, [j], g, [0, 1, 2, 3])
                 finish(0, j, "S")
-            for g in range(2, NH):
-                quant_h(1, g)
-                down_pass(1, range(4), g)
+            down_pass(1, range(4), 3)
             for j in range(4):
-                finish(1, j, "VS"[j % 2])
-            for j in range(4, 8):
-                for g in range(NH):
-                    down_pass(1, [j], g, [0, 1, 2, 3])
-                finish(1, j, "VS"[j % 2])
+                finish(1, j, "S")
+            for g in range(NH):
+                if g + 1 < NH:
+                    scale_weave(2, g + 1, False)
+                quant_h(2, g)
+                down_pass(2, range(4), g, lo)
+            for j in range(4):
+                finish(2, j, "VS"[j % 2])

@@ -25,7 +25,7 @@ NBANKS = 8
 
 CHUNKS = [(0, 512), (512, 512)]
 PARTS = [(0, 512), (512, 256), (768, 256)]
-BUFS = {"vflat": 2, "vgrp": 2, "wtgrp": 3, "w2grp": 2, "gate_a": 1, "gate_b": 2, "hgrp": 5, "sig": 6, "res": 6}
+BUFS = {"vflat": 2, "vgrp": 2, "wtgrp": 3, "w2grp": 2, "gate_a": 1, "gate_b": 2, "hgrp": 5, "sig": 6, "res": 5}
 RUN = 4
 XRUN = 4
 
@@ -52,6 +52,7 @@ def tile_rbm_mean_field_reconstruction_s7_kernel(tc, v_bytes, v_scale, w, beta, 
         h_codes = keep.tile([P, NH, B], U32, name="h_codes", align_bytes=64)
         h_sc = keep.tile([P, NH, B], U8, name="h_sc", align_bytes=64)
 
+        zeros = keep.tile([P, BANK], F32, name="zeros")
         live = {}
         copy_on = {"V": nc.vector.tensor_copy, "S": nc.scalar.copy}
 
@@ -79,8 +80,8 @@ def tile_rbm_mean_field_reconstruction_s7_kernel(tc, v_bytes, v_scale, w, beta, 
             nc.scalar.dma_start(out=beta_bf[:], in_=beta.rearrange("(g p t) o -> p g (t o)", p=P, t=T))
             make_identity(nc, ident[:])
             dummy = keep.tile([P, 1], F32, name="dummy")
-            nc.vector.memset(dummy[:], 0.0)
-            nc.scalar.activation(out=dummy[:], in_=dummy[:], func=ACT.Sigmoid)
+            nc.vector.memset(zeros[:], 0.0)
+            nc.scalar.activation(out=dummy[:], in_=zeros[:, 0:1], func=ACT.Sigmoid)
             nc.gpsimd.tensor_copy(out=beta32[:], in_=beta_bf[:])
 
         def load_v(c, lo, hi):
@@ -135,6 +136,10 @@ def tile_rbm_mean_field_reconstruction_s7_kernel(tc, v_bytes, v_scale, w, beta, 
         def quant_down(g, c):
             cols = slice(c * KP, (c + 1) * KP)
             quantise(w2_codes[:, g, cols], w2_sc[:, g, cols], live["w2", g, c][:])
+
+        def warm_up(cols):
+            bank = psum.tile([P, BANK], F32, name="bank7")
+            nc.tensor.matmul(out=bank[:, 0:cols], lhsT=zeros[:, 0:P], rhs=zeros[:, 0:cols], start=True, stop=True)
 
         def beta_to_bank(b):
             bank = psum.tile([P, BANK], F32, name="bank%d" % b)
@@ -209,6 +214,11 @@ def tile_rbm_mean_field_reconstruction_s7_kernel(tc, v_bytes, v_scale, w, beta, 
 
             def turn_group(g, tag="wtgrp"):
                 for c in range(NV):
+                    if g == 0 and c == 0:
+                        warm_up(BANK)
+                        warm_up(BANK)
+                    elif g < 2:
+                        warm_up(BANK // 2)
                     for a in range(2):
                         turn(g, c, a, bank())
                         empty_turn(g, c, a, "S", tag if c == 1 else "wtgrp")

@@ -37,7 +37,7 @@ def tile_rbm_mean_field_reconstruction_s7_kernel(tc, v_bytes, v_scale, w, beta, 
         rot = ctx.enter_context(tc.tile_pool(name="rot", bufs=1))
         psum = ctx.enter_context(tc.psum_pool(name="psum", bufs=1))
 
-        w_view = w.rearrange("(g p t) v -> g p t v", p=P, t=T)
+        w_view = w.rearrange("(g p t) v -> g p (t v)", p=P, t=T)
         v_view = v_bytes.rearrange("(c p t) n -> c p t n", p=P, t=T)
         vs = keep.tile([P, NV, T], F32, name="vs")
         beta_bf = keep.tile([P, NH, T], BF16, name="beta_bf")
@@ -45,8 +45,8 @@ def tile_rbm_mean_field_reconstruction_s7_kernel(tc, v_bytes, v_scale, w, beta, 
         ident = keep.tile([P, P], F32, name="ident")
         v_codes = keep.tile([P, NV, B], U32, name="v_codes", align_bytes=64)
         v_sc = keep.tile([P, NV, B], U8, name="v_sc", align_bytes=64)
-        wt_codes = keep.tile([P, NV, H], U32, name="wt_codes", align_bytes=64)
-        wt_sc = keep.tile([P, NV, H], U8, name="wt_sc", align_bytes=64)
+        wt_codes = keep.tile([P, NH, 2 * KP], U32, name="wt_codes", align_bytes=64)
+        wt_sc = keep.tile([P, NH, 2 * KP], U8, name="wt_sc", align_bytes=64)
         w2_codes = keep.tile([P, NH, V], U32, name="w2_codes", align_bytes=64)
         w2_sc = keep.tile([P, NH, V], U8, name="w2_sc", align_bytes=64)
         h_codes = keep.tile([P, NH, B], U32, name="h_codes", align_bytes=64)
@@ -91,10 +91,10 @@ def tile_rbm_mean_field_reconstruction_s7_kernel(tc, v_bytes, v_scale, w, beta, 
             for n in range(lo, hi):
                 live["vraw", c, n] = raw[:, :, CHUNKS[n][0] - first : CHUNKS[n][0] - first + CHUNKS[n][1]]
 
-        def load_w(g, c):
-            rows = keep.tile([P, T, KP], BF16, name="w_rows%d_%d" % (g, c), align_bytes=64)
-            nc.sync.dma_start(out=rows[:], in_=w_view[g][:, :, c * KP : (c + 1) * KP])
-            live["w", g, c] = rows
+        def load_w(g, a):
+            if a == 0:
+                live["w", g] = keep.tile([P, T * V], BF16, name="w_rows%d" % g, align_bytes=64)
+            nc.sync.dma_start(out=live["w", g][:, 2 * a * V : 2 * (a + 1) * V], in_=w_view[g][:, 2 * a * V : 2 * (a + 1) * V])
 
         def widen(c, n, t, e):
             flat = staged("vflat", (c, n), [P, T, CHUNKS[n][1]], BF16)
@@ -110,35 +110,36 @@ def tile_rbm_mean_field_reconstruction_s7_kernel(tc, v_bytes, v_scale, w, beta, 
         def quant_v(c, n):
             quantise(v_codes[:, c, samples(n)], v_sc[:, c, samples(n)], live["vgrp", (c, n)][:])
 
-        def turn(g, c, a, b):
+        def turn(g, a, c, b):
             bank = psum.tile([P, BANK], F32, name="bank%d" % b)
-            live["tb", g, c, a] = bank
+            live["tb", g, a, c] = bank
+            words = live["w", g][:].bitcast(F32)
             for i in range(2):
-                words = live["w", g, c][:, 2 * a + i, :].bitcast(F32)
+                first = (2 * a + i) * V // 2 + c * KP // 2
                 for u in range(2):
                     j = (2 * i + u) * P
-                    nc.tensor.transpose(bank[:, j : j + P], words[:, u : 2 * P : 2], ident[:])
+                    nc.tensor.transpose(bank[:, j : j + P], words[:, first + u : first + 2 * P : 2], ident[:])
 
-        def empty_turn(g, c, a, e, tag="wtgrp"):
-            grp = staged(tag, ("up", g, c), [P, KP, T], BF16)
-            live["wt", g, c] = grp
-            words = grp[:].rearrange("p m t -> p (m t)").bitcast(F32).rearrange("p (t m u) -> p t m u", t=T, u=2)
-            copy_on[e](out=words[:, 2 * a : 2 * a + 2], in_=live["tb", g, c, a][:].rearrange("p (t u m) -> p t m u", t=2, u=2))
+        def empty_turn(g, a, c, e, tag="wtgrp"):
+            grp = staged(tag, ("up", g, a), [P, KP, T], BF16)
+            live["wt", g, a] = grp
+            words = grp[:].rearrange("p m t -> p (m t)").bitcast(F32).rearrange("p (c i m u) -> p c i m u", c=NV, i=2, u=2)
+            copy_on[e](out=words[:, c], in_=live["tb", g, a, c][:].rearrange("p (i u m) -> p i m u", i=2, u=2))
 
-        def quant_up(g, c):
-            cols = slice(g * KP, (g + 1) * KP)
-            quantise(wt_codes[:, c, cols], wt_sc[:, c, cols], live["wt", g, c][:])
+        def quant_up(g, a):
+            cols = slice(a * KP, (a + 1) * KP)
+            quantise(wt_codes[:, g, cols], wt_sc[:, g, cols], live["wt", g, a][:])
 
         def weave_w(g, c, e, tag="w2grp"):
             live["w2", g, c] = staged(tag, (g, c), [P, KP, T], BF16)
-            weave(e, live["w2", g, c][:], live["w", g, c][:])
+            weave(e, live["w2", g, c][:], live["w", g][:].rearrange("p (t v) -> p t v", t=T)[:, :, c * KP : (c + 1) * KP])
 
         def quant_down(g, c):
             cols = slice(c * KP, (c + 1) * KP)
             quantise(w2_codes[:, g, cols], w2_sc[:, g, cols], live["w2", g, c][:])
 
         def warm_up(cols):
-            bank = psum.tile([P, BANK], F32, name="bank7")
+            bank = psum.tile([P, BANK], F32, name="bank6")
             nc.tensor.matmul(out=bank[:, 0:cols], lhsT=zeros[:, 0:P], rhs=zeros[:, 0:cols], start=True, stop=True)
 
         def beta_to_bank(b):
@@ -149,9 +150,10 @@ def tile_rbm_mean_field_reconstruction_s7_kernel(tc, v_bytes, v_scale, w, beta, 
         def up(n, g, t, b):
             bank = psum.tile([P, BANK], F32, name="bank%d" % b)
             live["mb", n, g, t] = bank
-            m = slice(g * KP + t * P, g * KP + (t + 1) * P)
             for c in range(NV):
-                nc.tensor.matmul_mx(out=bank[:, 0 : CHUNKS[n][1]], lhsT=wt_codes[:, c, m].bitcast(FP8X4), lhsT_scale=wt_sc[:, c, m],
+                first = (t // 2) * KP + c * 2 * P + (t % 2) * P
+                m = slice(first, first + P)
+                nc.tensor.matmul_mx(out=bank[:, 0 : CHUNKS[n][1]], lhsT=wt_codes[:, g, m].bitcast(FP8X4), lhsT_scale=wt_sc[:, g, m],
                                     rhs=v_codes[:, c, samples(n)].bitcast(FP8X4), rhs_scale=v_sc[:, c, samples(n)],
                                     start=(c == 0), stop=(c == NV - 1))
 
@@ -212,16 +214,11 @@ def tile_rbm_mean_field_reconstruction_s7_kernel(tc, v_bytes, v_scale, w, beta, 
                 nb.append(nb[-1] + 1)
                 return nb[-2] % (NBANKS - 1)
 
-            def turn_group(g, tag="wtgrp"):
+            def turn_unit(g, a, tag="wtgrp", last="S"):
                 for c in range(NV):
-                    if g == 0 and c == 0:
-                        warm_up(BANK)
-                        warm_up(BANK)
-                    elif g < 2:
-                        warm_up(BANK // 2)
-                    for a in range(2):
-                        turn(g, c, a, bank())
-                        empty_turn(g, c, a, "S", tag if c == 1 else "wtgrp")
+                    turn(g, a, c, bank())
+                    if c == 0 or last == "S":
+                        empty_turn(g, a, c, "S", tag)
 
             def up_group(n, g):
                 for t in range(T):
@@ -232,31 +229,39 @@ def tile_rbm_mean_field_reconstruction_s7_kernel(tc, v_bytes, v_scale, w, beta, 
                 for j in js:
                     down(n, j, g, (banks[j % 4] if banks else bank()) if g == 0 else 0, g == 0, g == NH - 1)
 
+            warm_up(BANK)
+            warm_up(BANK)
+            beta_to_bank(7)
             for t in range(T):
                 widen(0, 0, t, "V")
                 widen(1, 0, t, "S")
-            turn_group(0)
+            turn_unit(0, 0)
+            turn_unit(0, 1)
+            warm_up(BANK // 2)
             weave_v(0, 0, "V")
-            weave_v(1, 0, "V")
             quant_v(0, 0)
+            weave_v(1, 0, "V")
             quant_up(0, 0)
             quant_v(1, 0)
             quant_up(0, 1)
-            turn_group(1, "gate_a")
-            beta_to_bank(7)
+            turn_unit(1, 0)
+            turn_unit(1, 1, "gate_a")
             up_group(0, 0)
             for c in range(NV):
                 for t in range(T):
                     widen(c, 1, t, "V")
                 quant_up(1, c)
-            turn_group(2)
+            turn_unit(2, 0)
+            turn_unit(2, 1, last="V")
             weave_w(0, 0, "G", "gate_a")
             scale_weave(0, 0, True)
+            empty_turn(2, 1, 1, "V")
             up_group(0, 1)
             weave_v(0, 1, "V")
             quant_up(2, 0)
             quant_up(2, 1)
-            turn_group(3)
+            turn_unit(3, 0)
+            turn_unit(3, 1)
             up_group(0, 2)
             weave_v(1, 1, "V")
             quant_up(3, 0)

@@ -25,7 +25,7 @@ NBANKS = 8
 
 CHUNKS = [(0, 512), (512, 512)]
 PARTS = [(0, 512), (512, 256), (768, 256)]
-BUFS = {"vflat": 2, "vgrp": 2, "wtgrp": 3, "w2grp": 2, "gate_a": 1, "gate_b": 2, "hgrp": 5, "sig": 6, "res": 5}
+BUFS = {"vflat": 2, "vgrp": 2, "wtgrp": 3, "w2grp": 2, "gate_a": 1, "gate_b": 1, "gate_c": 1, "hgrp": 5, "sig": 6, "res": 5}
 RUN = 4
 XRUN = 4
 
@@ -130,9 +130,10 @@ def tile_rbm_mean_field_reconstruction_s7_kernel(tc, v_bytes, v_scale, w, beta, 
             cols = slice(a * KP, (a + 1) * KP)
             quantise(wt_codes[:, g, cols], wt_sc[:, g, cols], live["wt", g, a][:])
 
-        def weave_w(g, c, e, tag="w2grp"):
+        def weave_w(g, c, e, tag="w2grp", first=0, last=KP):
             live["w2", g, c] = staged(tag, (g, c), [P, KP, T], BF16)
-            weave(e, live["w2", g, c][:], live["w", g][:].rearrange("p (t v) -> p t v", t=T)[:, :, c * KP : (c + 1) * KP])
+            rows = live["w", g][:].rearrange("p (t v) -> p t v", t=T)
+            weave(e, live["w2", g, c][:, first:last, :], rows[:, :, c * KP + first : c * KP + last])
 
         def quant_down(g, c):
             cols = slice(c * KP, (c + 1) * KP)
@@ -273,7 +274,7 @@ def tile_rbm_mean_field_reconstruction_s7_kernel(tc, v_bytes, v_scale, w, beta, 
             quant_down(0, 0)
             weave_w(1, 0, "G", "gate_a")
             weave_w(2, 0, "G", "gate_b")
-            weave_w(3, 0, "G", "gate_b")
+            weave_w(3, 0, "G", "gate_c", last=3 * KP // 4)
             for g in range(1, NH):
                 scale_weave(0, g, True)
             for g in range(NH):
@@ -282,45 +283,55 @@ def tile_rbm_mean_field_reconstruction_s7_kernel(tc, v_bytes, v_scale, w, beta, 
             scale_weave(1, 1, True)
 
             weave_w(0, 1, "S")
-            weave_w(1, 1, "S")
+            weave_w(2, 1, "S", last=KP // 2)
             lo, hi = [0, 1, 2, 3], [4, 5, 6, 7]
             for g in range(NH):
                 if g > 0:
+                    if g == 2:
+                        weave_w(3, 0, "V", "gate_c", first=3 * KP // 4)
                     quant_h(0, g)
                     quant_down(g, 0)
                 down_pass(0, range(4), g, lo)
+            for j in range(4):
+                finish(0, j, "S")
             for g in range(2):
                 quant_h(1, g)
                 down_pass(1, range(2), g, hi)
             quant_down(0, 1)
+            weave_w(1, 1, "V", "gate_b")
+            weave_w(2, 1, "S", first=KP // 2)
             down_pass(1, range(2, 4), 0, hi)
-            weave_w(2, 1, "V")
-            for j in range(4):
-                finish(0, j, "S")
+            down_pass(0, range(4, 8), 0, lo)
+            scale_weave(1, 2, False)
             quant_down(1, 1)
             weave_w(3, 1, "S")
             down_pass(1, range(2, 4), 1)
-            for g in range(2):
-                down_pass(0, range(4, 8), g, lo)
-            scale_weave(1, 2, False)
-            quant_down(2, 1)
+            down_pass(0, range(4, 8), 1)
             scale_weave(1, 3, False)
             quant_h(1, 2)
-            down_pass(0, range(4, 8), 2)
-            down_pass(1, range(4), 2)
-            scale_weave(2, 0, False)
+            quant_down(2, 1)
             quant_h(1, 3)
+            down_pass(1, range(2), 2)
+            for j in range(2):
+                down_pass(1, [j], 3)
+                finish(1, j, "S")
+            down_pass(1, range(2, 4), 2)
+            down_pass(0, range(4, 8), 2)
+            scale_weave(2, 0, False)
             quant_down(3, 1)
-            down_pass(0, range(4, 8), 3)
             for j in range(4, 8):
+                down_pass(0, [j], 3)
                 finish(0, j, "S")
-            down_pass(1, range(4), 3)
-            for j in range(4):
+            for j in range(2, 4):
+                down_pass(1, [j], 3)
                 finish(1, j, "S")
             for g in range(NH):
                 if g + 1 < NH:
                     scale_weave(2, g + 1, False)
                 quant_h(2, g)
-                down_pass(2, range(4), g, lo)
+                if g < 2:
+                    down_pass(2, range(4), g, [4, 5, 0, 1])
             for j in range(4):
+                down_pass(2, [j], 2)
+                down_pass(2, [j], 3)
                 finish(2, j, "VS"[j % 2])

@@ -25,9 +25,10 @@ NBANKS = 8
 
 CHUNKS = [(0, 512), (512, 512)]
 PARTS = [(0, 512), (512, 256), (768, 256)]
-BUFS = {"vflat": 2, "vgrp": 2, "wtgrp": 3, "w2grp": 2, "gate_a": 1, "gate_b": 1, "gate_c": 1, "hgrp": 5, "sig": 6, "res": 5}
+BUFS = {"vflat": 2, "vgrp": 2, "wtgrp": 3, "w2grp": 2, "gate": 1, "hgrp": 5, "sig": 5, "res": 7, "hflat": 1}
 RUN = 4
 XRUN = 4
+TILES = [[(m, 1) for m in range(8)], [(m, 2) for m in range(0, 8, 2)], [(m, 2) for m in range(0, 8, 2)]]
 
 
 def tile_rbm_mean_field_reconstruction_s7_kernel(tc, v_bytes, v_scale, w, beta, out):
@@ -52,6 +53,7 @@ def tile_rbm_mean_field_reconstruction_s7_kernel(tc, v_bytes, v_scale, w, beta, 
         h_codes = keep.tile([P, NH, B], U32, name="h_codes", align_bytes=64)
         h_sc = keep.tile([P, NH, B], U8, name="h_sc", align_bytes=64)
 
+        w_rows = keep.tile([P, NH * T * V], BF16, name="w_rows", align_bytes=64)
         zeros = keep.tile([P, BANK], F32, name="zeros")
         live = {}
         copy_on = {"V": nc.vector.tensor_copy, "S": nc.scalar.copy}
@@ -67,10 +69,7 @@ def tile_rbm_mean_field_reconstruction_s7_kernel(tc, v_bytes, v_scale, w, beta, 
         def weave(e, dst, src):
             o = dst.rearrange("p (c i) t -> p c t i", i=RUN)
             s = src.rearrange("p t (c i) -> p c t i", i=RUN)
-            if e == "G":
-                nc.gpsimd.tensor_scalar(out=dst, in0=src.rearrange("p t n -> p n t"), scalar1=1.0, scalar2=0.0, op0=ALU.mult, op1=ALU.add)
-            else:
-                copy_on[e](out=o, in_=s)
+            copy_on[e](out=o, in_=s)
 
         def quantise(codes, scales, grouped):
             nc.vector.quantize_mx(out=codes.bitcast(FP8X4), scales=scales, in_=grouped.rearrange("p n t -> p (n t)"))
@@ -84,17 +83,18 @@ def tile_rbm_mean_field_reconstruction_s7_kernel(tc, v_bytes, v_scale, w, beta, 
             nc.scalar.activation(out=dummy[:], in_=zeros[:, 0:1], func=ACT.Sigmoid)
             nc.gpsimd.tensor_copy(out=beta32[:], in_=beta_bf[:])
 
-        def load_v(c, lo, hi):
+        def load_v(c, lo, hi, pieces=1):
             first, last = CHUNKS[lo][0], CHUNKS[hi - 1][0] + CHUNKS[hi - 1][1]
             raw = keep.tile([P, T, last - first], U8, name="v_raw%d_%d" % (c, lo), align_bytes=64)
-            nc.sync.dma_start(out=raw[:], in_=v_view[c][:, :, first:last])
+            for i in range(pieces):
+                rows = slice(i * T // pieces, (i + 1) * T // pieces)
+                nc.sync.dma_start(out=raw[:, rows, :], in_=v_view[c][:, rows, first:last])
             for n in range(lo, hi):
                 live["vraw", c, n] = raw[:, :, CHUNKS[n][0] - first : CHUNKS[n][0] - first + CHUNKS[n][1]]
 
         def load_w(g, a):
-            if a == 0:
-                live["w", g] = keep.tile([P, T * V], BF16, name="w_rows%d" % g, align_bytes=64)
-            nc.sync.dma_start(out=live["w", g][:, 2 * a * V : 2 * (a + 1) * V], in_=w_view[g][:, 2 * a * V : 2 * (a + 1) * V])
+            first = (g * T + 2 * a) * V
+            nc.sync.dma_start(out=w_rows[:, first : first + 2 * V], in_=w_view[g][:, 2 * a * V : 2 * (a + 1) * V])
 
         def widen(c, n, t, e):
             flat = staged("vflat", (c, n), [P, T, CHUNKS[n][1]], BF16)
@@ -113,9 +113,9 @@ def tile_rbm_mean_field_reconstruction_s7_kernel(tc, v_bytes, v_scale, w, beta, 
         def turn(g, a, c, b):
             bank = psum.tile([P, BANK], F32, name="bank%d" % b)
             live["tb", g, a, c] = bank
-            words = live["w", g][:].bitcast(F32)
+            words = w_rows[:].bitcast(F32)
             for i in range(2):
-                first = (2 * a + i) * V // 2 + c * KP // 2
+                first = (g * T + 2 * a + i) * V // 2 + c * KP // 2
                 for u in range(2):
                     j = (2 * i + u) * P
                     nc.tensor.transpose(bank[:, j : j + P], words[:, first + u : first + 2 * P : 2], ident[:])
@@ -131,13 +131,20 @@ def tile_rbm_mean_field_reconstruction_s7_kernel(tc, v_bytes, v_scale, w, beta, 
             quantise(wt_codes[:, g, cols], wt_sc[:, g, cols], live["wt", g, a][:])
 
         def weave_w(g, c, e, tag="w2grp", first=0, last=KP):
-            live["w2", g, c] = staged(tag, (g, c), [P, KP, T], BF16)
-            rows = live["w", g][:].rearrange("p (t v) -> p t v", t=T)
+            live["w2", g, c] = staged(tag, (g, c), [P, KP, T], BF16)[:]
+            rows = w_rows[:].rearrange("p (g t v) -> p g t v", g=NH, t=T)[:, g]
             weave(e, live["w2", g, c][:, first:last, :], rows[:, :, c * KP + first : c * KP + last])
+
+        def weave_w_beside(lo, hi, c):
+            grouped = staged("gate", (lo, c), [P, hi - lo, KP, T], BF16)
+            for g in range(lo, hi):
+                live["w2", g, c] = grouped[:, g - lo]
+            rows = w_rows[:].rearrange("p (g t v) -> p g v t", g=NH, t=T)[:, lo:hi, c * KP : (c + 1) * KP, :]
+            nc.gpsimd.tensor_scalar(out=grouped[:], in0=rows, scalar1=1.0, scalar2=0.0, op0=ALU.mult, op1=ALU.add)
 
         def quant_down(g, c):
             cols = slice(c * KP, (c + 1) * KP)
-            quantise(w2_codes[:, g, cols], w2_sc[:, g, cols], live["w2", g, c][:])
+            quantise(w2_codes[:, g, cols], w2_sc[:, g, cols], live["w2", g, c])
 
         def warm_up(cols):
             bank = psum.tile([P, BANK], F32, name="bank6")
@@ -176,32 +183,44 @@ def tile_rbm_mean_field_reconstruction_s7_kernel(tc, v_bytes, v_scale, w, beta, 
                 in1=factors[:, g, :].unsqueeze(1).unsqueeze(3).to_broadcast([P, width // XRUN, T, XRUN]),
                 op=ALU.mult)
 
+        def scale_rows(d, g):
+            first, width = PARTS[d]
+            n = first // BANK
+            flat = staged("hflat", (d, g), [P, T, width], BF16)
+            for t in range(T):
+                nc.scalar.activation(out=flat[:, t, :], in_=live["sig", (n, g)][:, t, first - n * BANK : first - n * BANK + width],
+                                     func=ACT.Copy, scale=beta32[:, g, t : t + 1])
+
+        def weave_h(d, g):
+            live["h", d, g] = staged("hgrp", ("h", d, g), [P, PARTS[d][1], T], BF16)
+            weave("V", live["h", d, g][:], live["hflat", (d, g)][:])
+
         def quant_h(d, g):
             quantise(h_codes[:, g, part_samples(d)], h_sc[:, g, part_samples(d)], live["h", d, g][:])
 
         def down(d, j, g, b, first, last):
             width = PARTS[d][1]
-            per = BANK // width
+            m0, count = TILES[d][j]
             if first:
                 live["nb", d, j] = psum.tile([P, BANK], F32, name="bank%d" % b)
-            for i in range(per):
-                mc = slice((j * per + i) * P, (j * per + i + 1) * P)
+            for i in range(count):
+                mc = slice((m0 + i) * P, (m0 + i + 1) * P)
                 nc.tensor.matmul_mx(out=live["nb", d, j][:, i * width : (i + 1) * width],
                                     lhsT=w2_codes[:, g, mc].bitcast(FP8X4), lhsT_scale=w2_sc[:, g, mc],
                                     rhs=h_codes[:, g, part_samples(d)].bitcast(FP8X4), rhs_scale=h_sc[:, g, part_samples(d)],
-                                    start=(first and i == 0), stop=(last and i == per - 1))
+                                    start=(first and i == 0), stop=(last and i == count - 1))
 
         def finish(d, j, e):
             width = PARTS[d][1]
-            per = BANK // width
-            res = staged("res", (d, j), [P, BANK], F32)
-            copy_on[e](out=res[:], in_=live["nb", d, j][:])
-            rows = out.rearrange("(j i p) n -> j p i n", i=per, p=P)[j]
-            nc.sync.dma_start(out=rows[:, :, part_samples(d)], in_=res[:].rearrange("p (i n) -> p i n", i=per))
+            m0, count = TILES[d][j]
+            res = staged("res", (d, j), [P, count * width], F32)
+            copy_on[e](out=res[:], in_=live["nb", d, j][:, 0 : count * width])
+            rows = out[m0 * P : (m0 + count) * P, part_samples(d)].rearrange("(i p) n -> p i n", p=P)
+            nc.sync.dma_start(out=rows, in_=res[:].rearrange("p (i n) -> p i n", i=count))
 
         with tc.manual_schedule():
             small_loads()
-            load_v(0, 0, 1)
+            load_v(0, 0, 1, 2)
             load_v(1, 0, 1)
             for g in range(NH):
                 load_w(g, 0)
@@ -218,7 +237,7 @@ def tile_rbm_mean_field_reconstruction_s7_kernel(tc, v_bytes, v_scale, w, beta, 
             def turn_unit(g, a, tag="wtgrp", last="S"):
                 for c in range(NV):
                     turn(g, a, c, bank())
-                    if c == 0 or last == "S":
+                    if last == "S":
                         empty_turn(g, a, c, "S", tag)
 
             def up_group(n, g):
@@ -240,23 +259,29 @@ def tile_rbm_mean_field_reconstruction_s7_kernel(tc, v_bytes, v_scale, w, beta, 
             turn_unit(0, 1)
             warm_up(BANK // 2)
             weave_v(0, 0, "V")
-            quant_v(0, 0)
             weave_v(1, 0, "V")
+            quant_v(0, 0)
             quant_up(0, 0)
             quant_v(1, 0)
             quant_up(0, 1)
             turn_unit(1, 0)
-            turn_unit(1, 1, "gate_a")
+            turn_unit(1, 1, "gate")
             up_group(0, 0)
-            for c in range(NV):
-                for t in range(T):
-                    widen(c, 1, t, "V")
-                quant_up(1, c)
+            widen(0, 1, 0, "V")
+            widen(0, 1, 1, "V")
+            quant_up(1, 0)
+            widen(0, 1, 2, "V")
+            widen(0, 1, 3, "V")
+            widen(1, 1, 0, "V")
+            quant_up(1, 1)
             turn_unit(2, 0)
             turn_unit(2, 1, last="V")
-            weave_w(0, 0, "G", "gate_a")
+            weave_w_beside(0, 1, 0)
             scale_weave(0, 0, True)
+            empty_turn(2, 1, 0, "V")
             empty_turn(2, 1, 1, "V")
+            for t in range(1, T):
+                widen(1, 1, t, "S")
             up_group(0, 1)
             weave_v(0, 1, "V")
             quant_up(2, 0)
@@ -272,9 +297,7 @@ def tile_rbm_mean_field_reconstruction_s7_kernel(tc, v_bytes, v_scale, w, beta, 
             quant_h(0, 0)
             up_group(0, 3)
             quant_down(0, 0)
-            weave_w(1, 0, "G", "gate_a")
-            weave_w(2, 0, "G", "gate_b")
-            weave_w(3, 0, "G", "gate_c", last=3 * KP // 4)
+            weave_w_beside(1, NH, 0)
             for g in range(1, NH):
                 scale_weave(0, g, True)
             for g in range(NH):
@@ -283,12 +306,9 @@ def tile_rbm_mean_field_reconstruction_s7_kernel(tc, v_bytes, v_scale, w, beta, 
             scale_weave(1, 1, True)
 
             weave_w(0, 1, "S")
-            weave_w(2, 1, "S", last=KP // 2)
             lo, hi = [0, 1, 2, 3], [4, 5, 6, 7]
             for g in range(NH):
                 if g > 0:
-                    if g == 2:
-                        weave_w(3, 0, "V", "gate_c", first=3 * KP // 4)
                     quant_h(0, g)
                     quant_down(g, 0)
                 down_pass(0, range(4), g, lo)
@@ -297,26 +317,28 @@ def tile_rbm_mean_field_reconstruction_s7_kernel(tc, v_bytes, v_scale, w, beta, 
             for g in range(2):
                 quant_h(1, g)
                 down_pass(1, range(2), g, hi)
+            weave_w(1, 1, "V", "gate")
             quant_down(0, 1)
-            weave_w(1, 1, "V", "gate_b")
-            weave_w(2, 1, "S", first=KP // 2)
+            weave_w(2, 1, "S")
             down_pass(1, range(2, 4), 0, hi)
             down_pass(0, range(4, 8), 0, lo)
             scale_weave(1, 2, False)
             quant_down(1, 1)
-            weave_w(3, 1, "S")
+            weave_w(3, 1, "S", last=3 * KP // 4)
             down_pass(1, range(2, 4), 1)
             down_pass(0, range(4, 8), 1)
             scale_weave(1, 3, False)
             quant_h(1, 2)
-            quant_down(2, 1)
             quant_h(1, 3)
+            quant_down(2, 1)
             down_pass(1, range(2), 2)
             for j in range(2):
                 down_pass(1, [j], 3)
                 finish(1, j, "S")
+            scale_rows(2, 3)
             down_pass(1, range(2, 4), 2)
             down_pass(0, range(4, 8), 2)
+            weave_w(3, 1, "V", first=3 * KP // 4)
             scale_weave(2, 0, False)
             quant_down(3, 1)
             for j in range(4, 8):
@@ -326,8 +348,10 @@ def tile_rbm_mean_field_reconstruction_s7_kernel(tc, v_bytes, v_scale, w, beta, 
                 down_pass(1, [j], 3)
                 finish(1, j, "S")
             for g in range(NH):
-                if g + 1 < NH:
+                if g + 2 < NH:
                     scale_weave(2, g + 1, False)
+                elif g + 1 < NH:
+                    weave_h(2, g + 1)
                 quant_h(2, g)
                 if g < 2:
                     down_pass(2, range(4), g, [4, 5, 0, 1])

@@ -237,7 +237,7 @@ def tile_rbm_mean_field_reconstruction_s7_kernel(tc, v_bytes, v_scale, w, beta, 
             def turn_unit(g, a, tag="wtgrp", last="S"):
                 for c in range(NV):
                     turn(g, a, c, bank())
-                    if last == "S":
+                    if c == 0 or last == "S":
                         empty_turn(g, a, c, "S", tag)
 
             def up_group(n, g):
@@ -254,7 +254,8 @@ def tile_rbm_mean_field_reconstruction_s7_kernel(tc, v_bytes, v_scale, w, beta, 
             beta_to_bank(7)
             for t in range(T):
                 widen(0, 0, t, "V")
-                widen(1, 0, t, "S")
+            for t in range(T):
+                widen(1, 0, t, "S" if t < 3 else "V")
             turn_unit(0, 0)
             turn_unit(0, 1)
             warm_up(BANK // 2)
@@ -267,23 +268,19 @@ def tile_rbm_mean_field_reconstruction_s7_kernel(tc, v_bytes, v_scale, w, beta, 
             turn_unit(1, 0)
             turn_unit(1, 1, "gate")
             up_group(0, 0)
-            widen(0, 1, 0, "V")
-            widen(0, 1, 1, "V")
+            for t in range(T):
+                widen(0, 1, t, "V")
             quant_up(1, 0)
-            widen(0, 1, 2, "V")
-            widen(0, 1, 3, "V")
-            widen(1, 1, 0, "V")
+            for t in range(T):
+                widen(1, 1, t, "V")
+            weave_v(0, 1, "V")
             quant_up(1, 1)
             turn_unit(2, 0)
             turn_unit(2, 1, last="V")
             weave_w_beside(0, 1, 0)
             scale_weave(0, 0, True)
-            empty_turn(2, 1, 0, "V")
             empty_turn(2, 1, 1, "V")
-            for t in range(1, T):
-                widen(1, 1, t, "S")
             up_group(0, 1)
-            weave_v(0, 1, "V")
             quant_up(2, 0)
             quant_up(2, 1)
             turn_unit(3, 0)
@@ -303,7 +300,6 @@ def tile_rbm_mean_field_reconstruction_s7_kernel(tc, v_bytes, v_scale, w, beta, 
             for g in range(NH):
                 up_group(1, g)
             scale_weave(1, 0, True)
-            scale_weave(1, 1, True)
 
             weave_w(0, 1, "S")
             lo, hi = [0, 1, 2, 3], [4, 5, 6, 7]
@@ -314,32 +310,32 @@ def tile_rbm_mean_field_reconstruction_s7_kernel(tc, v_bytes, v_scale, w, beta, 
                 down_pass(0, range(4), g, lo)
             for j in range(4):
                 finish(0, j, "S")
-            for g in range(2):
-                quant_h(1, g)
-                down_pass(1, range(2), g, hi)
-            weave_w(1, 1, "V", "gate")
+            quant_h(1, 0)
+            down_pass(1, range(2), 0, hi)
+            scale_weave(1, 1, False)
             quant_down(0, 1)
+            quant_h(1, 1)
+            weave_w(1, 1, "V", "gate")
             weave_w(2, 1, "S")
             down_pass(1, range(2, 4), 0, hi)
             down_pass(0, range(4, 8), 0, lo)
-            scale_weave(1, 2, False)
+            down_pass(1, range(2), 1)
             quant_down(1, 1)
-            weave_w(3, 1, "S", last=3 * KP // 4)
+            weave_w(3, 1, "S")
             down_pass(1, range(2, 4), 1)
             down_pass(0, range(4, 8), 1)
-            scale_weave(1, 3, False)
-            quant_h(1, 2)
-            quant_h(1, 3)
+            scale_weave(1, 2, False)
             quant_down(2, 1)
-            down_pass(1, range(2), 2)
+            quant_h(1, 2)
+            down_pass(0, range(4, 8), 2)
+            down_pass(1, range(4), 2)
+            scale_weave(1, 3, False)
+            scale_rows(2, 3)
+            scale_weave(2, 0, False)
+            quant_h(1, 3)
             for j in range(2):
                 down_pass(1, [j], 3)
                 finish(1, j, "S")
-            scale_rows(2, 3)
-            down_pass(1, range(2, 4), 2)
-            down_pass(0, range(4, 8), 2)
-            weave_w(3, 1, "V", first=3 * KP // 4)
-            scale_weave(2, 0, False)
             quant_down(3, 1)
             for j in range(4, 8):
                 down_pass(0, [j], 3)

@@ -25,7 +25,7 @@ NBANKS = 8
 
 CHUNKS = [(0, 512), (512, 512)]
 PARTS = [(0, 512), (512, 256), (768, 256)]
-BUFS = {"vflat": 2, "vgrp": 2, "wtgrp": 3, "w2grp": 2, "gate": 1, "hgrp": 5, "sig": 5, "res": 7, "hflat": 1}
+BUFS = {"vflat": 2, "vgrp": 2, "wtgrp": 3, "w2grp": 1, "late": 1, "gate": 1, "hgrp": 5, "sig": 5, "res": 7}
 RUN = 4
 XRUN = 4
 TILES = [[(m, 1) for m in range(8)], [(m, 2) for m in range(0, 8, 2)], [(m, 2) for m in range(0, 8, 2)]]
@@ -135,12 +135,16 @@ def tile_rbm_mean_field_reconstruction_s7_kernel(tc, v_bytes, v_scale, w, beta, 
             rows = w_rows[:].rearrange("p (g t v) -> p g t v", g=NH, t=T)[:, g]
             weave(e, live["w2", g, c][:, first:last, :], rows[:, :, c * KP + first : c * KP + last])
 
-        def weave_w_beside(lo, hi, c):
-            grouped = staged("gate", (lo, c), [P, hi - lo, KP, T], BF16)
+        def weave_w_beside(lo, hi, c, tag="gate", last=KP):
+            grouped = staged(tag, (lo, c), [P, hi - lo, KP, T], BF16)
             for g in range(lo, hi):
                 live["w2", g, c] = grouped[:, g - lo]
-            rows = w_rows[:].rearrange("p (g t v) -> p g v t", g=NH, t=T)[:, lo:hi, c * KP : (c + 1) * KP, :]
-            nc.gpsimd.tensor_scalar(out=grouped[:], in0=rows, scalar1=1.0, scalar2=0.0, op0=ALU.mult, op1=ALU.add)
+            rows = w_rows[:].rearrange("p (g t v) -> p g v t", g=NH, t=T)[:, lo:hi, c * KP : c * KP + last, :]
+            nc.gpsimd.tensor_scalar(out=grouped[:, :, 0:last, :], in0=rows, scalar1=1.0, scalar2=0.0, op0=ALU.mult, op1=ALU.add)
+
+        def weave_w_rest(g, c, first):
+            rows = w_rows[:].rearrange("p (g t v) -> p g t v", g=NH, t=T)[:, g]
+            weave("V", live["w2", g, c][:, first:KP, :], rows[:, :, c * KP + first : (c + 1) * KP])
 
         def quant_down(g, c):
             cols = slice(c * KP, (c + 1) * KP)
@@ -276,10 +280,9 @@ def tile_rbm_mean_field_reconstruction_s7_kernel(tc, v_bytes, v_scale, w, beta, 
             weave_v(0, 1, "V")
             quant_up(1, 1)
             turn_unit(2, 0)
-            turn_unit(2, 1, last="V")
-            weave_w_beside(0, 1, 0)
+            turn_unit(2, 1)
+            weave_w_beside(0, 1, 0, last=3 * KP // 4)
             scale_weave(0, 0, True)
-            empty_turn(2, 1, 1, "V")
             up_group(0, 1)
             quant_up(2, 0)
             quant_up(2, 1)
@@ -291,6 +294,7 @@ def tile_rbm_mean_field_reconstruction_s7_kernel(tc, v_bytes, v_scale, w, beta, 
             quant_up(3, 1)
             quant_v(0, 1)
             quant_v(1, 1)
+            weave_w_rest(0, 0, 3 * KP // 4)
             quant_h(0, 0)
             up_group(0, 3)
             quant_down(0, 0)
@@ -301,57 +305,56 @@ def tile_rbm_mean_field_reconstruction_s7_kernel(tc, v_bytes, v_scale, w, beta, 
                 up_group(1, g)
             scale_weave(1, 0, True)
 
-            weave_w(0, 1, "S")
+            weave_w(0, 1, "S", "late")
             lo, hi = [0, 1, 2, 3], [4, 5, 6, 7]
             for g in range(NH):
                 if g > 0:
                     quant_h(0, g)
                     quant_down(g, 0)
                 down_pass(0, range(4), g, lo)
+            quant_h(1, 0)
+            quant_down(0, 1)
             for j in range(4):
                 finish(0, j, "S")
-            quant_h(1, 0)
-            down_pass(1, range(2), 0, hi)
-            scale_weave(1, 1, False)
-            quant_down(0, 1)
-            quant_h(1, 1)
-            weave_w(1, 1, "V", "gate")
-            weave_w(2, 1, "S")
-            down_pass(1, range(2, 4), 0, hi)
-            down_pass(0, range(4, 8), 0, lo)
-            down_pass(1, range(2), 1)
-            quant_down(1, 1)
+            weave_w_beside(1, 2, 1, "late", 3 * KP // 4)
+            weave_w(2, 1, "S", "gate")
             weave_w(3, 1, "S")
-            down_pass(1, range(2, 4), 1)
-            down_pass(0, range(4, 8), 1)
-            scale_weave(1, 2, False)
-            quant_down(2, 1)
+            scale_weave(1, 1, True)
+            scale_weave(1, 2, True)
+            down_pass(1, range(3), 0, hi)
+            down_pass(0, range(4, 8), 0, lo)
+            quant_h(1, 1)
+            weave_w_rest(1, 1, 3 * KP // 4)
             quant_h(1, 2)
-            down_pass(0, range(4, 8), 2)
-            down_pass(1, range(4), 2)
+            for g in range(1, 3):
+                down_pass(1, range(2), g)
+            down_pass(1, [3], 0, hi)
+            quant_down(1, 1)
+            down_pass(0, range(4, 8), 1)
+            down_pass(1, range(2, 4), 1)
             scale_weave(1, 3, False)
-            scale_rows(2, 3)
-            scale_weave(2, 0, False)
+            quant_down(2, 1)
             quant_h(1, 3)
             for j in range(2):
                 down_pass(1, [j], 3)
                 finish(1, j, "S")
+            scale_weave(2, 0, False)
             quant_down(3, 1)
+            down_pass(0, range(4, 8), 2)
             for j in range(4, 8):
                 down_pass(0, [j], 3)
                 finish(0, j, "S")
             for j in range(2, 4):
+                down_pass(1, [j], 2)
                 down_pass(1, [j], 3)
                 finish(1, j, "S")
             for g in range(NH):
-                if g + 2 < NH:
+                if g + 1 < NH:
                     scale_weave(2, g + 1, False)
-                elif g + 1 < NH:
-                    weave_h(2, g + 1)
                 quant_h(2, g)
                 if g < 2:
                     down_pass(2, range(4), g, [4, 5, 0, 1])
             for j in range(4):
-                down_pass(2, [j], 2)
-                down_pass(2, [j], 3)
+                for g in range(2, NH):
+                    down_pass(2, [j], g)
                 finish(2, j, "VS"[j % 2])

@@ -25,10 +25,12 @@ NBANKS = 8
 
 CHUNKS = [(0, 512), (512, 512)]
 PARTS = [(0, 512), (512, 256), (768, 256)]
-BUFS = {"vflat": 2, "vgrp": 2, "wtgrp": 3, "w2grp": 1, "late": 1, "gate": 1, "hgrp": 5, "sig": 5, "res": 7}
+BUFS = {"vflat": 2, "vgrp": 2, "wtgrp": 3, "w2grp": 1, "late": 1, "gate": 1, "hgrp": 5, "sig": 5, "res": 7, "hflat": 1}
 RUN = 4
 XRUN = 4
-TILES = [[(m, 1) for m in range(8)], [(m, 2) for m in range(0, 8, 2)], [(m, 2) for m in range(0, 8, 2)]]
+TILES = [[(m, 1) for m in range(8)], [(m, 2) for m in range(0, 8, 2)], [(0, 2), (2, 2), (4, 2), (6, 1), (7, 1)]]
+SHARE = 320
+LONG = 480
 
 
 def tile_rbm_mean_field_reconstruction_s7_kernel(tc, v_bytes, v_scale, w, beta, out):
@@ -137,10 +139,16 @@ def tile_rbm_mean_field_reconstruction_s7_kernel(tc, v_bytes, v_scale, w, beta, 
 
         def weave_w_beside(lo, hi, c, tag="gate", last=KP):
             grouped = staged(tag, (lo, c), [P, hi - lo, KP, T], BF16)
+            live["beside", lo, c] = grouped
             for g in range(lo, hi):
                 live["w2", g, c] = grouped[:, g - lo]
             rows = w_rows[:].rearrange("p (g t v) -> p g v t", g=NH, t=T)[:, lo:hi, c * KP : c * KP + last, :]
             nc.gpsimd.tensor_scalar(out=grouped[:, :, 0:last, :], in0=rows, scalar1=1.0, scalar2=0.0, op0=ALU.mult, op1=ALU.add)
+
+        def weave_w_left(lo, hi, c, first):
+            rows = w_rows[:].rearrange("p (g t v) -> p g t v", g=NH, t=T)[:, lo:hi, :, c * KP + first : (c + 1) * KP]
+            nc.vector.tensor_copy(out=live["beside", lo, c][:, :, first:KP, :].rearrange("p g (c i) t -> p g c t i", i=RUN),
+                                  in_=rows.rearrange("p g t (c i) -> p g c t i", i=RUN))
 
         def weave_w_rest(g, c, first):
             rows = w_rows[:].rearrange("p (g t v) -> p g t v", g=NH, t=T)[:, g]
@@ -251,7 +259,7 @@ def tile_rbm_mean_field_reconstruction_s7_kernel(tc, v_bytes, v_scale, w, beta, 
 
             def down_pass(n, js, g, banks=None):
                 for j in js:
-                    down(n, j, g, (banks[j % 4] if banks else bank()) if g == 0 else 0, g == 0, g == NH - 1)
+                    down(n, j, g, (banks[j % len(banks)] if banks else bank()) if g == 0 else 0, g == 0, g == NH - 1)
 
             warm_up(BANK)
             warm_up(BANK)
@@ -291,14 +299,14 @@ def tile_rbm_mean_field_reconstruction_s7_kernel(tc, v_bytes, v_scale, w, beta, 
             up_group(0, 2)
             weave_v(1, 1, "V")
             quant_up(3, 0)
-            quant_up(3, 1)
             quant_v(0, 1)
+            quant_up(3, 1)
             quant_v(1, 1)
             weave_w_rest(0, 0, 3 * KP // 4)
             quant_h(0, 0)
             up_group(0, 3)
             quant_down(0, 0)
-            weave_w_beside(1, NH, 0)
+            weave_w_beside(1, NH, 0, last=LONG)
             for g in range(1, NH):
                 scale_weave(0, g, True)
             for g in range(NH):
@@ -308,6 +316,8 @@ def tile_rbm_mean_field_reconstruction_s7_kernel(tc, v_bytes, v_scale, w, beta, 
             weave_w(0, 1, "S", "late")
             lo, hi = [0, 1, 2, 3], [4, 5, 6, 7]
             for g in range(NH):
+                if g == 1:
+                    weave_w_left(1, NH, 0, LONG)
                 if g > 0:
                     quant_h(0, g)
                     quant_down(g, 0)
@@ -316,15 +326,16 @@ def tile_rbm_mean_field_reconstruction_s7_kernel(tc, v_bytes, v_scale, w, beta, 
             quant_down(0, 1)
             for j in range(4):
                 finish(0, j, "S")
-            weave_w_beside(1, 2, 1, "late", 3 * KP // 4)
+            weave_w_beside(1, 2, 1, "late", SHARE)
             weave_w(2, 1, "S", "gate")
             weave_w(3, 1, "S")
+            scale_rows(2, 3)
             scale_weave(1, 1, True)
             scale_weave(1, 2, True)
             down_pass(1, range(3), 0, hi)
             down_pass(0, range(4, 8), 0, lo)
             quant_h(1, 1)
-            weave_w_rest(1, 1, 3 * KP // 4)
+            weave_w_rest(1, 1, SHARE)
             quant_h(1, 2)
             for g in range(1, 3):
                 down_pass(1, range(2), g)
@@ -349,12 +360,16 @@ def tile_rbm_mean_field_reconstruction_s7_kernel(tc, v_bytes, v_scale, w, beta, 
                 down_pass(1, [j], 3)
                 finish(1, j, "S")
             for g in range(NH):
-                if g + 1 < NH:
+                if g + 2 < NH:
                     scale_weave(2, g + 1, False)
+                elif g + 1 < NH:
+                    weave_h(2, g + 1)
                 quant_h(2, g)
-                if g < 2:
-                    down_pass(2, range(4), g, [4, 5, 0, 1])
-            for j in range(4):
-                for g in range(2, NH):
+                if g == 0:
+                    down_pass(2, range(5), g, [4, 5, 0, 1, 2])
+                elif g < NH - 1:
+                    down_pass(2, range(2), g)
+            for j in range(5):
+                for g in range(NH - 1 if j < 2 else 1, NH):
                     down_pass(2, [j], g)
                 finish(2, j, "VS"[j % 2])

@@ -21,16 +21,10 @@ KP = P * T
 NV = V // KP
 NH = H // KP
 BANK = 512
-NBANKS = 8
-
-CHUNKS = [(0, 512), (512, 512)]
-PARTS = [(0, 512), (512, 256), (768, 256)]
-BUFS = {"vflat": 2, "vgrp": 2, "wtgrp": 3, "w2grp": 1, "late": 1, "gate": 1, "hgrp": 5, "sig": 5, "res": 7, "hflat": 1}
+BETA_BANK = 7
 RUN = 4
-XRUN = 4
-TILES = [[(m, 1) for m in range(8)], [(m, 2) for m in range(0, 8, 2)], [(0, 2), (2, 2), (4, 2), (6, 1), (7, 1)]]
-SHARE = 320
-LONG = 480
+BUFS = {"vflat": 4, "vgrp": 2, "wtgrp": 3, "w2grp": 1, "gate_a": 1, "gate_b": 1, "gate_c": 1, "hgrp": 3, "sig": 4, "res": 8}
+SHARE_A = 128
 
 
 def tile_rbm_mean_field_reconstruction_s7_kernel(tc, v_bytes, v_scale, w, beta, out):
@@ -50,23 +44,28 @@ def tile_rbm_mean_field_reconstruction_s7_kernel(tc, v_bytes, v_scale, w, beta, 
         v_sc = keep.tile([P, NV, B], U8, name="v_sc", align_bytes=64)
         wt_codes = keep.tile([P, NH, 2 * KP], U32, name="wt_codes", align_bytes=64)
         wt_sc = keep.tile([P, NH, 2 * KP], U8, name="wt_sc", align_bytes=64)
-        w2_codes = keep.tile([P, NH, V], U32, name="w2_codes", align_bytes=64)
-        w2_sc = keep.tile([P, NH, V], U8, name="w2_sc", align_bytes=64)
+        w2_codes = keep.tile([P, 2 * NH, KP], U32, name="w2_codes", align_bytes=64)
+        w2_sc = keep.tile([P, 2 * NH, KP], U8, name="w2_sc", align_bytes=64)
         h_codes = keep.tile([P, NH, B], U32, name="h_codes", align_bytes=64)
         h_sc = keep.tile([P, NH, B], U8, name="h_sc", align_bytes=64)
-
         w_rows = keep.tile([P, NH * T * V], BF16, name="w_rows", align_bytes=64)
         zeros = keep.tile([P, BANK], F32, name="zeros")
         live = {}
         copy_on = {"V": nc.vector.tensor_copy, "S": nc.scalar.copy}
+        w_gtv = w_rows[:].rearrange("p (g t v) -> p g t v", g=NH, t=T)
+        w_gvt = w_rows[:].rearrange("p (g t v) -> p g v t", g=NH, t=T)
 
         def samples(n):
-            return slice(CHUNKS[n][0], CHUNKS[n][0] + CHUNKS[n][1])
+            return slice(n * BANK, (n + 1) * BANK)
 
         def staged(tag, key, shape, dtype):
-            if (tag, key) not in live:
-                live[tag, key] = rot.tile(shape, dtype, name=tag, align_bytes=64, bufs=BUFS[tag])
-            return live[tag, key]
+            if key not in live:
+                live[key] = rot.tile(shape, dtype, name=tag, align_bytes=64, bufs=BUFS[tag])
+            return live[key]
+
+        def new_bank(key, b):
+            live[key] = psum.tile([P, BANK], F32, name="bank%d" % b)
+            return live[key]
 
         def weave(e, dst, src):
             o = dst.rearrange("p (c i) t -> p c t i", i=RUN)
@@ -83,293 +82,287 @@ def tile_rbm_mean_field_reconstruction_s7_kernel(tc, v_bytes, v_scale, w, beta, 
             dummy = keep.tile([P, 1], F32, name="dummy")
             nc.vector.memset(zeros[:], 0.0)
             nc.scalar.activation(out=dummy[:], in_=zeros[:, 0:1], func=ACT.Sigmoid)
-            nc.gpsimd.tensor_copy(out=beta32[:], in_=beta_bf[:])
 
-        def load_v(c, lo, hi, pieces=1):
-            first, last = CHUNKS[lo][0], CHUNKS[hi - 1][0] + CHUNKS[hi - 1][1]
-            raw = keep.tile([P, T, last - first], U8, name="v_raw%d_%d" % (c, lo), align_bytes=64)
-            for i in range(pieces):
-                rows = slice(i * T // pieces, (i + 1) * T // pieces)
-                nc.sync.dma_start(out=raw[:, rows, :], in_=v_view[c][:, rows, first:last])
+        def load_v(c, a, lo, hi):
+            raw = keep.tile([P, 2, (hi - lo) * BANK], U8, name="v_raw%d_%d_%d" % (c, a, lo), align_bytes=64)
+            nc.sync.dma_start(out=raw[:], in_=v_view[c][:, 2 * a : 2 * a + 2, lo * BANK : hi * BANK])
             for n in range(lo, hi):
-                live["vraw", c, n] = raw[:, :, CHUNKS[n][0] - first : CHUNKS[n][0] - first + CHUNKS[n][1]]
+                for i in range(2):
+                    live["vraw", c, n, 2 * a + i] = raw[:, i, (n - lo) * BANK : (n - lo + 1) * BANK]
 
         def load_w(g, a):
             first = (g * T + 2 * a) * V
             nc.sync.dma_start(out=w_rows[:, first : first + 2 * V], in_=w_view[g][:, 2 * a * V : 2 * (a + 1) * V])
 
-        def widen(c, n, t, e):
-            flat = staged("vflat", (c, n), [P, T, CHUNKS[n][1]], BF16)
-            src = live["vraw", c, n][:, t, :].bitcast(FP8)
-            if e == "V":
-                nc.vector.tensor_scalar(out=flat[:, t, :], in0=src, scalar1=vs[:, c, t : t + 1], scalar2=None, op0=ALU.mult)
-            else:
-                nc.scalar.activation(out=flat[:, t, :], in_=src, func=ACT.Copy, scale=vs[:, c, t : t + 1])
+        def widen(e, c, n, ts):
+            flat = staged("vflat", ("vflat", c, n), [P, T, BANK], BF16)
+            for t in ts:
+                src = live["vraw", c, n, t].bitcast(FP8)
+                if e == "V":
+                    nc.vector.tensor_scalar(out=flat[:, t, :], in0=src, scalar1=vs[:, c, t : t + 1], scalar2=None, op0=ALU.mult)
+                else:
+                    nc.scalar.activation(out=flat[:, t, :], in_=src, func=ACT.Copy, scale=vs[:, c, t : t + 1])
 
-        def weave_v(c, n, e):
-            weave(e, staged("vgrp", (c, n), [P, CHUNKS[n][1], T], BF16)[:], live["vflat", (c, n)][:])
+        def weave_v(c, n, tag="vgrp"):
+            weave("V", staged(tag, ("vgrp", c, n), [P, BANK, T], BF16)[:], live["vflat", c, n][:])
 
         def quant_v(c, n):
-            quantise(v_codes[:, c, samples(n)], v_sc[:, c, samples(n)], live["vgrp", (c, n)][:])
+            quantise(v_codes[:, c, samples(n)], v_sc[:, c, samples(n)], live["vgrp", c, n][:])
 
-        def turn(g, a, c, b):
-            bank = psum.tile([P, BANK], F32, name="bank%d" % b)
-            live["tb", g, a, c] = bank
+        def turn(g, a, banks, tag="wtgrp"):
             words = w_rows[:].bitcast(F32)
-            for i in range(2):
-                first = (g * T + 2 * a + i) * V // 2 + c * KP // 2
-                for u in range(2):
-                    j = (2 * i + u) * P
-                    nc.tensor.transpose(bank[:, j : j + P], words[:, first + u : first + 2 * P : 2], ident[:])
-
-        def empty_turn(g, a, c, e, tag="wtgrp"):
-            grp = staged(tag, ("up", g, a), [P, KP, T], BF16)
-            live["wt", g, a] = grp
-            words = grp[:].rearrange("p m t -> p (m t)").bitcast(F32).rearrange("p (c i m u) -> p c i m u", c=NV, i=2, u=2)
-            copy_on[e](out=words[:, c], in_=live["tb", g, a, c][:].rearrange("p (i u m) -> p i m u", i=2, u=2))
+            grp = staged(tag, ("wt", g, a), [P, KP, T], BF16)
+            dst = grp[:].rearrange("p m t -> p (m t)").bitcast(F32).rearrange("p (c i m u) -> p c i m u", c=NV, i=2, u=2)
+            for c in range(NV):
+                bank = new_bank(("tb", g, a, c), banks[c])
+                for i in range(2):
+                    first = (g * T + 2 * a + i) * V // 2 + c * KP // 2
+                    for u in range(2):
+                        j = (2 * i + u) * P
+                        nc.tensor.transpose(bank[:, j : j + P], words[:, first + u : first + 2 * P : 2], ident[:])
+                nc.scalar.copy(out=dst[:, c], in_=bank[:].rearrange("p (i u m) -> p i m u", i=2, u=2))
 
         def quant_up(g, a):
             cols = slice(a * KP, (a + 1) * KP)
             quantise(wt_codes[:, g, cols], wt_sc[:, g, cols], live["wt", g, a][:])
 
-        def weave_w(g, c, e, tag="w2grp", first=0, last=KP):
-            live["w2", g, c] = staged(tag, (g, c), [P, KP, T], BF16)[:]
-            rows = w_rows[:].rearrange("p (g t v) -> p g t v", g=NH, t=T)[:, g]
-            weave(e, live["w2", g, c][:, first:last, :], rows[:, :, c * KP + first : c * KP + last])
-
-        def weave_w_beside(lo, hi, c, tag="gate", last=KP):
-            grouped = staged(tag, (lo, c), [P, hi - lo, KP, T], BF16)
-            live["beside", lo, c] = grouped
+        def left_tile(lo, hi, tag):
+            grouped = staged(tag, ("left", lo), [P, hi - lo, KP, T], BF16)
             for g in range(lo, hi):
-                live["w2", g, c] = grouped[:, g - lo]
-            rows = w_rows[:].rearrange("p (g t v) -> p g v t", g=NH, t=T)[:, lo:hi, c * KP : c * KP + last, :]
-            nc.gpsimd.tensor_scalar(out=grouped[:, :, 0:last, :], in0=rows, scalar1=1.0, scalar2=0.0, op0=ALU.mult, op1=ALU.add)
+                live["w2", g] = grouped[:, g - lo]
 
-        def weave_w_left(lo, hi, c, first):
-            rows = w_rows[:].rearrange("p (g t v) -> p g t v", g=NH, t=T)[:, lo:hi, :, c * KP + first : (c + 1) * KP]
-            nc.vector.tensor_copy(out=live["beside", lo, c][:, :, first:KP, :].rearrange("p g (c i) t -> p g c t i", i=RUN),
-                                  in_=rows.rearrange("p g t (c i) -> p g c t i", i=RUN))
+        def weave_left_beside(lo, hi, base, first=0, last=KP):
+            nc.gpsimd.tensor_scalar(out=live["left", base][:, lo - base : hi - base, first:last, :], in0=w_gvt[:, lo:hi, first:last, :],
+                                    scalar1=1.0, scalar2=0.0, op0=ALU.mult, op1=ALU.add)
 
-        def weave_w_rest(g, c, first):
-            rows = w_rows[:].rearrange("p (g t v) -> p g t v", g=NH, t=T)[:, g]
-            weave("V", live["w2", g, c][:, first:KP, :], rows[:, :, c * KP + first : (c + 1) * KP])
+        def weave_left(e, g, first=0, last=KP):
+            weave(e, live["w2", g][:, first:last, :], w_gtv[:, g, :, first:last])
 
-        def quant_down(g, c):
-            cols = slice(c * KP, (c + 1) * KP)
-            quantise(w2_codes[:, g, cols], w2_sc[:, g, cols], live["w2", g, c])
+        def right_tile(m, tag, lo=0, hi=NH):
+            staged(tag, ("right", m, lo), [P, hi - lo, P, T], BF16)
 
-        def warm_up(cols):
-            bank = psum.tile([P, BANK], F32, name="bank6")
+        def weave_right_beside(m, lo, hi):
+            nc.gpsimd.tensor_scalar(out=live["right", m, lo][:], in0=w_gvt[:, lo:hi, m * P : (m + 1) * P, :],
+                                    scalar1=1.0, scalar2=0.0, op0=ALU.mult, op1=ALU.add)
+
+        def weave_right(e, m):
+            copy_on[e](out=live["right", m, 0][:].rearrange("p g (c i) t -> p g c t i", i=RUN),
+                       in_=w_gtv[:, :, :, m * P : (m + 1) * P].rearrange("p g t (c i) -> p g c t i", i=RUN))
+
+        def quant_left(g):
+            quantise(w2_codes[:, g, :], w2_sc[:, g, :], live["w2", g])
+
+        def quant_right(m, lo=0, hi=NH):
+            cols = slice(lo * P, hi * P)
+            quantise(w2_codes[:, m, cols], w2_sc[:, m, cols], live["right", m, lo][:].rearrange("p g v t -> p (g v) t"))
+
+        def warm_up(cols, b):
+            bank = new_bank("warm", b)
             nc.tensor.matmul(out=bank[:, 0:cols], lhsT=zeros[:, 0:P], rhs=zeros[:, 0:cols], start=True, stop=True)
 
-        def beta_to_bank(b):
-            bank = psum.tile([P, BANK], F32, name="bank%d" % b)
+        def beta_to_bank():
+            nc.scalar.copy(out=beta32[:], in_=beta_bf[:])
+            bank = new_bank("betabank", BETA_BANK)
             nc.tensor.matmul(out=bank[:, 0 : NH * T], lhsT=ident[:], rhs=beta32[:].rearrange("p g t -> p (g t)"), start=True, stop=True)
             live["beta"] = bank[:, 0 : NH * T].rearrange("p (g t) -> p g t", t=T)
 
         def up(n, g, t, b):
-            bank = psum.tile([P, BANK], F32, name="bank%d" % b)
-            live["mb", n, g, t] = bank
+            bank = new_bank(("mb", n, g, t), b)
             for c in range(NV):
                 first = (t // 2) * KP + c * 2 * P + (t % 2) * P
                 m = slice(first, first + P)
-                nc.tensor.matmul_mx(out=bank[:, 0 : CHUNKS[n][1]], lhsT=wt_codes[:, g, m].bitcast(FP8X4), lhsT_scale=wt_sc[:, g, m],
+                nc.tensor.matmul_mx(out=bank[:], lhsT=wt_codes[:, g, m].bitcast(FP8X4), lhsT_scale=wt_sc[:, g, m],
                                     rhs=v_codes[:, c, samples(n)].bitcast(FP8X4), rhs_scale=v_sc[:, c, samples(n)],
                                     start=(c == 0), stop=(c == NV - 1))
 
         def sigmoid(n, g, t):
-            sig = staged("sig", (n, g), [P, T, CHUNKS[n][1]], F32)
-            nc.scalar.activation(out=sig[:, t, :], in_=live["mb", n, g, t][:, 0 : CHUNKS[n][1]], func=ACT.Sigmoid, scale=beta32[:, g, t : t + 1])
+            sig = staged("sig", ("sig", n, g), [P, T, BANK], F32)
+            nc.scalar.activation(out=sig[:, t, :], in_=live["mb", n, g, t][:], func=ACT.Sigmoid, scale=beta32[:, g, t : t + 1])
 
-        def part_samples(d):
-            return slice(PARTS[d][0], PARTS[d][0] + PARTS[d][1])
-
-        def scale_weave(d, g, from_bank, tag="hgrp"):
-            first, width = PARTS[d]
-            n = first // BANK
+        def scale_weave(n, g, from_bank=True, tag="hgrp", first=0, last=BANK):
             factors = live["beta"] if from_bank else beta32[:]
-            live["h", d, g] = staged(tag, ("h", d, g), [P, width, T], BF16)
+            grp = staged(tag, ("h", n, g), [P, BANK, T], BF16)
             nc.vector.tensor_tensor(
-                out=live["h", d, g][:].rearrange("p (c i) t -> p c t i", i=XRUN),
-                in0=live["sig", (n, g)][:, :, first - n * BANK : first - n * BANK + width].rearrange("p t (c i) -> p c t i", i=XRUN),
-                in1=factors[:, g, :].unsqueeze(1).unsqueeze(3).to_broadcast([P, width // XRUN, T, XRUN]),
+                out=grp[:, first:last, :].rearrange("p (c i) t -> p c t i", i=RUN),
+                in0=live["sig", n, g][:, :, first:last].rearrange("p t (c i) -> p c t i", i=RUN),
+                in1=factors[:, g, :].unsqueeze(1).unsqueeze(3).to_broadcast([P, (last - first) // RUN, T, RUN]),
                 op=ALU.mult)
 
-        def scale_rows(d, g):
-            first, width = PARTS[d]
-            n = first // BANK
-            flat = staged("hflat", (d, g), [P, T, width], BF16)
+        def scale_rows(n, g, first=0, last=BANK):
+            flat = staged("vflat", ("hflat", n, g), [P, T, BANK], BF16)
             for t in range(T):
-                nc.scalar.activation(out=flat[:, t, :], in_=live["sig", (n, g)][:, t, first - n * BANK : first - n * BANK + width],
+                nc.scalar.activation(out=flat[:, t, first:last], in_=live["sig", n, g][:, t, first:last],
                                      func=ACT.Copy, scale=beta32[:, g, t : t + 1])
 
-        def weave_h(d, g):
-            live["h", d, g] = staged("hgrp", ("h", d, g), [P, PARTS[d][1], T], BF16)
-            weave("V", live["h", d, g][:], live["hflat", (d, g)][:])
+        def weave_h(n, g, first=0, last=BANK, tag="hgrp"):
+            grp = staged(tag, ("h", n, g), [P, BANK, T], BF16)
+            weave("V", grp[:, first:last, :], live["hflat", n, g][:, :, first:last])
 
-        def quant_h(d, g):
-            quantise(h_codes[:, g, part_samples(d)], h_sc[:, g, part_samples(d)], live["h", d, g][:])
+        def quant_h(n, g, first=0, last=BANK):
+            cols = slice(n * BANK + first, n * BANK + last)
+            quantise(h_codes[:, g, cols], h_sc[:, g, cols], live["h", n, g][:, first:last, :])
 
-        def down(d, j, g, b, first, last):
-            width = PARTS[d][1]
-            m0, count = TILES[d][j]
-            if first:
-                live["nb", d, j] = psum.tile([P, BANK], F32, name="bank%d" % b)
-            for i in range(count):
-                mc = slice((m0 + i) * P, (m0 + i + 1) * P)
-                nc.tensor.matmul_mx(out=live["nb", d, j][:, i * width : (i + 1) * width],
-                                    lhsT=w2_codes[:, g, mc].bitcast(FP8X4), lhsT_scale=w2_sc[:, g, mc],
-                                    rhs=h_codes[:, g, part_samples(d)].bitcast(FP8X4), rhs_scale=h_sc[:, g, part_samples(d)],
-                                    start=(first and i == 0), stop=(last and i == count - 1))
+        def open_tile(n, m, b, first=0, last=BANK):
+            new_bank(("nb", n, m, first), b)
+            live["todo", n, m, first] = NH
+            live["width", n, m, first] = last - first
 
-        def finish(d, j, e):
-            width = PARTS[d][1]
-            m0, count = TILES[d][j]
-            res = staged("res", (d, j), [P, count * width], F32)
-            copy_on[e](out=res[:], in_=live["nb", d, j][:, 0 : count * width])
-            rows = out[m0 * P : (m0 + count) * P, part_samples(d)].rearrange("(i p) n -> p i n", p=P)
-            nc.sync.dma_start(out=rows, in_=res[:].rearrange("p (i n) -> p i n", i=count))
+        def down(n, ms, gs, first=0):
+            for m in ms:
+                width = live["width", n, m, first]
+                cols = slice(n * BANK + first, n * BANK + first + width)
+                for g in gs:
+                    k, j = (g, m) if m < NH else (m, g)
+                    mc = slice(j * P, (j + 1) * P)
+                    left = live["todo", n, m, first]
+                    nc.tensor.matmul_mx(out=live["nb", n, m, first][:, 0:width], lhsT=w2_codes[:, k, mc].bitcast(FP8X4), lhsT_scale=w2_sc[:, k, mc],
+                                        rhs=h_codes[:, g, cols].bitcast(FP8X4), rhs_scale=h_sc[:, g, cols],
+                                        start=(left == NH), stop=(left == 1))
+                    live["todo", n, m, first] = left - 1
+
+        def finish(e, n, m, first=0):
+            width = live["width", n, m, first]
+            res = staged("res", ("res", n, m, first), [P, BANK], F32)
+            copy_on[e](out=res[:, 0:width], in_=live["nb", n, m, first][:, 0:width])
+            nc.sync.dma_start(out=out[m * P : (m + 1) * P, n * BANK + first : n * BANK + first + width], in_=res[:, 0:width])
+
+        turns = [0]
+
+        def next_bank():
+            turns.append(turns[-1] + 1)
+            return turns[-2] % BETA_BANK
+
+        def turn_pair(g, a, tag="wtgrp"):
+            turn(g, a, [next_bank(), next_bank()], tag)
+
+        def up_group(n, g, ts=range(T), banks=None):
+            for t in ts:
+                up(n, g, t, banks[t] if banks else next_bank())
+                sigmoid(n, g, t)
 
         with tc.manual_schedule():
             small_loads()
-            load_v(0, 0, 1, 2)
-            load_v(1, 0, 1)
+            for c in range(NV):
+                load_v(c, 0, 0, 2)
+                load_v(c, 1, 0, 2)
             for g in range(NH):
                 load_w(g, 0)
                 load_w(g, 1)
-                if g == 1:
-                    load_v(0, 1, 2)
-                    load_v(1, 1, 2)
-            nb = [0]
-
-            def bank():
-                nb.append(nb[-1] + 1)
-                return nb[-2] % (NBANKS - 1)
-
-            def turn_unit(g, a, tag="wtgrp", last="S"):
-                for c in range(NV):
-                    turn(g, a, c, bank())
-                    if c == 0 or last == "S":
-                        empty_turn(g, a, c, "S", tag)
-
-            def up_group(n, g):
-                for t in range(T):
-                    up(n, g, t, bank())
-                    sigmoid(n, g, t)
-
-            def down_pass(n, js, g, banks=None):
-                for j in js:
-                    down(n, j, g, (banks[j % len(banks)] if banks else bank()) if g == 0 else 0, g == 0, g == NH - 1)
-
-            warm_up(BANK)
-            warm_up(BANK)
-            beta_to_bank(7)
-            for t in range(T):
-                widen(0, 0, t, "V")
-            for t in range(T):
-                widen(1, 0, t, "S" if t < 3 else "V")
-            turn_unit(0, 0)
-            turn_unit(0, 1)
-            warm_up(BANK // 2)
-            weave_v(0, 0, "V")
-            weave_v(1, 0, "V")
+            warm_up(BANK, 6)
+            warm_up(BANK, 6)
+            warm_up(BANK // 2, 6)
+            widen("V", 0, 0, range(T))
+            widen("S", 0, 1, range(T))
+            beta_to_bank()
+            widen("V", 1, 0, range(T))
+            widen("S", 1, 1, [0, 1, 2])
+            turn_pair(0, 0)
+            turn_pair(0, 1)
+            warm_up(BANK // 2, 6)
+            weave_v(0, 0)
+            widen("V", 1, 1, [3])
             quant_v(0, 0)
+            weave_v(1, 0)
             quant_up(0, 0)
             quant_v(1, 0)
             quant_up(0, 1)
-            turn_unit(1, 0)
-            turn_unit(1, 1, "gate")
+            turn_pair(1, 0)
+            turn_pair(1, 1)
             up_group(0, 0)
-            for t in range(T):
-                widen(0, 1, t, "V")
+            weave_v(0, 1)
             quant_up(1, 0)
-            for t in range(T):
-                widen(1, 1, t, "V")
-            weave_v(0, 1, "V")
+            weave_v(1, 1)
             quant_up(1, 1)
-            turn_unit(2, 0)
-            turn_unit(2, 1)
-            weave_w_beside(0, 1, 0, last=3 * KP // 4)
-            scale_weave(0, 0, True)
+            quant_v(0, 1)
+            quant_v(1, 1)
+            left_tile(1, 2, "w2grp")
+            weave_left("V", 1, first=SHARE_A)
+            turn_pair(2, 0)
+            turn_pair(2, 1, "gate_a")
             up_group(0, 1)
             quant_up(2, 0)
             quant_up(2, 1)
-            turn_unit(3, 0)
-            turn_unit(3, 1)
+            left_tile(0, 1, "gate_a")
+            weave_left_beside(0, 1, 0)
+            weave_left_beside(1, 2, 1, last=SHARE_A)
+            scale_weave(0, 0)
+            scale_weave(0, 1, tag="gate_b")
+            turn_pair(3, 0)
+            turn_pair(3, 1)
             up_group(0, 2)
-            weave_v(1, 1, "V")
+            up_group(1, 0)
             quant_up(3, 0)
-            quant_v(0, 1)
             quant_up(3, 1)
-            quant_v(1, 1)
-            weave_w_rest(0, 0, 3 * KP // 4)
-            quant_h(0, 0)
             up_group(0, 3)
-            quant_down(0, 0)
-            weave_w_beside(1, NH, 0, last=LONG)
-            for g in range(1, NH):
-                scale_weave(0, g, True)
-            for g in range(NH):
-                up_group(1, g)
-            scale_weave(1, 0, True)
-
-            weave_w(0, 1, "S", "late")
-            lo, hi = [0, 1, 2, 3], [4, 5, 6, 7]
-            for g in range(NH):
-                if g == 1:
-                    weave_w_left(1, NH, 0, LONG)
-                if g > 0:
-                    quant_h(0, g)
-                    quant_down(g, 0)
-                down_pass(0, range(4), g, lo)
+            quant_h(0, 0)
+            quant_left(0)
+            quant_h(0, 1)
+            left_tile(2, 4, "gate_b")
+            weave_left_beside(2, 4, 2)
+            scale_weave(0, 2)
+            scale_weave(1, 0, tag="gate_a")
+            scale_weave(0, 3)
+            up_group(1, 1)
+            up_group(1, 2)
+            up_group(1, 3, banks=[3, 4, 5, 6])
+            quant_left(1)
+            quant_h(0, 2)
+            quant_left(2)
+            quant_h(0, 3)
+            quant_left(3)
             quant_h(1, 0)
-            quant_down(0, 1)
-            for j in range(4):
-                finish(0, j, "S")
-            weave_w_beside(1, 2, 1, "late", SHARE)
-            weave_w(2, 1, "S", "gate")
-            weave_w(3, 1, "S")
-            scale_rows(2, 3)
-            scale_weave(1, 1, True)
-            scale_weave(1, 2, True)
-            down_pass(1, range(3), 0, hi)
-            down_pass(0, range(4, 8), 0, lo)
+            right_tile(5, "gate_a", 0, 2)
+            weave_right_beside(5, 0, 2)
+            scale_weave(1, 1)
+            for m in range(4):
+                open_tile(0, m, m)
+            for g in range(NH - 1):
+                down(0, range(4), [g])
+            right_tile(4, "gate_c")
+            weave_right("S", 4)
+            for m in range(4):
+                down(0, [m], [3])
+                if m == 3:
+                    scale_rows(1, 3)
+                finish("S", 0, m)
+            quant_right(5, 0, 2)
             quant_h(1, 1)
-            weave_w_rest(1, 1, SHARE)
+            quant_right(4)
+            right_tile(5, "gate_c", 2, 4)
+            weave_right_beside(5, 2, 4)
+            scale_weave(1, 2)
+            quant_right(5, 2, 4)
+            for m, b in zip(range(4), [4, 5, 6, 0]):
+                open_tile(1, m, b)
+            down(1, range(4), [0])
+            down(1, range(4), [1])
+            for m, b in [(4, 1), (5, 2)]:
+                open_tile(0, m, b)
+                down(0, [m], range(NH))
+                finish("S", 0, m)
             quant_h(1, 2)
-            for g in range(1, 3):
-                down_pass(1, range(2), g)
-            down_pass(1, [3], 0, hi)
-            quant_down(1, 1)
-            down_pass(0, range(4, 8), 1)
-            down_pass(1, range(2, 4), 1)
-            scale_weave(1, 3, False)
-            quant_down(2, 1)
+            weave_h(1, 3)
             quant_h(1, 3)
-            for j in range(2):
-                down_pass(1, [j], 3)
-                finish(1, j, "S")
-            scale_weave(2, 0, False)
-            quant_down(3, 1)
-            down_pass(0, range(4, 8), 2)
-            for j in range(4, 8):
-                down_pass(0, [j], 3)
-                finish(0, j, "S")
-            for j in range(2, 4):
-                down_pass(1, [j], 2)
-                down_pass(1, [j], 3)
-                finish(1, j, "S")
-            for g in range(NH):
-                if g + 2 < NH:
-                    scale_weave(2, g + 1, False)
-                elif g + 1 < NH:
-                    weave_h(2, g + 1)
-                quant_h(2, g)
-                if g == 0:
-                    down_pass(2, range(5), g, [4, 5, 0, 1, 2])
-                elif g < NH - 1:
-                    down_pass(2, range(2), g)
-            for j in range(5):
-                for g in range(NH - 1 if j < 2 else 1, NH):
-                    down_pass(2, [j], g)
-                finish(2, j, "VS"[j % 2])
+            right_tile(6, "gate_a")
+            weave_right("V", 6)
+            quant_right(6)
+            right_tile(7, "gate_b")
+            weave_right("V", 7)
+            down(1, range(4), [2])
+            open_tile(1, 4, 3)
+            down(1, [4], [0, 1, 2])
+            for m in range(5):
+                down(1, [m], [3])
+                finish("S", 1, m)
+            quant_right(7)
+            open_tile(1, 5, 7)
+            down(1, [5], range(NH))
+            finish("V", 1, 5)
+            for n, m, b in [(0, 6, 1), (1, 6, 2), (0, 7, 4)]:
+                open_tile(n, m, b)
+                down(n, [m], range(NH))
+                finish("VS"[n], n, m)
+            for e, first, last, b in [("S", 0, 256, 5), ("V", 256, 512, 6)]:
+                open_tile(1, 7, b, first, last)
+                down(1, [7], range(NH), first)
+                finish(e, 1, 7, first)

@@ -23,8 +23,12 @@ NH = H // KP
 BANK = 512
 BETA_BANK = 7
 RUN = 4
-BUFS = {"vflat": 4, "vgrp": 2, "wtgrp": 3, "w2grp": 1, "gate_a": 1, "gate_b": 1, "gate_c": 1, "hgrp": 3, "sig": 4, "res": 8}
-SHARE_A = 128
+BUFS = {"flat": 4, "one": 6, "two": 1, "last": 1, "gate_c": 1, "gate_a": 1, "gate_b": 1, "sig": 4, "res": 8}
+FLAT = [T, BANK]
+WOVEN = [BANK, T]
+SHARE_A = 160
+SHARE_A2 = 256
+SPLIT_H = 256
 
 
 def tile_rbm_mean_field_reconstruction_s7_kernel(tc, v_bytes, v_scale, w, beta, out):
@@ -40,14 +44,14 @@ def tile_rbm_mean_field_reconstruction_s7_kernel(tc, v_bytes, v_scale, w, beta, 
         beta_bf = keep.tile([P, NH, T], BF16, name="beta_bf")
         beta32 = keep.tile([P, NH, T], F32, name="beta32")
         ident = keep.tile([P, P], F32, name="ident")
-        v_codes = keep.tile([P, NV, B], U32, name="v_codes", align_bytes=64)
-        v_sc = keep.tile([P, NV, B], U8, name="v_sc", align_bytes=64)
+        v_codes = keep.tile([P, 2, NV * BANK], U32, name="v_codes", align_bytes=64)
+        v_sc = keep.tile([P, 2, NV * BANK], U8, name="v_sc", align_bytes=64)
         wt_codes = keep.tile([P, NH, 2 * KP], U32, name="wt_codes", align_bytes=64)
         wt_sc = keep.tile([P, NH, 2 * KP], U8, name="wt_sc", align_bytes=64)
         w2_codes = keep.tile([P, 2 * NH, KP], U32, name="w2_codes", align_bytes=64)
         w2_sc = keep.tile([P, 2 * NH, KP], U8, name="w2_sc", align_bytes=64)
-        h_codes = keep.tile([P, NH, B], U32, name="h_codes", align_bytes=64)
-        h_sc = keep.tile([P, NH, B], U8, name="h_sc", align_bytes=64)
+        h_codes = keep.tile([P, 2, NH * BANK], U32, name="h_codes", align_bytes=64)
+        h_sc = keep.tile([P, 2, NH * BANK], U8, name="h_sc", align_bytes=64)
         w_rows = keep.tile([P, NH * T * V], BF16, name="w_rows", align_bytes=64)
         zeros = keep.tile([P, BANK], F32, name="zeros")
         live = {}
@@ -94,8 +98,13 @@ def tile_rbm_mean_field_reconstruction_s7_kernel(tc, v_bytes, v_scale, w, beta, 
             first = (g * T + 2 * a) * V
             nc.sync.dma_start(out=w_rows[:, first : first + 2 * V], in_=w_view[g][:, 2 * a * V : 2 * (a + 1) * V])
 
+        def group(kind, keys, shape, dtype, tag):
+            tile = staged(tag, (kind, keys[0], "tile"), [P, len(keys)] + shape, dtype)
+            for i, key in enumerate(keys):
+                live[(kind,) + key] = tile[:, i]
+
         def widen(e, c, n, ts):
-            flat = staged("vflat", ("vflat", c, n), [P, T, BANK], BF16)
+            flat = live["vflat", c, n]
             for t in ts:
                 src = live["vraw", c, n, t].bitcast(FP8)
                 if e == "V":
@@ -103,16 +112,19 @@ def tile_rbm_mean_field_reconstruction_s7_kernel(tc, v_bytes, v_scale, w, beta, 
                 else:
                     nc.scalar.activation(out=flat[:, t, :], in_=src, func=ACT.Copy, scale=vs[:, c, t : t + 1])
 
-        def weave_v(c, n, tag="vgrp"):
-            weave("V", staged(tag, ("vgrp", c, n), [P, BANK, T], BF16)[:], live["vflat", c, n][:])
+        def weave_v(c, n):
+            weave("V", live["vgrp", c, n], live["vflat", c, n])
 
-        def quant_v(c, n):
-            quantise(v_codes[:, c, samples(n)], v_sc[:, c, samples(n)], live["vgrp", c, n][:])
+        def whole(kind, key):
+            return live[kind, key, "tile"][:].rearrange("p a n t -> p (a n) t")
 
-        def turn(g, a, banks, tag="wtgrp"):
+        def quant_v(n, lo, hi):
+            cols = slice(lo * BANK, hi * BANK)
+            quantise(v_codes[:, n, cols], v_sc[:, n, cols], whole("vgrp", (lo, n)))
+
+        def turn(g, a, banks):
             words = w_rows[:].bitcast(F32)
-            grp = staged(tag, ("wt", g, a), [P, KP, T], BF16)
-            dst = grp[:].rearrange("p m t -> p (m t)").bitcast(F32).rearrange("p (c i m u) -> p c i m u", c=NV, i=2, u=2)
+            dst = live["wt", g, a].rearrange("p m t -> p (m t)").bitcast(F32).rearrange("p (c i m u) -> p c i m u", c=NV, i=2, u=2)
             for c in range(NV):
                 bank = new_bank(("tb", g, a, c), banks[c])
                 for i in range(2):
@@ -122,9 +134,9 @@ def tile_rbm_mean_field_reconstruction_s7_kernel(tc, v_bytes, v_scale, w, beta, 
                         nc.tensor.transpose(bank[:, j : j + P], words[:, first + u : first + 2 * P : 2], ident[:])
                 nc.scalar.copy(out=dst[:, c], in_=bank[:].rearrange("p (i u m) -> p i m u", i=2, u=2))
 
-        def quant_up(g, a):
-            cols = slice(a * KP, (a + 1) * KP)
-            quantise(wt_codes[:, g, cols], wt_sc[:, g, cols], live["wt", g, a][:])
+        def quant_up(g, lo, hi):
+            cols = slice(lo * KP, hi * KP)
+            quantise(wt_codes[:, g, cols], wt_sc[:, g, cols], whole("wt", (g, lo)))
 
         def left_tile(lo, hi, tag):
             grouped = staged(tag, ("left", lo), [P, hi - lo, KP, T], BF16)
@@ -141,15 +153,19 @@ def tile_rbm_mean_field_reconstruction_s7_kernel(tc, v_bytes, v_scale, w, beta, 
         def right_tile(m, tag, lo=0, hi=NH):
             staged(tag, ("right", m, lo), [P, hi - lo, P, T], BF16)
 
-        def weave_right_beside(m, lo, hi):
-            nc.gpsimd.tensor_scalar(out=live["right", m, lo][:], in0=w_gvt[:, lo:hi, m * P : (m + 1) * P, :],
+        def weave_right_beside(m, lo, hi, first=0, last=P):
+            nc.gpsimd.tensor_scalar(out=live["right", m, lo][:, :, first:last, :], in0=w_gvt[:, lo:hi, m * P + first : m * P + last, :],
                                     scalar1=1.0, scalar2=0.0, op0=ALU.mult, op1=ALU.add)
 
-        def weave_right(e, m):
-            copy_on[e](out=live["right", m, 0][:].rearrange("p g (c i) t -> p g c t i", i=RUN),
-                       in_=w_gtv[:, :, :, m * P : (m + 1) * P].rearrange("p g t (c i) -> p g c t i", i=RUN))
+        def weave_right(e, m, first=0, last=P):
+            copy_on[e](out=live["right", m, 0][:, :, first:last, :].rearrange("p g (c i) t -> p g c t i", i=RUN),
+                       in_=w_gtv[:, :, :, m * P + first : m * P + last].rearrange("p g t (c i) -> p g c t i", i=RUN))
 
-        def quant_left(g):
+        def quant_left(lo, hi):
+            quantise(w2_codes[:, lo:hi, :].rearrange("p k v -> p (k v)"), w2_sc[:, lo:hi, :].rearrange("p k v -> p (k v)"),
+                     live["left", lo][:].rearrange("p g v t -> p (g v) t"))
+
+        def quant_left_one(g):
             quantise(w2_codes[:, g, :], w2_sc[:, g, :], live["w2", g])
 
         def quant_right(m, lo=0, hi=NH):
@@ -172,35 +188,31 @@ def tile_rbm_mean_field_reconstruction_s7_kernel(tc, v_bytes, v_scale, w, beta, 
                 first = (t // 2) * KP + c * 2 * P + (t % 2) * P
                 m = slice(first, first + P)
                 nc.tensor.matmul_mx(out=bank[:], lhsT=wt_codes[:, g, m].bitcast(FP8X4), lhsT_scale=wt_sc[:, g, m],
-                                    rhs=v_codes[:, c, samples(n)].bitcast(FP8X4), rhs_scale=v_sc[:, c, samples(n)],
+                                    rhs=v_codes[:, n, samples(c)].bitcast(FP8X4), rhs_scale=v_sc[:, n, samples(c)],
                                     start=(c == 0), stop=(c == NV - 1))
 
         def sigmoid(n, g, t):
             sig = staged("sig", ("sig", n, g), [P, T, BANK], F32)
             nc.scalar.activation(out=sig[:, t, :], in_=live["mb", n, g, t][:], func=ACT.Sigmoid, scale=beta32[:, g, t : t + 1])
 
-        def scale_weave(n, g, from_bank=True, tag="hgrp", first=0, last=BANK):
-            factors = live["beta"] if from_bank else beta32[:]
-            grp = staged(tag, ("h", n, g), [P, BANK, T], BF16)
+        def scale_weave(n, g):
             nc.vector.tensor_tensor(
-                out=grp[:, first:last, :].rearrange("p (c i) t -> p c t i", i=RUN),
-                in0=live["sig", n, g][:, :, first:last].rearrange("p t (c i) -> p c t i", i=RUN),
-                in1=factors[:, g, :].unsqueeze(1).unsqueeze(3).to_broadcast([P, (last - first) // RUN, T, RUN]),
+                out=live["h", n, g].rearrange("p (c i) t -> p c t i", i=RUN),
+                in0=live["sig", n, g][:].rearrange("p t (c i) -> p c t i", i=RUN),
+                in1=live["beta"][:, g, :].unsqueeze(1).unsqueeze(3).to_broadcast([P, BANK // RUN, T, RUN]),
                 op=ALU.mult)
 
-        def scale_rows(n, g, first=0, last=BANK):
-            flat = staged("vflat", ("hflat", n, g), [P, T, BANK], BF16)
-            for t in range(T):
-                nc.scalar.activation(out=flat[:, t, first:last], in_=live["sig", n, g][:, t, first:last],
+        def scale_rows(n, g, ts=range(T)):
+            for t in ts:
+                nc.scalar.activation(out=live["hflat", n, g][:, t, :], in_=live["sig", n, g][:, t, :],
                                      func=ACT.Copy, scale=beta32[:, g, t : t + 1])
 
-        def weave_h(n, g, first=0, last=BANK, tag="hgrp"):
-            grp = staged(tag, ("h", n, g), [P, BANK, T], BF16)
-            weave("V", grp[:, first:last, :], live["hflat", n, g][:, :, first:last])
+        def weave_h(e, n, g, first=0, last=BANK):
+            weave(e, live["h", n, g][:, first:last, :], live["hflat", n, g][:, :, first:last])
 
-        def quant_h(n, g, first=0, last=BANK):
-            cols = slice(n * BANK + first, n * BANK + last)
-            quantise(h_codes[:, g, cols], h_sc[:, g, cols], live["h", n, g][:, first:last, :])
+        def quant_h(n, lo, hi):
+            cols = slice(lo * BANK, hi * BANK)
+            quantise(h_codes[:, n, cols], h_sc[:, n, cols], whole("h", (n, lo)))
 
         def open_tile(n, m, b, first=0, last=BANK):
             new_bank(("nb", n, m, first), b)
@@ -210,13 +222,13 @@ def tile_rbm_mean_field_reconstruction_s7_kernel(tc, v_bytes, v_scale, w, beta, 
         def down(n, ms, gs, first=0):
             for m in ms:
                 width = live["width", n, m, first]
-                cols = slice(n * BANK + first, n * BANK + first + width)
                 for g in gs:
+                    cols = slice(g * BANK + first, g * BANK + first + width)
                     k, j = (g, m) if m < NH else (m, g)
                     mc = slice(j * P, (j + 1) * P)
                     left = live["todo", n, m, first]
                     nc.tensor.matmul_mx(out=live["nb", n, m, first][:, 0:width], lhsT=w2_codes[:, k, mc].bitcast(FP8X4), lhsT_scale=w2_sc[:, k, mc],
-                                        rhs=h_codes[:, g, cols].bitcast(FP8X4), rhs_scale=h_sc[:, g, cols],
+                                        rhs=h_codes[:, n, cols].bitcast(FP8X4), rhs_scale=h_sc[:, n, cols],
                                         start=(left == NH), stop=(left == 1))
                     live["todo", n, m, first] = left - 1
 
@@ -232,8 +244,8 @@ def tile_rbm_mean_field_reconstruction_s7_kernel(tc, v_bytes, v_scale, w, beta, 
             turns.append(turns[-1] + 1)
             return turns[-2] % BETA_BANK
 
-        def turn_pair(g, a, tag="wtgrp"):
-            turn(g, a, [next_bank(), next_bank()], tag)
+        def turn_pair(g, a):
+            turn(g, a, [next_bank(), next_bank()])
 
         def up_group(n, g, ts=range(T), banks=None):
             for t in ts:
@@ -251,118 +263,142 @@ def tile_rbm_mean_field_reconstruction_s7_kernel(tc, v_bytes, v_scale, w, beta, 
             warm_up(BANK, 6)
             warm_up(BANK, 6)
             warm_up(BANK // 2, 6)
+            for n in range(2):
+                for c in range(NV):
+                    group("vflat", [(c, n)], FLAT, BF16, "flat")
             widen("V", 0, 0, range(T))
             widen("S", 0, 1, range(T))
             beta_to_bank()
             widen("V", 1, 0, range(T))
             widen("S", 1, 1, [0, 1, 2])
-            turn_pair(0, 0)
-            turn_pair(0, 1)
-            warm_up(BANK // 2, 6)
+            for a in range(2):
+                group("wt", [(0, a)], WOVEN, BF16, "one")
+                turn_pair(0, a)
+            warm_up(BANK // 4, 6)
+
+            for c in range(NV):
+                group("vgrp", [(c, 0)], WOVEN, BF16, "one")
             weave_v(0, 0)
             widen("V", 1, 1, [3])
-            quant_v(0, 0)
+            quant_v(0, 0, 1)
             weave_v(1, 0)
-            quant_up(0, 0)
-            quant_v(1, 0)
-            quant_up(0, 1)
-            turn_pair(1, 0)
-            turn_pair(1, 1)
+            quant_up(0, 0, 1)
+            quant_v(0, 1, 2)
+            quant_up(0, 1, 2)
+            for a in range(2):
+                group("wt", [(1, a)], WOVEN, BF16, "one")
+                turn_pair(1, a)
             up_group(0, 0)
+            group("vgrp", [(0, 1), (1, 1)], WOVEN, BF16, "two")
             weave_v(0, 1)
-            quant_up(1, 0)
             weave_v(1, 1)
-            quant_up(1, 1)
-            quant_v(0, 1)
-            quant_v(1, 1)
-            left_tile(1, 2, "w2grp")
-            weave_left("V", 1, first=SHARE_A)
+            quant_up(1, 0, 1)
+            quant_up(1, 1, 2)
+            left_tile(1, 2, "one")
+            weave_left("V", 1, first=SHARE_A2)
+            quant_v(1, 0, 2)
+            group("wt", [(2, 0)], WOVEN, BF16, "one")
             turn_pair(2, 0)
-            turn_pair(2, 1, "gate_a")
+            group("wt", [(2, 1)], WOVEN, BF16, "gate_a")
+            turn_pair(2, 1)
             up_group(0, 1)
-            quant_up(2, 0)
-            quant_up(2, 1)
+            quant_up(2, 0, 1)
+            quant_up(2, 1, 2)
             left_tile(0, 1, "gate_a")
             weave_left_beside(0, 1, 0)
             weave_left_beside(1, 2, 1, last=SHARE_A)
+            group("h", [(0, 0), (0, 1)], WOVEN, BF16, "gate_b")
             scale_weave(0, 0)
-            scale_weave(0, 1, tag="gate_b")
-            turn_pair(3, 0)
-            turn_pair(3, 1)
+            scale_weave(0, 1)
+            for a in range(2):
+                group("wt", [(3, a)], WOVEN, BF16, "one")
+                turn_pair(3, a)
             up_group(0, 2)
             up_group(1, 0)
-            quant_up(3, 0)
-            quant_up(3, 1)
+            quant_up(3, 0, 1)
+            quant_up(3, 1, 2)
             up_group(0, 3)
-            quant_h(0, 0)
-            quant_left(0)
-            quant_h(0, 1)
+            quant_h(0, 0, 2)
+            quant_left(0, 1)
             left_tile(2, 4, "gate_b")
             weave_left_beside(2, 4, 2)
+            weave_left_beside(1, 2, 1, first=SHARE_A, last=SHARE_A2)
+            group("h", [(0, 2)], WOVEN, BF16, "one")
+            group("h", [(0, 3)], WOVEN, BF16, "two")
+            group("h", [(1, 0)], WOVEN, BF16, "one")
             scale_weave(0, 2)
-            scale_weave(1, 0, tag="gate_a")
+            scale_weave(1, 0)
             scale_weave(0, 3)
             up_group(1, 1)
             up_group(1, 2)
             up_group(1, 3, banks=[3, 4, 5, 6])
-            quant_left(1)
-            quant_h(0, 2)
-            quant_left(2)
-            quant_h(0, 3)
-            quant_left(3)
-            quant_h(1, 0)
-            right_tile(5, "gate_a", 0, 2)
+            quant_left(1, 2)
+            quant_h(0, 2, 3)
+            quant_left_one(2)
+            quant_h(0, 3, 4)
+            quant_left_one(3)
+            quant_h(1, 0, 1)
+            right_tile(5, "gate_b", 0, 2)
             weave_right_beside(5, 0, 2)
+            group("h", [(1, 1)], WOVEN, BF16, "gate_c")
             scale_weave(1, 1)
             for m in range(4):
                 open_tile(0, m, m)
             for g in range(NH - 1):
                 down(0, range(4), [g])
-            right_tile(4, "gate_c")
+            right_tile(4, "gate_a")
             weave_right("S", 4)
+            group("hflat", [(1, 3)], FLAT, BF16, "flat")
+            group("h", [(1, 3)], WOVEN, BF16, "last")
             for m in range(4):
                 down(0, [m], [3])
-                if m == 3:
-                    scale_rows(1, 3)
                 finish("S", 0, m)
-            quant_right(5, 0, 2)
-            quant_h(1, 1)
+            scale_rows(1, 3)
+            weave_h("S", 1, 3, first=SPLIT_H)
             quant_right(4)
+            quant_h(1, 1, 2)
+            quant_right(5, 0, 2)
             right_tile(5, "gate_c", 2, 4)
             weave_right_beside(5, 2, 4)
+            group("h", [(1, 2)], WOVEN, BF16, "one")
             scale_weave(1, 2)
-            quant_right(5, 2, 4)
             for m, b in zip(range(4), [4, 5, 6, 0]):
                 open_tile(1, m, b)
             down(1, range(4), [0])
+            open_tile(0, 4, 1)
+            down(0, [4], range(NH))
+            finish("S", 0, 4)
             down(1, range(4), [1])
-            for m, b in [(4, 1), (5, 2)]:
-                open_tile(0, m, b)
-                down(0, [m], range(NH))
-                finish("S", 0, m)
-            quant_h(1, 2)
-            weave_h(1, 3)
-            quant_h(1, 3)
-            right_tile(6, "gate_a")
+            quant_right(5, 2, 4)
+            for n, m, b in [(0, 5, 2), (1, 4, 3)]:
+                open_tile(n, m, b)
+                down(n, [m], [0, 1])
+            down(0, [5], [2, 3])
+            finish("S", 0, 5)
+            quant_h(1, 2, 3)
+            weave_h("V", 1, 3, last=SPLIT_H)
+            quant_h(1, 3, 4)
+            right_tile(6, "two")
             weave_right("V", 6)
             quant_right(6)
             right_tile(7, "gate_b")
             weave_right("V", 7)
-            down(1, range(4), [2])
-            open_tile(1, 4, 3)
-            down(1, [4], [0, 1, 2])
+            down(1, range(5), [2])
+            open_tile(1, 5, 7)
+            down(1, [5], [0])
             for m in range(5):
                 down(1, [m], [3])
                 finish("S", 1, m)
             quant_right(7)
-            open_tile(1, 5, 7)
-            down(1, [5], range(NH))
+            down(1, [5], [1, 2, 3])
             finish("V", 1, 5)
-            for n, m, b in [(0, 6, 1), (1, 6, 2), (0, 7, 4)]:
+            for n, m, b in [(0, 6, 1), (1, 6, 2)]:
                 open_tile(n, m, b)
                 down(n, [m], range(NH))
                 finish("VS"[n], n, m)
-            for e, first, last, b in [("S", 0, 256, 5), ("V", 256, 512, 6)]:
-                open_tile(1, 7, b, first, last)
-                down(1, [7], range(NH), first)
-                finish(e, 1, 7, first)
+            for n in range(2):
+                for half, b in enumerate([[4, 5], [6, 0]][n]):
+                    first = half * BANK // 2
+                    open_tile(n, 7, b, first, first + BANK // 2)
+                    down(n, [7], range(NH), first)
+                    finish("SV"[half], n, 7, first)

@@ -262,7 +262,6 @@ def tile_rbm_mean_field_reconstruction_s7_kernel(tc, v_bytes, v_scale, w, beta, 
                 load_w(g, 1)
             warm_up(BANK, 6)
             warm_up(BANK, 6)
-            warm_up(BANK // 2, 6)
             for n in range(2):
                 for c in range(NV):
                     group("vflat", [(c, n)], FLAT, BF16, "flat")

@@ -21,14 +21,12 @@ KP = P * T
 NV = V // KP
 NH = H // KP
 BANK = 512
-BETA_BANK = 7
+FACTOR_BANK = 7
+BETA_COLUMN = 16
 RUN = 4
-BUFS = {"flat": 4, "one": 6, "two": 1, "last": 1, "gate_c": 1, "gate_a": 1, "gate_b": 1, "sig": 4, "res": 8}
 FLAT = [T, BANK]
 WOVEN = [BANK, T]
-SHARE_A = 160
-SHARE_A2 = 256
-SPLIT_H = 256
+BUFS = {"flat": 4, "one": 6, "two": 1, "gate_a": 1, "gate_b": 1, "gate_c": 1, "last": 1, "sig": 4, "res": 8}
 
 
 def tile_rbm_mean_field_reconstruction_s7_kernel(tc, v_bytes, v_scale, w, beta, out):
@@ -48,13 +46,14 @@ def tile_rbm_mean_field_reconstruction_s7_kernel(tc, v_bytes, v_scale, w, beta, 
         v_sc = keep.tile([P, 2, NV * BANK], U8, name="v_sc", align_bytes=64)
         wt_codes = keep.tile([P, NH, 2 * KP], U32, name="wt_codes", align_bytes=64)
         wt_sc = keep.tile([P, NH, 2 * KP], U8, name="wt_sc", align_bytes=64)
-        w2_codes = keep.tile([P, 2 * NH, KP], U32, name="w2_codes", align_bytes=64)
-        w2_sc = keep.tile([P, 2 * NH, KP], U8, name="w2_sc", align_bytes=64)
+        w2_codes = keep.tile([P, NH * V], U32, name="w2_codes", align_bytes=64)
+        w2_sc = keep.tile([P, NH * V], U8, name="w2_sc", align_bytes=64)
         h_codes = keep.tile([P, 2, NH * BANK], U32, name="h_codes", align_bytes=64)
         h_sc = keep.tile([P, 2, NH * BANK], U8, name="h_sc", align_bytes=64)
         w_rows = keep.tile([P, NH * T * V], BF16, name="w_rows", align_bytes=64)
         zeros = keep.tile([P, BANK], F32, name="zeros")
         live = {}
+        used = [0]
         copy_on = {"V": nc.vector.tensor_copy, "S": nc.scalar.copy}
         w_gtv = w_rows[:].rearrange("p (g t v) -> p g t v", g=NH, t=T)
         w_gvt = w_rows[:].rearrange("p (g t v) -> p g v t", g=NH, t=T)
@@ -76,6 +75,14 @@ def tile_rbm_mean_field_reconstruction_s7_kernel(tc, v_bytes, v_scale, w, beta, 
             s = src.rearrange("p t (c i) -> p c t i", i=RUN)
             copy_on[e](out=o, in_=s)
 
+        def weave_times(dst, src, factor):
+            width = src.shape[2]
+            nc.vector.tensor_tensor(
+                out=dst.rearrange("p (c i) t -> p c t i", i=RUN),
+                in0=src.rearrange("p t (c i) -> p c t i", i=RUN),
+                in1=factor.unsqueeze(1).unsqueeze(3).to_broadcast([P, width // RUN, T, RUN]),
+                op=ALU.mult)
+
         def quantise(codes, scales, grouped):
             nc.vector.quantize_mx(out=codes.bitcast(FP8X4), scales=scales, in_=grouped.rearrange("p n t -> p (n t)"))
 
@@ -87,12 +94,10 @@ def tile_rbm_mean_field_reconstruction_s7_kernel(tc, v_bytes, v_scale, w, beta, 
             nc.vector.memset(zeros[:], 0.0)
             nc.scalar.activation(out=dummy[:], in_=zeros[:, 0:1], func=ACT.Sigmoid)
 
-        def load_v(c, a, lo, hi):
-            raw = keep.tile([P, 2, (hi - lo) * BANK], U8, name="v_raw%d_%d_%d" % (c, a, lo), align_bytes=64)
-            nc.sync.dma_start(out=raw[:], in_=v_view[c][:, 2 * a : 2 * a + 2, lo * BANK : hi * BANK])
-            for n in range(lo, hi):
-                for i in range(2):
-                    live["vraw", c, n, 2 * a + i] = raw[:, i, (n - lo) * BANK : (n - lo + 1) * BANK]
+        def load_v(c, a):
+            raw = keep.tile([P, 2, B], U8, name="v_raw%d_%d" % (c, a), align_bytes=64)
+            nc.sync.dma_start(out=raw[:], in_=v_view[c][:, 2 * a : 2 * a + 2, :])
+            live["vraw", c, a] = raw
 
         def load_w(g, a):
             first = (g * T + 2 * a) * V
@@ -106,7 +111,7 @@ def tile_rbm_mean_field_reconstruction_s7_kernel(tc, v_bytes, v_scale, w, beta, 
         def widen(e, c, n, ts):
             flat = live["vflat", c, n]
             for t in ts:
-                src = live["vraw", c, n, t].bitcast(FP8)
+                src = live["vraw", c, t // 2][:, t % 2, samples(n)].bitcast(FP8)
                 if e == "V":
                     nc.vector.tensor_scalar(out=flat[:, t, :], in0=src, scalar1=vs[:, c, t : t + 1], scalar2=None, op0=ALU.mult)
                 else:
@@ -118,11 +123,10 @@ def tile_rbm_mean_field_reconstruction_s7_kernel(tc, v_bytes, v_scale, w, beta, 
         def whole(kind, key):
             return live[kind, key, "tile"][:].rearrange("p a n t -> p (a n) t")
 
-        def quant_v(n, lo, hi):
-            cols = slice(lo * BANK, hi * BANK)
-            quantise(v_codes[:, n, cols], v_sc[:, n, cols], whole("vgrp", (lo, n)))
+        def quant_v(c, n):
+            quantise(v_codes[:, n, samples(c)], v_sc[:, n, samples(c)], live["vgrp", c, n])
 
-        def turn(g, a, banks):
+        def turn(g, a, banks, engines="SS"):
             words = w_rows[:].bitcast(F32)
             dst = live["wt", g, a].rearrange("p m t -> p (m t)").bitcast(F32).rearrange("p (c i m u) -> p c i m u", c=NV, i=2, u=2)
             for c in range(NV):
@@ -132,87 +136,79 @@ def tile_rbm_mean_field_reconstruction_s7_kernel(tc, v_bytes, v_scale, w, beta, 
                     for u in range(2):
                         j = (2 * i + u) * P
                         nc.tensor.transpose(bank[:, j : j + P], words[:, first + u : first + 2 * P : 2], ident[:])
-                nc.scalar.copy(out=dst[:, c], in_=bank[:].rearrange("p (i u m) -> p i m u", i=2, u=2))
+                live["tdst", g, a, c] = dst[:, c]
+                if engines[c] != "-":
+                    empty_turned(engines[c], g, a, c)
 
-        def quant_up(g, lo, hi):
-            cols = slice(lo * KP, hi * KP)
-            quantise(wt_codes[:, g, cols], wt_sc[:, g, cols], whole("wt", (g, lo)))
+        def empty_turned(e, g, a, c):
+            copy_on[e](out=live["tdst", g, a, c], in_=live["tb", g, a, c][:].rearrange("p (i u m) -> p i m u", i=2, u=2))
 
-        def left_tile(lo, hi, tag):
-            grouped = staged(tag, ("left", lo), [P, hi - lo, KP, T], BF16)
-            for g in range(lo, hi):
-                live["w2", g] = grouped[:, g - lo]
+        def quant_up(g, a):
+            cols = slice(a * KP, (a + 1) * KP)
+            quantise(wt_codes[:, g, cols], wt_sc[:, g, cols], live["wt", g, a])
 
-        def weave_left_beside(lo, hi, base, first=0, last=KP):
-            nc.gpsimd.tensor_scalar(out=live["left", base][:, lo - base : hi - base, first:last, :], in0=w_gvt[:, lo:hi, first:last, :],
-                                    scalar1=1.0, scalar2=0.0, op0=ALU.mult, op1=ALU.add)
+        def w2_piece(name, gs, ms, tag):
+            tile = staged(tag, ("w2", name), [P, len(gs), len(ms) * P, T], BF16)
+            live["w2span", name] = (slice(gs[0], gs[-1] + 1), ms[0] * P)
+            for i, g in enumerate(gs):
+                for j, m in enumerate(ms):
+                    live["w2col", g, m] = used[-1] + (i * len(ms) + j) * P
+            live["w2base", name] = used[-1]
+            used.append(used[-1] + len(gs) * len(ms) * P)
+            return tile
 
-        def weave_left(e, g, first=0, last=KP):
-            weave(e, live["w2", g][:, first:last, :], w_gtv[:, g, :, first:last])
+        def weave_w2(e, name, first=0, last=None):
+            tile = live["w2", name]
+            gs, v0 = live["w2span", name]
+            last = tile.shape[2] if last is None else last
+            if e == "G":
+                nc.gpsimd.tensor_scalar(out=tile[:, :, first:last, :], in0=w_gvt[:, gs, v0 + first : v0 + last, :],
+                                        scalar1=1.0, scalar2=0.0, op0=ALU.mult, op1=ALU.add)
+            else:
+                copy_on[e](out=tile[:, :, first:last, :].rearrange("p g (c i) t -> p g c t i", i=RUN),
+                           in_=w_gtv[:, gs, :, v0 + first : v0 + last].rearrange("p g t (c i) -> p g c t i", i=RUN))
 
-        def right_tile(m, tag, lo=0, hi=NH):
-            staged(tag, ("right", m, lo), [P, hi - lo, P, T], BF16)
-
-        def weave_right_beside(m, lo, hi, first=0, last=P):
-            nc.gpsimd.tensor_scalar(out=live["right", m, lo][:, :, first:last, :], in0=w_gvt[:, lo:hi, m * P + first : m * P + last, :],
-                                    scalar1=1.0, scalar2=0.0, op0=ALU.mult, op1=ALU.add)
-
-        def weave_right(e, m, first=0, last=P):
-            copy_on[e](out=live["right", m, 0][:, :, first:last, :].rearrange("p g (c i) t -> p g c t i", i=RUN),
-                       in_=w_gtv[:, :, :, m * P + first : m * P + last].rearrange("p g t (c i) -> p g c t i", i=RUN))
-
-        def quant_left(lo, hi):
-            quantise(w2_codes[:, lo:hi, :].rearrange("p k v -> p (k v)"), w2_sc[:, lo:hi, :].rearrange("p k v -> p (k v)"),
-                     live["left", lo][:].rearrange("p g v t -> p (g v) t"))
-
-        def quant_left_one(g):
-            quantise(w2_codes[:, g, :], w2_sc[:, g, :], live["w2", g])
-
-        def quant_right(m, lo=0, hi=NH):
-            cols = slice(lo * P, hi * P)
-            quantise(w2_codes[:, m, cols], w2_sc[:, m, cols], live["right", m, lo][:].rearrange("p g v t -> p (g v) t"))
+        def quant_w2(name, first=0, last=None):
+            words = live["w2", name][:].rearrange("p g v t -> p (g v) t")
+            last = words.shape[1] if last is None else last
+            cols = slice(live["w2base", name] + first, live["w2base", name] + last)
+            quantise(w2_codes[:, cols], w2_sc[:, cols], words[:, first:last, :])
 
         def warm_up(cols, b):
             bank = new_bank("warm", b)
             nc.tensor.matmul(out=bank[:, 0:cols], lhsT=zeros[:, 0:P], rhs=zeros[:, 0:cols], start=True, stop=True)
 
         def beta_to_bank():
-            nc.scalar.copy(out=beta32[:], in_=beta_bf[:])
-            bank = new_bank("betabank", BETA_BANK)
-            nc.tensor.matmul(out=bank[:, 0 : NH * T], lhsT=ident[:], rhs=beta32[:].rearrange("p g t -> p (g t)"), start=True, stop=True)
-            live["beta"] = bank[:, 0 : NH * T].rearrange("p (g t) -> p g t", t=T)
+            cols = slice(BETA_COLUMN, BETA_COLUMN + NH * T)
+            nc.tensor.matmul(out=live["factors"][:, cols], lhsT=ident[:], rhs=beta32[:].rearrange("p g t -> p (g t)"), start=True, stop=True)
+            live["beta"] = live["factors"][:, cols].rearrange("p (g t) -> p g t", t=T)
 
-        def up(n, g, t, b):
-            bank = new_bank(("mb", n, g, t), b)
-            for c in range(NV):
-                first = (t // 2) * KP + c * 2 * P + (t % 2) * P
-                m = slice(first, first + P)
-                nc.tensor.matmul_mx(out=bank[:], lhsT=wt_codes[:, g, m].bitcast(FP8X4), lhsT_scale=wt_sc[:, g, m],
-                                    rhs=v_codes[:, n, samples(c)].bitcast(FP8X4), rhs_scale=v_sc[:, n, samples(c)],
-                                    start=(c == 0), stop=(c == NV - 1))
+        def up_pass(n, g, t, c, b=None):
+            if c == 0:
+                new_bank(("mb", n, g, t), b)
+            first = (t // 2) * KP + c * 2 * P + (t % 2) * P
+            m = slice(first, first + P)
+            nc.tensor.matmul_mx(out=live["mb", n, g, t][:], lhsT=wt_codes[:, g, m].bitcast(FP8X4), lhsT_scale=wt_sc[:, g, m],
+                                rhs=v_codes[:, n, samples(c)].bitcast(FP8X4), rhs_scale=v_sc[:, n, samples(c)],
+                                start=(c == 0), stop=(c == NV - 1))
 
         def sigmoid(n, g, t):
             sig = staged("sig", ("sig", n, g), [P, T, BANK], F32)
             nc.scalar.activation(out=sig[:, t, :], in_=live["mb", n, g, t][:], func=ACT.Sigmoid, scale=beta32[:, g, t : t + 1])
 
-        def scale_weave(n, g):
-            nc.vector.tensor_tensor(
-                out=live["h", n, g].rearrange("p (c i) t -> p c t i", i=RUN),
-                in0=live["sig", n, g][:].rearrange("p t (c i) -> p c t i", i=RUN),
-                in1=live["beta"][:, g, :].unsqueeze(1).unsqueeze(3).to_broadcast([P, BANK // RUN, T, RUN]),
-                op=ALU.mult)
+        def scale_h(n, g, first=0, last=BANK):
+            weave_times(live["h", n, g][:, first:last, :], live["sig", n, g][:, :, first:last], live["beta"][:, g, :])
 
-        def scale_rows(n, g, ts=range(T)):
+        def scale_h_rows(n, g, ts=range(T), first=0, last=BANK):
             for t in ts:
-                nc.scalar.activation(out=live["hflat", n, g][:, t, :], in_=live["sig", n, g][:, t, :],
+                nc.scalar.activation(out=live["hflat", n, g][:, t, first:last], in_=live["sig", n, g][:, t, first:last],
                                      func=ACT.Copy, scale=beta32[:, g, t : t + 1])
 
         def weave_h(e, n, g, first=0, last=BANK):
             weave(e, live["h", n, g][:, first:last, :], live["hflat", n, g][:, :, first:last])
 
-        def quant_h(n, lo, hi):
-            cols = slice(lo * BANK, hi * BANK)
-            quantise(h_codes[:, n, cols], h_sc[:, n, cols], whole("h", (n, lo)))
+        def quant_h(n, g):
+            quantise(h_codes[:, n, samples(g)], h_sc[:, n, samples(g)], live["h", n, g])
 
         def open_tile(n, m, b, first=0, last=BANK):
             new_bank(("nb", n, m, first), b)
@@ -224,10 +220,9 @@ def tile_rbm_mean_field_reconstruction_s7_kernel(tc, v_bytes, v_scale, w, beta, 
                 width = live["width", n, m, first]
                 for g in gs:
                     cols = slice(g * BANK + first, g * BANK + first + width)
-                    k, j = (g, m) if m < NH else (m, g)
-                    mc = slice(j * P, (j + 1) * P)
+                    mc = slice(live["w2col", g, m], live["w2col", g, m] + P)
                     left = live["todo", n, m, first]
-                    nc.tensor.matmul_mx(out=live["nb", n, m, first][:, 0:width], lhsT=w2_codes[:, k, mc].bitcast(FP8X4), lhsT_scale=w2_sc[:, k, mc],
+                    nc.tensor.matmul_mx(out=live["nb", n, m, first][:, 0:width], lhsT=w2_codes[:, mc].bitcast(FP8X4), lhsT_scale=w2_sc[:, mc],
                                         rhs=h_codes[:, n, cols].bitcast(FP8X4), rhs_scale=h_sc[:, n, cols],
                                         start=(left == NH), stop=(left == 1))
                     live["todo", n, m, first] = left - 1
@@ -238,25 +233,23 @@ def tile_rbm_mean_field_reconstruction_s7_kernel(tc, v_bytes, v_scale, w, beta, 
             copy_on[e](out=res[:, 0:width], in_=live["nb", n, m, first][:, 0:width])
             nc.sync.dma_start(out=out[m * P : (m + 1) * P, n * BANK + first : n * BANK + first + width], in_=res[:, 0:width])
 
-        turns = [0]
+        def woven(kind, key, tag):
+            group(kind, [key], WOVEN, BF16, tag)
 
-        def next_bank():
-            turns.append(turns[-1] + 1)
-            return turns[-2] % BETA_BANK
+        def flat(kind, key):
+            group(kind, [key], FLAT, BF16, "flat")
 
-        def turn_pair(g, a):
-            turn(g, a, [next_bank(), next_bank()])
-
-        def up_group(n, g, ts=range(T), banks=None):
-            for t in ts:
-                up(n, g, t, banks[t] if banks else next_bank())
+        def up_group(n, g, banks):
+            for t in range(T):
+                for c in range(NV):
+                    up_pass(n, g, t, c, banks[t])
                 sigmoid(n, g, t)
 
         with tc.manual_schedule():
             small_loads()
             for c in range(NV):
-                load_v(c, 0, 0, 2)
-                load_v(c, 1, 0, 2)
+                load_v(c, 0)
+                load_v(c, 1)
             for g in range(NH):
                 load_w(g, 0)
                 load_w(g, 1)
@@ -264,134 +257,143 @@ def tile_rbm_mean_field_reconstruction_s7_kernel(tc, v_bytes, v_scale, w, beta, 
             warm_up(BANK, 6)
             for n in range(2):
                 for c in range(NV):
-                    group("vflat", [(c, n)], FLAT, BF16, "flat")
+                    flat("vflat", (c, n))
             widen("V", 0, 0, range(T))
             widen("S", 0, 1, range(T))
+            nc.scalar.copy(out=beta32[:], in_=beta_bf[:])
+            new_bank("factors", FACTOR_BANK)
             beta_to_bank()
             widen("V", 1, 0, range(T))
             widen("S", 1, 1, [0, 1, 2])
-            for a in range(2):
-                group("wt", [(0, a)], WOVEN, BF16, "one")
-                turn_pair(0, a)
+            woven("wt", (0, 0), "one")
+            turn(0, 0, [0, 1])
+            woven("wt", (0, 1), "one")
+            turn(0, 1, [2, 3])
             warm_up(BANK // 4, 6)
-
-            for c in range(NV):
-                group("vgrp", [(c, 0)], WOVEN, BF16, "one")
+            woven("vgrp", (0, 0), "one")
+            woven("vgrp", (1, 0), "one")
             weave_v(0, 0)
             widen("V", 1, 1, [3])
-            quant_v(0, 0, 1)
+            quant_v(0, 0)
             weave_v(1, 0)
-            quant_up(0, 0, 1)
-            quant_v(0, 1, 2)
-            quant_up(0, 1, 2)
-            for a in range(2):
-                group("wt", [(1, a)], WOVEN, BF16, "one")
-                turn_pair(1, a)
-            up_group(0, 0)
-            group("vgrp", [(0, 1), (1, 1)], WOVEN, BF16, "two")
+            quant_up(0, 0)
+            quant_v(1, 0)
+            quant_up(0, 1)
+            woven("wt", (1, 0), "one")
+            turn(1, 0, [4, 5])
+            woven("wt", (1, 1), "one")
+            turn(1, 1, [6, 0])
+            up_group(0, 0, [1, 2, 3, 4])
+            woven("vgrp", (0, 1), "two")
+            woven("vgrp", (1, 1), "one")
             weave_v(0, 1)
             weave_v(1, 1)
-            quant_up(1, 0, 1)
-            quant_up(1, 1, 2)
-            left_tile(1, 2, "one")
-            weave_left("V", 1, first=SHARE_A2)
-            quant_v(1, 0, 2)
-            group("wt", [(2, 0)], WOVEN, BF16, "one")
-            turn_pair(2, 0)
-            group("wt", [(2, 1)], WOVEN, BF16, "gate_a")
-            turn_pair(2, 1)
-            up_group(0, 1)
-            quant_up(2, 0, 1)
-            quant_up(2, 1, 2)
-            left_tile(0, 1, "gate_a")
-            weave_left_beside(0, 1, 0)
-            weave_left_beside(1, 2, 1, last=SHARE_A)
-            group("h", [(0, 0), (0, 1)], WOVEN, BF16, "gate_b")
-            scale_weave(0, 0)
-            scale_weave(0, 1)
-            for a in range(2):
-                group("wt", [(3, a)], WOVEN, BF16, "one")
-                turn_pair(3, a)
-            up_group(0, 2)
-            up_group(1, 0)
-            quant_up(3, 0, 1)
-            quant_up(3, 1, 2)
-            up_group(0, 3)
-            quant_h(0, 0, 2)
-            quant_left(0, 1)
-            left_tile(2, 4, "gate_b")
-            weave_left_beside(2, 4, 2)
-            weave_left_beside(1, 2, 1, first=SHARE_A, last=SHARE_A2)
-            group("h", [(0, 2)], WOVEN, BF16, "one")
-            group("h", [(0, 3)], WOVEN, BF16, "two")
-            group("h", [(1, 0)], WOVEN, BF16, "one")
-            scale_weave(0, 2)
-            scale_weave(1, 0)
-            scale_weave(0, 3)
-            up_group(1, 1)
-            up_group(1, 2)
-            up_group(1, 3, banks=[3, 4, 5, 6])
-            quant_left(1, 2)
-            quant_h(0, 2, 3)
-            quant_left_one(2)
-            quant_h(0, 3, 4)
-            quant_left_one(3)
-            quant_h(1, 0, 1)
-            right_tile(5, "gate_b", 0, 2)
-            weave_right_beside(5, 0, 2)
-            group("h", [(1, 1)], WOVEN, BF16, "gate_c")
-            scale_weave(1, 1)
-            for m in range(4):
-                open_tile(0, m, m)
+            quant_up(1, 0)
+            quant_up(1, 1)
+            w2_piece("c", [0, 1], [3], "one")
+            weave_w2("V", "c")
+            quant_v(0, 1)
+            woven("wt", (2, 0), "one")
+            turn(2, 0, [5, 6])
+            woven("wt", (2, 1), "gate_a")
+            turn(2, 1, [0, 1])
+            up_group(0, 1, [2, 3, 4, 5])
+            quant_w2("c")
+            quant_up(2, 0)
+            quant_up(2, 1)
+            quant_v(1, 1)
+            w2_piece("a", [0, 1], [0, 1, 2], "gate_a")
+            weave_w2("G", "a")
+            woven("h", (0, 0), "one")
+            woven("h", (0, 1), "gate_b")
+            scale_h(0, 0)
+            scale_h(0, 1)
+            woven("wt", (3, 0), "one")
+            turn(3, 0, [6, 0])
+            woven("wt", (3, 1), "one")
+            turn(3, 1, [1, 2])
+            up_group(0, 2, [3, 4, 5, 6])
+            up_group(1, 0, [0, 1, 2, 3])
+            quant_up(3, 0)
+            quant_up(3, 1)
+            up_group(0, 3, [4, 5, 6, 0])
+            quant_h(0, 0)
+            quant_w2("a", 0, 3 * P)
+            quant_h(0, 1)
+            quant_w2("a", 3 * P, 6 * P)
+            w2_piece("b", [2, 3], [0, 1, 2, 3, 4], "gate_b")
+            weave_w2("G", "b")
+            woven("h", (0, 2), "one")
+            woven("h", (0, 3), "two")
+            woven("h", (1, 0), "one")
+            scale_h(0, 2)
+            scale_h(1, 0)
+            scale_h(0, 3)
+            up_group(1, 1, [1, 2, 3, 4])
+            up_group(1, 2, [5, 6, 0, 1])
+            up_group(1, 3, [2, 3, 4, 5])
+            w2_piece("d", [0, 1], [4], "gate_a")
+            weave_w2("S", "d")
+            quant_h(0, 2)
+            quant_w2("b", 0, 4 * P)
+            quant_h(0, 3)
+            quant_w2("b", 4 * P, 8 * P)
+            quant_w2("b", 8 * P, 10 * P)
+            quant_h(1, 0)
+            quant_w2("d")
+
+            w2_piece("e", [0, 1], [5], "gate_a")
+            weave_w2("G", "e")
+            woven("h", (1, 1), "gate_c")
+            scale_h(1, 1)
+            for m, b in zip(range(4), [6, 0, 1, 2]):
+                open_tile(0, m, b)
             for g in range(NH - 1):
                 down(0, range(4), [g])
-            right_tile(4, "gate_a")
-            weave_right("S", 4)
-            group("hflat", [(1, 3)], FLAT, BF16, "flat")
-            group("h", [(1, 3)], WOVEN, BF16, "last")
+            flat("hflat", (1, 3))
+            woven("h", (1, 3), "last")
+            scale_h_rows(1, 3, [0, 1, 2])
             for m in range(4):
                 down(0, [m], [3])
                 finish("S", 0, m)
-            scale_rows(1, 3)
-            weave_h("S", 1, 3, first=SPLIT_H)
-            quant_right(4)
-            quant_h(1, 1, 2)
-            quant_right(5, 0, 2)
-            right_tile(5, "gate_c", 2, 4)
-            weave_right_beside(5, 2, 4)
-            group("h", [(1, 2)], WOVEN, BF16, "one")
-            scale_weave(1, 2)
-            for m, b in zip(range(4), [4, 5, 6, 0]):
-                open_tile(1, m, b)
-            down(1, range(4), [0])
-            open_tile(0, 4, 1)
+            scale_h_rows(1, 3, [3])
+            quant_w2("e")
+            quant_h(1, 1)
+            w2_piece("f", [2, 3], [5], "gate_c")
+            weave_w2("G", "f")
+            woven("h", (1, 2), "one")
+            scale_h(1, 2)
+            open_tile(0, 4, 3)
             down(0, [4], range(NH))
             finish("S", 0, 4)
-            down(1, range(4), [1])
-            quant_right(5, 2, 4)
-            for n, m, b in [(0, 5, 2), (1, 4, 3)]:
-                open_tile(n, m, b)
-                down(n, [m], [0, 1])
+            weave_h("S", 1, 3)
+            for m, b in zip(range(5), [4, 5, 6, 0, 1]):
+                open_tile(1, m, b)
+            down(1, range(5), [0])
+            open_tile(0, 5, 2)
+            down(0, [5], [0, 1])
+            down(1, range(5), [1])
+            quant_w2("f")
+            open_tile(1, 5, 3)
+            down(1, [5], [0, 1])
             down(0, [5], [2, 3])
             finish("S", 0, 5)
-            quant_h(1, 2, 3)
-            weave_h("V", 1, 3, last=SPLIT_H)
-            quant_h(1, 3, 4)
-            right_tile(6, "two")
-            weave_right("V", 6)
-            quant_right(6)
-            right_tile(7, "gate_b")
-            weave_right("V", 7)
-            down(1, range(5), [2])
-            open_tile(1, 5, 7)
-            down(1, [5], [0])
+            quant_h(1, 2)
+            quant_h(1, 3)
+            w2_piece("r6", range(NH), [6], "two")
+            weave_w2("V", "r6")
+            w2_piece("r7", range(NH), [7], "gate_b")
+            weave_w2("V", "r7", 0, 32)
+            quant_w2("r6")
+            weave_w2("V", "r7", 32, P)
+            down(1, range(3), [2])
             for m in range(5):
-                down(1, [m], [3])
+                down(1, [m], [3] if m < 3 else [2, 3])
                 finish("S", 1, m)
-            quant_right(7)
-            down(1, [5], [1, 2, 3])
+            quant_w2("r7")
+            down(1, [5], [2, 3])
             finish("V", 1, 5)
-            for n, m, b in [(0, 6, 1), (1, 6, 2)]:
+            for n, m, b in [(0, 6, 7), (1, 6, 2)]:
                 open_tile(n, m, b)
                 down(n, [m], range(NH))
                 finish("VS"[n], n, m)

@@ -26,7 +26,7 @@ BETA_COLUMN = 16
 RUN = 4
 FLAT = [T, BANK]
 WOVEN = [BANK, T]
-BUFS = {"flat": 4, "one": 6, "two": 1, "gate_a": 1, "gate_b": 1, "gate_c": 1, "last": 1, "sig": 4, "res": 8}
+BUFS = {"rows": 2, "flat": 1, "one": 5, "two": 1, "gate_a": 1, "gate_b": 1, "gate_c": 1, "last": 1, "sig": 4, "res": 7}
 
 
 def tile_rbm_mean_field_reconstruction_s7_kernel(tc, v_bytes, v_scale, w, beta, out):
@@ -108,23 +108,30 @@ def tile_rbm_mean_field_reconstruction_s7_kernel(tc, v_bytes, v_scale, w, beta, 
             for i, key in enumerate(keys):
                 live[(kind,) + key] = tile[:, i]
 
-        def widen(e, c, n, ts):
-            flat = live["vflat", c, n]
-            for t in ts:
-                src = live["vraw", c, t // 2][:, t % 2, samples(n)].bitcast(FP8)
-                if e == "V":
-                    nc.vector.tensor_scalar(out=flat[:, t, :], in0=src, scalar1=vs[:, c, t : t + 1], scalar2=None, op0=ALU.mult)
-                else:
-                    nc.scalar.activation(out=flat[:, t, :], in_=src, func=ACT.Copy, scale=vs[:, c, t : t + 1])
+        def widen(e, c, t, first=0, last=B):
+            src = live["vraw", c, t // 2][:, t % 2, first:last].bitcast(FP8)
+            dst = live["vrows", c][:, t, first:last]
+            if e == "V":
+                nc.vector.tensor_scalar(out=dst, in0=src, scalar1=vs[:, c, t : t + 1], scalar2=None, op0=ALU.mult)
+            else:
+                nc.scalar.activation(out=dst, in_=src, func=ACT.Copy, scale=vs[:, c, t : t + 1])
 
-        def weave_v(c, n):
-            weave("V", live["vgrp", c, n], live["vflat", c, n])
+        def v_rows(c):
+            rows = staged("rows", ("vrows", c), [P, T, B], BF16)
+            for n in range(2):
+                live["vflat", c, n] = rows[:, :, samples(n)]
+
+        def weave_v(c, n, first=0, last=BANK):
+            weave("V", live["vgrp", c, n][:, first:last, :], live["vflat", c, n][:, :, first:last])
 
         def whole(kind, key):
             return live[kind, key, "tile"][:].rearrange("p a n t -> p (a n) t")
 
         def quant_v(c, n):
             quantise(v_codes[:, n, samples(c)], v_sc[:, n, samples(c)], live["vgrp", c, n])
+
+        def quant_v_both(n):
+            quantise(v_codes[:, n, :], v_sc[:, n, :], whole("vgrp", (0, n)))
 
         def turn(g, a, banks, engines="SS"):
             words = w_rows[:].bitcast(F32)
@@ -146,6 +153,9 @@ def tile_rbm_mean_field_reconstruction_s7_kernel(tc, v_bytes, v_scale, w, beta, 
         def quant_up(g, a):
             cols = slice(a * KP, (a + 1) * KP)
             quantise(wt_codes[:, g, cols], wt_sc[:, g, cols], live["wt", g, a])
+
+        def quant_up_both(g):
+            quantise(wt_codes[:, g, :], wt_sc[:, g, :], whole("wt", (g, 0)))
 
         def w2_piece(name, gs, ms, tag):
             tile = staged(tag, ("w2", name), [P, len(gs), len(ms) * P, T], BF16)
@@ -205,10 +215,18 @@ def tile_rbm_mean_field_reconstruction_s7_kernel(tc, v_bytes, v_scale, w, beta, 
                                      func=ACT.Copy, scale=beta32[:, g, t : t + 1])
 
         def weave_h(e, n, g, first=0, last=BANK):
-            weave(e, live["h", n, g][:, first:last, :], live["hflat", n, g][:, :, first:last])
+            if e == "G":
+                nc.gpsimd.tensor_scalar(out=live["h", n, g][:, first:last, :], in0=live["hflat", n, g][:, :, first:last].rearrange("p t n -> p n t"),
+                                        scalar1=1.0, scalar2=0.0, op0=ALU.mult, op1=ALU.add)
+            else:
+                weave(e, live["h", n, g][:, first:last, :], live["hflat", n, g][:, :, first:last])
 
         def quant_h(n, g):
             quantise(h_codes[:, n, samples(g)], h_sc[:, n, samples(g)], live["h", n, g])
+
+        def quant_h_both(n, g):
+            cols = slice(g * BANK, (g + 2) * BANK)
+            quantise(h_codes[:, n, cols], h_sc[:, n, cols], whole("h", (n, g)))
 
         def open_tile(n, m, b, first=0, last=BANK):
             new_bank(("nb", n, m, first), b)
@@ -227,11 +245,11 @@ def tile_rbm_mean_field_reconstruction_s7_kernel(tc, v_bytes, v_scale, w, beta, 
                                         start=(left == NH), stop=(left == 1))
                     live["todo", n, m, first] = left - 1
 
-        def finish(e, n, m, first=0):
+        def finish(e, n, m, first=0, queue=nc.sync):
             width = live["width", n, m, first]
             res = staged("res", ("res", n, m, first), [P, BANK], F32)
             copy_on[e](out=res[:, 0:width], in_=live["nb", n, m, first][:, 0:width])
-            nc.sync.dma_start(out=out[m * P : (m + 1) * P, n * BANK + first : n * BANK + first + width], in_=res[:, 0:width])
+            queue.dma_start(out=out[m * P : (m + 1) * P, n * BANK + first : n * BANK + first + width], in_=res[:, 0:width])
 
         def woven(kind, key, tag):
             group(kind, [key], WOVEN, BF16, tag)
@@ -255,16 +273,20 @@ def tile_rbm_mean_field_reconstruction_s7_kernel(tc, v_bytes, v_scale, w, beta, 
                 load_w(g, 1)
             warm_up(BANK, 6)
             warm_up(BANK, 6)
-            for n in range(2):
-                for c in range(NV):
-                    flat("vflat", (c, n))
-            widen("V", 0, 0, range(T))
-            widen("S", 0, 1, range(T))
+            v_rows(0)
+            v_rows(1)
+            widen("V", 0, 0)
+            widen("S", 0, 1)
             nc.scalar.copy(out=beta32[:], in_=beta_bf[:])
             new_bank("factors", FACTOR_BANK)
             beta_to_bank()
-            widen("V", 1, 0, range(T))
-            widen("S", 1, 1, [0, 1, 2])
+            widen("V", 0, 2)
+            widen("S", 0, 3)
+            widen("V", 1, 0)
+            widen("V", 1, 2)
+            widen("V", 1, 3, last=BANK)
+            widen("S", 1, 1)
+            widen("S", 1, 3, first=BANK)
             woven("wt", (0, 0), "one")
             turn(0, 0, [0, 1])
             woven("wt", (0, 1), "one")
@@ -273,9 +295,8 @@ def tile_rbm_mean_field_reconstruction_s7_kernel(tc, v_bytes, v_scale, w, beta, 
             woven("vgrp", (0, 0), "one")
             woven("vgrp", (1, 0), "one")
             weave_v(0, 0)
-            widen("V", 1, 1, [3])
-            quant_v(0, 0)
             weave_v(1, 0)
+            quant_v(0, 0)
             quant_up(0, 0)
             quant_v(1, 0)
             quant_up(0, 1)
@@ -284,28 +305,23 @@ def tile_rbm_mean_field_reconstruction_s7_kernel(tc, v_bytes, v_scale, w, beta, 
             woven("wt", (1, 1), "one")
             turn(1, 1, [6, 0])
             up_group(0, 0, [1, 2, 3, 4])
-            woven("vgrp", (0, 1), "two")
-            woven("vgrp", (1, 1), "one")
+            group("vgrp", [(0, 1), (1, 1)], WOVEN, BF16, "two")
             weave_v(0, 1)
             weave_v(1, 1)
             quant_up(1, 0)
             quant_up(1, 1)
             w2_piece("c", [0, 1], [3], "one")
             weave_w2("V", "c")
-            quant_v(0, 1)
-            woven("wt", (2, 0), "one")
+            group("wt", [(2, 0), (2, 1)], WOVEN, BF16, "gate_a")
             turn(2, 0, [5, 6])
-            woven("wt", (2, 1), "gate_a")
             turn(2, 1, [0, 1])
             up_group(0, 1, [2, 3, 4, 5])
+            quant_v_both(1)
+            quant_up_both(2)
             quant_w2("c")
-            quant_up(2, 0)
-            quant_up(2, 1)
-            quant_v(1, 1)
             w2_piece("a", [0, 1], [0, 1, 2], "gate_a")
             weave_w2("G", "a")
-            woven("h", (0, 0), "one")
-            woven("h", (0, 1), "gate_b")
+            group("h", [(0, 0), (0, 1)], WOVEN, BF16, "gate_b")
             scale_h(0, 0)
             scale_h(0, 1)
             woven("wt", (3, 0), "one")
@@ -317,9 +333,8 @@ def tile_rbm_mean_field_reconstruction_s7_kernel(tc, v_bytes, v_scale, w, beta, 
             quant_up(3, 0)
             quant_up(3, 1)
             up_group(0, 3, [4, 5, 6, 0])
-            quant_h(0, 0)
             quant_w2("a", 0, 3 * P)
-            quant_h(0, 1)
+            quant_h_both(0, 0)
             quant_w2("a", 3 * P, 6 * P)
             w2_piece("b", [2, 3], [0, 1, 2, 3, 4], "gate_b")
             weave_w2("G", "b")
@@ -331,25 +346,29 @@ def tile_rbm_mean_field_reconstruction_s7_kernel(tc, v_bytes, v_scale, w, beta, 
             scale_h(0, 3)
             up_group(1, 1, [1, 2, 3, 4])
             up_group(1, 2, [5, 6, 0, 1])
-            up_group(1, 3, [2, 3, 4, 5])
             w2_piece("d", [0, 1], [4], "gate_a")
-            weave_w2("S", "d")
+            for t, b in enumerate([2, 3, 4, 5]):
+                for c in range(NV):
+                    up_pass(1, 3, t, c, b)
+                sigmoid(1, 3, t)
+                if t == 1:
+                    weave_w2("S", "d")
             quant_h(0, 2)
             quant_w2("b", 0, 4 * P)
             quant_h(0, 3)
             quant_w2("b", 4 * P, 8 * P)
+            quant_w2("d")
             quant_w2("b", 8 * P, 10 * P)
             quant_h(1, 0)
-            quant_w2("d")
 
-            w2_piece("e", [0, 1], [5], "gate_a")
+            w2_piece("e", [0, 1], [5], "gate_b")
             weave_w2("G", "e")
             woven("h", (1, 1), "gate_c")
             scale_h(1, 1)
             for m, b in zip(range(4), [6, 0, 1, 2]):
                 open_tile(0, m, b)
-            for g in range(NH - 1):
-                down(0, range(4), [g])
+            down(0, range(4), [0, 1])
+            down(0, range(4), [2])
             flat("hflat", (1, 3))
             woven("h", (1, 3), "last")
             scale_h_rows(1, 3, [0, 1, 2])
@@ -359,7 +378,7 @@ def tile_rbm_mean_field_reconstruction_s7_kernel(tc, v_bytes, v_scale, w, beta, 
             scale_h_rows(1, 3, [3])
             quant_w2("e")
             quant_h(1, 1)
-            w2_piece("f", [2, 3], [5], "gate_c")
+            w2_piece("f", [2, 3], [5], "gate_b")
             weave_w2("G", "f")
             woven("h", (1, 2), "one")
             scale_h(1, 2)
@@ -397,9 +416,7 @@ def tile_rbm_mean_field_reconstruction_s7_kernel(tc, v_bytes, v_scale, w, beta, 
                 open_tile(n, m, b)
                 down(n, [m], range(NH))
                 finish("VS"[n], n, m)
-            for n in range(2):
-                for half, b in enumerate([[4, 5], [6, 0]][n]):
-                    first = half * BANK // 2
-                    open_tile(n, 7, b, first, first + BANK // 2)
-                    down(n, [7], range(NH), first)
-                    finish("SV"[half], n, 7, first)
+            for n, first, last, b, e in [(0, 0, 256, 4, "S"), (0, 256, 512, 5, "V"), (1, 0, 256, 6, "S"), (1, 256, 384, 0, "V"), (1, 384, 512, 1, "S")]:
+                open_tile(n, 7, b, first, last)
+                down(n, [7], range(NH), first)
+                finish(e, n, 7, first, nc.scalar if last == BANK and n == 1 else nc.sync)

@@ -133,6 +133,11 @@ def tile_rbm_mean_field_reconstruction_s7_kernel(tc, v_bytes, v_scale, w, beta, 
         def quant_v_both(n):
             quantise(v_codes[:, n, :], v_sc[:, n, :], whole("vgrp", (0, n)))
 
+        def part_words(g, a, tag):
+            parted = staged(tag, ("parted", g, a), [P, 2 * NV, 2, P], F32)
+            first = (g * T + 2 * a) * V // 2
+            nc.vector.tensor_copy(out=parted[:], in_=w_rows[:].bitcast(F32)[:, first : first + V].rearrange("p (k m u) -> p k u m", m=P, u=2))
+
         def turn(g, a, banks, engines="SS"):
             words = w_rows[:].bitcast(F32)
             dst = live["wt", g, a].rearrange("p m t -> p (m t)").bitcast(F32).rearrange("p (c i m u) -> p c i m u", c=NV, i=2, u=2)
@@ -142,7 +147,11 @@ def tile_rbm_mean_field_reconstruction_s7_kernel(tc, v_bytes, v_scale, w, beta, 
                     first = (g * T + 2 * a + i) * V // 2 + c * KP // 2
                     for u in range(2):
                         j = (2 * i + u) * P
-                        nc.tensor.transpose(bank[:, j : j + P], words[:, first + u : first + 2 * P : 2], ident[:])
+                        if ("parted", g, a) in live:
+                            rows = live["parted", g, a][:, 2 * i + c, u, :]
+                        else:
+                            rows = words[:, first + u : first + 2 * P : 2]
+                        nc.tensor.transpose(bank[:, j : j + P], rows, ident[:])
                 live["tdst", g, a, c] = dst[:, c]
                 if engines[c] != "-":
                     empty_turned(engines[c], g, a, c)
@@ -317,6 +326,7 @@ def tile_rbm_mean_field_reconstruction_s7_kernel(tc, v_bytes, v_scale, w, beta, 
             turn(2, 1, [0, 1])
             up_group(0, 1, [2, 3, 4, 5])
             quant_v_both(1)
+            part_words(3, 1, "last")
             quant_up_both(2)
             quant_w2("c")
             w2_piece("a", [0, 1], [0, 1, 2], "gate_a")
@@ -324,15 +334,12 @@ def tile_rbm_mean_field_reconstruction_s7_kernel(tc, v_bytes, v_scale, w, beta, 
             group("h", [(0, 0), (0, 1)], WOVEN, BF16, "gate_b")
             scale_h(0, 0)
             scale_h(0, 1)
-            woven("wt", (3, 0), "one")
+            group("wt", [(3, 0), (3, 1)], WOVEN, BF16, "two")
             turn(3, 0, [6, 0])
-            woven("wt", (3, 1), "one")
             turn(3, 1, [1, 2])
             up_group(0, 2, [3, 4, 5, 6])
             up_group(1, 0, [0, 1, 2, 3])
-            quant_up(3, 0)
-            quant_up(3, 1)
-            up_group(0, 3, [4, 5, 6, 0])
+            quant_up_both(3)
             quant_w2("a", 0, 3 * P)
             quant_h_both(0, 0)
             quant_w2("a", 3 * P, 6 * P)
@@ -342,9 +349,10 @@ def tile_rbm_mean_field_reconstruction_s7_kernel(tc, v_bytes, v_scale, w, beta, 
             woven("h", (0, 3), "two")
             woven("h", (1, 0), "one")
             scale_h(0, 2)
+            up_group(1, 1, [4, 5, 6, 0])
             scale_h(1, 0)
+            up_group(0, 3, [1, 2, 3, 4])
             scale_h(0, 3)
-            up_group(1, 1, [1, 2, 3, 4])
             up_group(1, 2, [5, 6, 0, 1])
             w2_piece("d", [0, 1], [4], "gate_a")
             for t, b in enumerate([2, 3, 4, 5]):

@@ -21,12 +21,12 @@ KP = P * T
 NV = V // KP
 NH = H // KP
 BANK = 512
-FACTOR_BANK = 7
-BETA_COLUMN = 16
+HALF = 256
+BETA_BANK = 7
 RUN = 4
-FLAT = [T, BANK]
-WOVEN = [BANK, T]
-BUFS = {"rows": 2, "flat": 1, "one": 5, "two": 1, "gate_a": 1, "gate_b": 1, "gate_c": 1, "last": 1, "sig": 4, "res": 7}
+SLOT = 4096
+SIG_BUFS = 5
+RES_BUFS = 10
 
 
 def tile_rbm_mean_field_reconstruction_s7_kernel(tc, v_bytes, v_scale, w, beta, out):
@@ -34,6 +34,7 @@ def tile_rbm_mean_field_reconstruction_s7_kernel(tc, v_bytes, v_scale, w, beta, 
     with ExitStack() as ctx:
         keep = ctx.enter_context(tc.tile_pool(name="keep", bufs=1))
         rot = ctx.enter_context(tc.tile_pool(name="rot", bufs=1))
+        arena = ctx.enter_context(tc.tile_pool(name="arena", bufs=1))
         psum = ctx.enter_context(tc.psum_pool(name="psum", bufs=1))
 
         w_view = w.rearrange("(g p t) v -> g p (t v)", p=P, t=T)
@@ -48,12 +49,12 @@ def tile_rbm_mean_field_reconstruction_s7_kernel(tc, v_bytes, v_scale, w, beta, 
         wt_sc = keep.tile([P, NH, 2 * KP], U8, name="wt_sc", align_bytes=64)
         w2_codes = keep.tile([P, NH * V], U32, name="w2_codes", align_bytes=64)
         w2_sc = keep.tile([P, NH * V], U8, name="w2_sc", align_bytes=64)
-        h_codes = keep.tile([P, 2, NH * BANK], U32, name="h_codes", align_bytes=64)
-        h_sc = keep.tile([P, 2, NH * BANK], U8, name="h_sc", align_bytes=64)
+        h_codes = keep.tile([P, 2 * NH * BANK], U32, name="h_codes", align_bytes=64)
+        h_sc = keep.tile([P, 2 * NH * BANK], U8, name="h_sc", align_bytes=64)
         w_rows = keep.tile([P, NH * T * V], BF16, name="w_rows", align_bytes=64)
         zeros = keep.tile([P, BANK], F32, name="zeros")
         live = {}
-        used = [0]
+        used = {"w2": 0, "h": 0}
         copy_on = {"V": nc.vector.tensor_copy, "S": nc.scalar.copy}
         w_gtv = w_rows[:].rearrange("p (g t v) -> p g t v", g=NH, t=T)
         w_gvt = w_rows[:].rearrange("p (g t v) -> p g v t", g=NH, t=T)
@@ -61,86 +62,62 @@ def tile_rbm_mean_field_reconstruction_s7_kernel(tc, v_bytes, v_scale, w, beta, 
         def samples(n):
             return slice(n * BANK, (n + 1) * BANK)
 
-        def staged(tag, key, shape, dtype):
-            if key not in live:
-                live[key] = rot.tile(shape, dtype, name=tag, align_bytes=64, bufs=BUFS[tag])
+        def stage(key, slot, shape, dtype=BF16):
+            live[key] = arena.tile([P] + shape, dtype, name="at%d" % slot, align_bytes=64, offset=slot * SLOT)
             return live[key]
 
         def new_bank(key, b):
             live[key] = psum.tile([P, BANK], F32, name="bank%d" % b)
             return live[key]
 
-        def weave(e, dst, src):
-            o = dst.rearrange("p (c i) t -> p c t i", i=RUN)
-            s = src.rearrange("p t (c i) -> p c t i", i=RUN)
-            copy_on[e](out=o, in_=s)
+        def runs_out(dst):
+            return dst.rearrange("p (c i) t -> p c t i", i=RUN)
 
-        def weave_times(dst, src, factor):
-            width = src.shape[2]
-            nc.vector.tensor_tensor(
-                out=dst.rearrange("p (c i) t -> p c t i", i=RUN),
-                in0=src.rearrange("p t (c i) -> p c t i", i=RUN),
-                in1=factor.unsqueeze(1).unsqueeze(3).to_broadcast([P, width // RUN, T, RUN]),
-                op=ALU.mult)
+        def runs_in(src):
+            return src.rearrange("p t (c i) -> p c t i", i=RUN)
 
         def quantise(codes, scales, grouped):
             nc.vector.quantize_mx(out=codes.bitcast(FP8X4), scales=scales, in_=grouped.rearrange("p n t -> p (n t)"))
 
-        def small_loads():
-            nc.scalar.dma_start(out=vs[:], in_=v_scale.rearrange("(c p t) o -> p c (t o)", p=P, t=T))
-            nc.scalar.dma_start(out=beta_bf[:], in_=beta.rearrange("(g p t) o -> p g (t o)", p=P, t=T))
-            make_identity(nc, ident[:])
-            dummy = keep.tile([P, 1], F32, name="dummy")
-            nc.vector.memset(zeros[:], 0.0)
-            nc.scalar.activation(out=dummy[:], in_=zeros[:, 0:1], func=ACT.Sigmoid)
+        def load_v(c, n, first=0, last=T):
+            raw = keep.tile([P, last - first, BANK], U8, name="v_raw%d_%d_%d" % (c, n, first), align_bytes=64)
+            nc.sync.dma_start(out=raw[:], in_=v_view[c][:, first:last, samples(n)])
+            for t in range(first, last):
+                live["vraw", c, n, t] = raw[:, t - first, :]
 
-        def load_v(c, a):
-            raw = keep.tile([P, 2, B], U8, name="v_raw%d_%d" % (c, a), align_bytes=64)
-            nc.sync.dma_start(out=raw[:], in_=v_view[c][:, 2 * a : 2 * a + 2, :])
-            live["vraw", c, a] = raw
+        def load_v_rows(c, first, last):
+            raw = keep.tile([P, last - first, B], U8, name="v_rows%d_%d" % (c, first), align_bytes=64)
+            nc.sync.dma_start(out=raw[:], in_=v_view[c][:, first:last, :])
+            for t in range(first, last):
+                for n in range(2):
+                    live["vraw", c, n, t] = raw[:, t - first, samples(n)]
 
         def load_w(g, a):
             first = (g * T + 2 * a) * V
             nc.sync.dma_start(out=w_rows[:, first : first + 2 * V], in_=w_view[g][:, 2 * a * V : 2 * (a + 1) * V])
 
-        def group(kind, keys, shape, dtype, tag):
-            tile = staged(tag, (kind, keys[0], "tile"), [P, len(keys)] + shape, dtype)
-            for i, key in enumerate(keys):
-                live[(kind,) + key] = tile[:, i]
-
-        def widen(e, c, t, first=0, last=B):
-            src = live["vraw", c, t // 2][:, t % 2, first:last].bitcast(FP8)
-            dst = live["vrows", c][:, t, first:last]
+        def widen(e, c, n, t):
+            src = live["vraw", c, n, t].bitcast(FP8)
+            dst = live["vflat", c, n][:, t, :]
             if e == "V":
                 nc.vector.tensor_scalar(out=dst, in0=src, scalar1=vs[:, c, t : t + 1], scalar2=None, op0=ALU.mult)
             else:
                 nc.scalar.activation(out=dst, in_=src, func=ACT.Copy, scale=vs[:, c, t : t + 1])
 
-        def v_rows(c):
-            rows = staged("rows", ("vrows", c), [P, T, B], BF16)
-            for n in range(2):
-                live["vflat", c, n] = rows[:, :, samples(n)]
+        def weave_v(e, c, n, first=0, last=BANK):
+            copy_on[e](out=runs_out(live["v", n][:, c * BANK + first : c * BANK + last, :]), in_=runs_in(live["vflat", c, n][:, :, first:last]))
 
-        def weave_v(c, n, first=0, last=BANK):
-            weave("V", live["vgrp", c, n][:, first:last, :], live["vflat", c, n][:, :, first:last])
+        def quant_v(n, first=0, last=NV):
+            cols = slice(first * BANK, last * BANK)
+            quantise(v_codes[:, n, cols], v_sc[:, n, cols], live["v", n][:, cols, :])
 
-        def whole(kind, key):
-            return live[kind, key, "tile"][:].rearrange("p a n t -> p (a n) t")
-
-        def quant_v(c, n):
-            quantise(v_codes[:, n, samples(c)], v_sc[:, n, samples(c)], live["vgrp", c, n])
-
-        def quant_v_both(n):
-            quantise(v_codes[:, n, :], v_sc[:, n, :], whole("vgrp", (0, n)))
-
-        def part_words(g, a, tag):
-            parted = staged(tag, ("parted", g, a), [P, 2 * NV, 2, P], F32)
+        def part_words(g, a, slot):
+            parted = stage(("parted", g, a), slot, [2 * NV, 2, P], F32)
             first = (g * T + 2 * a) * V // 2
             nc.vector.tensor_copy(out=parted[:], in_=w_rows[:].bitcast(F32)[:, first : first + V].rearrange("p (k m u) -> p k u m", m=P, u=2))
 
-        def turn(g, a, banks, engines="SS"):
+        def turn(g, a, banks):
             words = w_rows[:].bitcast(F32)
-            dst = live["wt", g, a].rearrange("p m t -> p (m t)").bitcast(F32).rearrange("p (c i m u) -> p c i m u", c=NV, i=2, u=2)
             for c in range(NV):
                 bank = new_bank(("tb", g, a, c), banks[c])
                 for i in range(2):
@@ -152,33 +129,27 @@ def tile_rbm_mean_field_reconstruction_s7_kernel(tc, v_bytes, v_scale, w, beta, 
                         else:
                             rows = words[:, first + u : first + 2 * P : 2]
                         nc.tensor.transpose(bank[:, j : j + P], rows, ident[:])
-                live["tdst", g, a, c] = dst[:, c]
-                if engines[c] != "-":
-                    empty_turned(engines[c], g, a, c)
 
-        def empty_turned(e, g, a, c):
-            copy_on[e](out=live["tdst", g, a, c], in_=live["tb", g, a, c][:].rearrange("p (i u m) -> p i m u", i=2, u=2))
+        def empty_turned(g, a, engines="SS"):
+            dst = live["wt", g][:, a * KP : (a + 1) * KP, :].rearrange("p m t -> p (m t)").bitcast(F32).rearrange("p (c i m u) -> p c i m u", c=NV, i=2, u=2)
+            for c in range(NV):
+                copy_on[engines[c]](out=dst[:, c], in_=live["tb", g, a, c][:].rearrange("p (i u m) -> p i m u", i=2, u=2))
 
-        def quant_up(g, a):
-            cols = slice(a * KP, (a + 1) * KP)
-            quantise(wt_codes[:, g, cols], wt_sc[:, g, cols], live["wt", g, a])
+        def quant_up(g, first=0, last=2):
+            cols = slice(first * KP, last * KP)
+            quantise(wt_codes[:, g, cols], wt_sc[:, g, cols], live["wt", g][:, cols, :])
 
-        def quant_up_both(g):
-            quantise(wt_codes[:, g, :], wt_sc[:, g, :], whole("wt", (g, 0)))
-
-        def w2_piece(name, gs, ms, tag):
-            tile = staged(tag, ("w2", name), [P, len(gs), len(ms) * P, T], BF16)
-            live["w2span", name] = (slice(gs[0], gs[-1] + 1), ms[0] * P)
-            for i, g in enumerate(gs):
-                for j, m in enumerate(ms):
-                    live["w2col", g, m] = used[-1] + (i * len(ms) + j) * P
-            live["w2base", name] = used[-1]
-            used.append(used[-1] + len(gs) * len(ms) * P)
-            return tile
+        def w2_piece(name, gs, ms, slot):
+            stage(("w2", name), slot, [len(gs), len(ms) * P, T])
+            live["w2span", name] = (slice(gs[0], gs[-1] + 1), ms[0] * P, used["w2"])
+            for g in gs:
+                for m in ms:
+                    live["w2col", g, m] = used["w2"]
+                    used["w2"] = used["w2"] + P
 
         def weave_w2(e, name, first=0, last=None):
             tile = live["w2", name]
-            gs, v0 = live["w2span", name]
+            gs, v0, base = live["w2span", name]
             last = tile.shape[2] if last is None else last
             if e == "G":
                 nc.gpsimd.tensor_scalar(out=tile[:, :, first:last, :], in0=w_gvt[:, gs, v0 + first : v0 + last, :],
@@ -189,242 +160,287 @@ def tile_rbm_mean_field_reconstruction_s7_kernel(tc, v_bytes, v_scale, w, beta, 
 
         def quant_w2(name, first=0, last=None):
             words = live["w2", name][:].rearrange("p g v t -> p (g v) t")
-            last = words.shape[1] if last is None else last
-            cols = slice(live["w2base", name] + first, live["w2base", name] + last)
-            quantise(w2_codes[:, cols], w2_sc[:, cols], words[:, first:last, :])
+            base = live["w2span", name][2]
+            last = words.shape[1] // P if last is None else last
+            cols = slice(base + first * P, base + last * P)
+            quantise(w2_codes[:, cols], w2_sc[:, cols], words[:, first * P : last * P, :])
 
         def warm_up(cols, b):
             bank = new_bank("warm", b)
             nc.tensor.matmul(out=bank[:, 0:cols], lhsT=zeros[:, 0:P], rhs=zeros[:, 0:cols], start=True, stop=True)
 
         def beta_to_bank():
-            cols = slice(BETA_COLUMN, BETA_COLUMN + NH * T)
-            nc.tensor.matmul(out=live["factors"][:, cols], lhsT=ident[:], rhs=beta32[:].rearrange("p g t -> p (g t)"), start=True, stop=True)
-            live["beta"] = live["factors"][:, cols].rearrange("p (g t) -> p g t", t=T)
+            bank = new_bank("factors", BETA_BANK)
+            nc.tensor.matmul(out=bank[:, 0 : NH * T], lhsT=ident[:], rhs=beta32[:].rearrange("p g t -> p (g t)"), start=True, stop=True)
+            live["beta"] = bank[:, 0 : NH * T].rearrange("p (g t) -> p g t", t=T)
 
-        def up_pass(n, g, t, c, b=None):
-            if c == 0:
-                new_bank(("mb", n, g, t), b)
-            first = (t // 2) * KP + c * 2 * P + (t % 2) * P
-            m = slice(first, first + P)
-            nc.tensor.matmul_mx(out=live["mb", n, g, t][:], lhsT=wt_codes[:, g, m].bitcast(FP8X4), lhsT_scale=wt_sc[:, g, m],
-                                rhs=v_codes[:, n, samples(c)].bitcast(FP8X4), rhs_scale=v_sc[:, n, samples(c)],
-                                start=(c == 0), stop=(c == NV - 1))
+        def up(n, g, banks, ts=range(T)):
+            for t, b in zip(ts, banks):
+                bank = new_bank(("mb", n, g, t), b)
+                for c in range(NV):
+                    first = (t // 2) * KP + c * 2 * P + (t % 2) * P
+                    m = slice(first, first + P)
+                    nc.tensor.matmul_mx(out=bank[:], lhsT=wt_codes[:, g, m].bitcast(FP8X4), lhsT_scale=wt_sc[:, g, m],
+                                        rhs=v_codes[:, n, samples(c)].bitcast(FP8X4), rhs_scale=v_sc[:, n, samples(c)],
+                                        start=(c == 0), stop=(c == NV - 1))
 
-        def sigmoid(n, g, t):
-            sig = staged("sig", ("sig", n, g), [P, T, BANK], F32)
-            nc.scalar.activation(out=sig[:, t, :], in_=live["mb", n, g, t][:], func=ACT.Sigmoid, scale=beta32[:, g, t : t + 1])
+        def sigmoids(n, g, ts=range(T)):
+            if ("sig", n, g) not in live:
+                live["sig", n, g] = rot.tile([P, T, BANK], F32, name="sig", align_bytes=64, bufs=SIG_BUFS)
+            for t in ts:
+                nc.scalar.activation(out=live["sig", n, g][:, t, :], in_=live["mb", n, g, t][:], func=ACT.Sigmoid, scale=beta32[:, g, t : t + 1])
 
-        def scale_h(n, g, first=0, last=BANK):
-            weave_times(live["h", n, g][:, first:last, :], live["sig", n, g][:, :, first:last], live["beta"][:, g, :])
+        def h_piece(name, parts, slot):
+            tile = stage(("h", name), slot, [sum(last - first for n, g, first, last in parts), T])
+            live["hbase", name] = used["h"]
+            at = 0
+            for n, g, first, last in parts:
+                live["h", n, g, first] = tile[:, at : at + last - first, :]
+                live["hcol", n, g, first] = used["h"] + at
+                at = at + last - first
+            used["h"] = used["h"] + at
+
+        def scale_h(n, g, first=0, skip=0, stop=None):
+            dst = live["h", n, g, first]
+            stop = dst.shape[1] if stop is None else stop
+            nc.vector.tensor_tensor(
+                out=runs_out(dst[:, skip:stop, :]), in0=runs_in(live["sig", n, g][:, :, first + skip : first + stop]),
+                in1=live["beta"][:, g, :].unsqueeze(1).unsqueeze(3).to_broadcast([P, (stop - skip) // RUN, T, RUN]), op=ALU.mult)
 
         def scale_h_rows(n, g, ts=range(T), first=0, last=BANK):
             for t in ts:
                 nc.scalar.activation(out=live["hflat", n, g][:, t, first:last], in_=live["sig", n, g][:, t, first:last],
                                      func=ACT.Copy, scale=beta32[:, g, t : t + 1])
 
-        def weave_h(e, n, g, first=0, last=BANK):
-            if e == "G":
-                nc.gpsimd.tensor_scalar(out=live["h", n, g][:, first:last, :], in0=live["hflat", n, g][:, :, first:last].rearrange("p t n -> p n t"),
-                                        scalar1=1.0, scalar2=0.0, op0=ALU.mult, op1=ALU.add)
-            else:
-                weave(e, live["h", n, g][:, first:last, :], live["hflat", n, g][:, :, first:last])
+        def weave_h(e, n, g, first=0, skip=0, stop=None):
+            dst = live["h", n, g, first]
+            stop = dst.shape[1] if stop is None else stop
+            copy_on[e](out=runs_out(dst[:, skip:stop, :]), in_=runs_in(live["hflat", n, g][:, :, first + skip : first + stop]))
 
-        def quant_h(n, g):
-            quantise(h_codes[:, n, samples(g)], h_sc[:, n, samples(g)], live["h", n, g])
+        def quant_h(name, first=0, last=None):
+            tile = live["h", name]
+            last = tile.shape[1] if last is None else last
+            cols = slice(live["hbase", name] + first, live["hbase", name] + last)
+            quantise(h_codes[:, cols], h_sc[:, cols], tile[:, first:last, :])
 
-        def quant_h_both(n, g):
-            cols = slice(g * BANK, (g + 2) * BANK)
-            quantise(h_codes[:, n, cols], h_sc[:, n, cols], whole("h", (n, g)))
-
-        def open_tile(n, m, b, first=0, last=BANK):
+        def open_tile(n, m, b, first=0, last=BANK, base=0):
             new_bank(("nb", n, m, first), b)
             live["todo", n, m, first] = NH
-            live["width", n, m, first] = last - first
+            live["span", n, m, first] = (last - first, base)
 
         def down(n, ms, gs, first=0):
             for m in ms:
-                width = live["width", n, m, first]
+                width, base = live["span", n, m, first]
                 for g in gs:
-                    cols = slice(g * BANK + first, g * BANK + first + width)
+                    at = live["hcol", n, g, base] + first - base
+                    cols = slice(at, at + width)
                     mc = slice(live["w2col", g, m], live["w2col", g, m] + P)
                     left = live["todo", n, m, first]
                     nc.tensor.matmul_mx(out=live["nb", n, m, first][:, 0:width], lhsT=w2_codes[:, mc].bitcast(FP8X4), lhsT_scale=w2_sc[:, mc],
-                                        rhs=h_codes[:, n, cols].bitcast(FP8X4), rhs_scale=h_sc[:, n, cols],
+                                        rhs=h_codes[:, cols].bitcast(FP8X4), rhs_scale=h_sc[:, cols],
                                         start=(left == NH), stop=(left == 1))
                     live["todo", n, m, first] = left - 1
 
         def finish(e, n, m, first=0, queue=nc.sync):
-            width = live["width", n, m, first]
-            res = staged("res", ("res", n, m, first), [P, BANK], F32)
+            width = live["span", n, m, first][0]
+            res = rot.tile([P, BANK], F32, name="res", align_bytes=64, bufs=RES_BUFS)
             copy_on[e](out=res[:, 0:width], in_=live["nb", n, m, first][:, 0:width])
             queue.dma_start(out=out[m * P : (m + 1) * P, n * BANK + first : n * BANK + first + width], in_=res[:, 0:width])
 
-        def woven(kind, key, tag):
-            group(kind, [key], WOVEN, BF16, tag)
-
-        def flat(kind, key):
-            group(kind, [key], FLAT, BF16, "flat")
-
-        def up_group(n, g, banks):
-            for t in range(T):
-                for c in range(NV):
-                    up_pass(n, g, t, c, banks[t])
-                sigmoid(n, g, t)
-
+        flat = [T, BANK]
         with tc.manual_schedule():
-            small_loads()
-            for c in range(NV):
-                load_v(c, 0)
-                load_v(c, 1)
-            for g in range(NH):
+            nc.scalar.dma_start(out=vs[:], in_=v_scale.rearrange("(c p t) o -> p c (t o)", p=P, t=T))
+            make_identity(nc, ident[:])
+            dummy = keep.tile([P, 1], F32, name="dummy")
+            nc.vector.memset(zeros[:], 0.0)
+            nc.scalar.activation(out=dummy[:], in_=zeros[:, 0:1], func=ACT.Sigmoid)
+            load_v(0, 0, 0, 2)
+            load_v(0, 0, 2, 4)
+            load_v(1, 0)
+            for g in range(2):
+                load_w(g, 0)
+                load_w(g, 1)
+            nc.sync.dma_start(out=beta_bf[:], in_=beta.rearrange("(g p t) o -> p g (t o)", p=P, t=T))
+            load_v(0, 1)
+            load_v(1, 1)
+            for g in range(2, NH):
                 load_w(g, 0)
                 load_w(g, 1)
             warm_up(BANK, 6)
             warm_up(BANK, 6)
-            v_rows(0)
-            v_rows(1)
-            widen("V", 0, 0)
-            widen("S", 0, 1)
-            nc.scalar.copy(out=beta32[:], in_=beta_bf[:])
-            new_bank("factors", FACTOR_BANK)
-            beta_to_bank()
-            widen("V", 0, 2)
-            widen("S", 0, 3)
-            widen("V", 1, 0)
-            widen("V", 1, 2)
-            widen("V", 1, 3, last=BANK)
-            widen("S", 1, 1)
-            widen("S", 1, 3, first=BANK)
-            woven("wt", (0, 0), "one")
+            stage(("vflat", 0, 0), 0, flat)
+            stage(("vflat", 1, 0), 1, flat)
+            stage(("v", 0), 2, [2 * BANK, T])
+            for c, t, e in [(0, 0, "V"), (0, 1, "S"), (0, 2, "V"), (0, 3, "S"), (1, 0, "V"), (1, 1, "V"), (1, 2, "S"), (1, 3, "S")]:
+                widen(e, c, 0, t)
+            weave_v("V", 0, 0)
+            weave_v("S", 1, 0, 256, 512)
+            weave_v("V", 1, 0, 0, 256)
+            stage(("wt", 0), 4, [2 * KP, T])
             turn(0, 0, [0, 1])
-            woven("wt", (0, 1), "one")
+            empty_turned(0, 0)
             turn(0, 1, [2, 3])
+            empty_turned(0, 1)
             warm_up(BANK // 4, 6)
-            woven("vgrp", (0, 0), "one")
-            woven("vgrp", (1, 0), "one")
-            weave_v(0, 0)
-            weave_v(1, 0)
-            quant_v(0, 0)
-            quant_up(0, 0)
-            quant_v(1, 0)
-            quant_up(0, 1)
-            woven("wt", (1, 0), "one")
-            turn(1, 0, [4, 5])
-            woven("wt", (1, 1), "one")
-            turn(1, 1, [6, 0])
-            up_group(0, 0, [1, 2, 3, 4])
-            group("vgrp", [(0, 1), (1, 1)], WOVEN, BF16, "two")
-            weave_v(0, 1)
-            weave_v(1, 1)
-            quant_up(1, 0)
-            quant_up(1, 1)
-            w2_piece("c", [0, 1], [3], "one")
+            quant_v(0, 0, 1)
+            quant_v(0, 1, 2)
+            w2_piece("c", [0], [3, 4], 6)
             weave_w2("V", "c")
-            group("wt", [(2, 0), (2, 1)], WOVEN, BF16, "gate_a")
-            turn(2, 0, [5, 6])
-            turn(2, 1, [0, 1])
-            up_group(0, 1, [2, 3, 4, 5])
-            quant_v_both(1)
-            part_words(3, 1, "last")
-            quant_up_both(2)
+            quant_up(0, 0, 1)
+            quant_up(0, 1, 2)
             quant_w2("c")
-            w2_piece("a", [0, 1], [0, 1, 2], "gate_a")
+            stage(("wt", 1), 7, [2 * KP, T])
+            turn(1, 0, [4, 5])
+            empty_turned(1, 0)
+            turn(1, 1, [6, 0])
+            empty_turned(1, 1)
+            nc.scalar.copy(out=beta32[:], in_=beta_bf[:])
+            stage(("vflat", 0, 1), 0, flat)
+            stage(("vflat", 1, 1), 1, flat)
+            stage(("v", 1), 2, [2 * BANK, T])
+            for c in range(NV):
+                for t in range(T):
+                    widen("S" if (c, t) == (1, 3) else "V", c, 1, t)
+            up(0, 0, [1, 2, 3, 4])
+            sigmoids(0, 0)
+            beta_to_bank()
+            quant_up(1)
+            weave_v("V", 0, 1)
+            weave_v("V", 1, 1)
+            stage(("wt", 2), 4, [2 * KP, T])
+            turn(2, 0, [5, 6])
+            empty_turned(2, 0)
+            turn(2, 1, [0, 1])
+            empty_turned(2, 1)
+            up(0, 1, [2, 3, 4, 5])
+            sigmoids(0, 1)
+            quant_v(1, 0, 1)
+            quant_up(2)
+            quant_v(1, 1, 2)
+            w2_piece("a", [0, 1], [0, 1, 2], 4)
             weave_w2("G", "a")
-            group("h", [(0, 0), (0, 1)], WOVEN, BF16, "gate_b")
+            h_piece("p01", [(0, 0, 0, BANK), (0, 1, 0, BANK)], 9)
             scale_h(0, 0)
             scale_h(0, 1)
-            group("wt", [(3, 0), (3, 1)], WOVEN, BF16, "two")
+            stage(("wt", 3), 7, [2 * KP, T])
             turn(3, 0, [6, 0])
+            empty_turned(3, 0)
             turn(3, 1, [1, 2])
-            up_group(0, 2, [3, 4, 5, 6])
-            up_group(1, 0, [0, 1, 2, 3])
-            quant_up_both(3)
-            quant_w2("a", 0, 3 * P)
-            quant_h_both(0, 0)
-            quant_w2("a", 3 * P, 6 * P)
-            w2_piece("b", [2, 3], [0, 1, 2, 3, 4], "gate_b")
+            empty_turned(3, 1)
+            up(0, 2, [3, 4, 5, 6])
+            sigmoids(0, 2)
+            up(1, 0, [0, 1, 2, 3])
+            sigmoids(1, 0)
+            quant_up(3)
+            quant_w2("a", 0, 4)
+            quant_h("p01")
+            quant_w2("a", 4, 6)
+            w2_piece("b", [2, 3], [0, 1, 2, 3, 4], 9)
             weave_w2("G", "b")
-            woven("h", (0, 2), "one")
-            woven("h", (0, 3), "two")
-            woven("h", (1, 0), "one")
+            h_piece("p2", [(0, 2, 0, BANK)], 0)
+            h_piece("p3", [(0, 3, 0, BANK)], 1)
+            h_piece("b01", [(1, 0, 0, HALF), (1, 1, 0, HALF)], 2)
             scale_h(0, 2)
-            up_group(1, 1, [4, 5, 6, 0])
             scale_h(1, 0)
-            up_group(0, 3, [1, 2, 3, 4])
-            scale_h(0, 3)
-            up_group(1, 2, [5, 6, 0, 1])
-            w2_piece("d", [0, 1], [4], "gate_a")
-            for t, b in enumerate([2, 3, 4, 5]):
-                for c in range(NV):
-                    up_pass(1, 3, t, c, b)
-                sigmoid(1, 3, t)
-                if t == 1:
-                    weave_w2("S", "d")
-            quant_h(0, 2)
-            quant_w2("b", 0, 4 * P)
-            quant_h(0, 3)
-            quant_w2("b", 4 * P, 8 * P)
-            quant_w2("d")
-            quant_w2("b", 8 * P, 10 * P)
-            quant_h(1, 0)
-
-            w2_piece("e", [0, 1], [5], "gate_b")
-            weave_w2("G", "e")
-            woven("h", (1, 1), "gate_c")
+            up(1, 1, [4, 5, 6, 0])
+            sigmoids(1, 1)
             scale_h(1, 1)
-            for m, b in zip(range(4), [6, 0, 1, 2]):
-                open_tile(0, m, b)
-            down(0, range(4), [0, 1])
-            down(0, range(4), [2])
-            flat("hflat", (1, 3))
-            woven("h", (1, 3), "last")
-            scale_h_rows(1, 3, [0, 1, 2])
-            for m in range(4):
-                down(0, [m], [3])
-                finish("S", 0, m)
-            scale_h_rows(1, 3, [3])
-            quant_w2("e")
-            quant_h(1, 1)
-            w2_piece("f", [2, 3], [5], "gate_b")
-            weave_w2("G", "f")
-            woven("h", (1, 2), "one")
+            up(0, 3, [1, 2, 3, 4])
+            sigmoids(0, 3)
+            scale_h(0, 3)
+            up(1, 2, [5, 6, 0, 1])
+            sigmoids(1, 2)
+            up(1, 3, [2, 3, 4, 5])
+            sigmoids(1, 3)
+            w2_piece("d", [1], [3, 4], 6)
+            weave_w2("S", "d")
+            w2_piece("e", [0, 1], [5], 7)
+            weave_w2("S", "e")
+            quant_h("p2")
+            quant_w2("b", 0, 4)
+            quant_h("p3")
+            quant_w2("b", 4, 8)
+            quant_h("b01")
+            quant_w2("b", 8, 10)
+            quant_w2("d")
+            w2_piece("g6a", [0, 1], [6], 6)
+            weave_w2("G", "g6a")
+            h_piece("b23", [(1, 2, 0, HALF), (1, 3, 0, HALF)], 0)
             scale_h(1, 2)
-            open_tile(0, 4, 3)
-            down(0, [4], range(NH))
-            finish("S", 0, 4)
-            weave_h("S", 1, 3)
+            scale_h(1, 3)
+            for m, b in zip(range(5), [6, 0, 1, 2, 3]):
+                open_tile(0, m, b)
+            down(0, range(3), [0, 1])
+            down(0, [3, 4], [0])
+            down(0, range(4), [2])
+            w2_piece("f", [2, 3], [5], 8)
+            for m in range(5):
+                down(0, [m], [[3], [3], [3], [3, 1], [1, 2, 3]][m])
+                if m == 4:
+                    weave_w2("S", "f")
+                finish("S", 0, m)
             for m, b in zip(range(5), [4, 5, 6, 0, 1]):
-                open_tile(1, m, b)
-            down(1, range(5), [0])
+                open_tile(1, m, b, 0, HALF)
+            down(1, range(5), [0, 1])
+            quant_w2("e")
             open_tile(0, 5, 2)
             down(0, [5], [0, 1])
-            down(1, range(5), [1])
+            quant_h("b23")
+            quant_w2("g6a")
             quant_w2("f")
-            open_tile(1, 5, 3)
-            down(1, [5], [0, 1])
+            w2_piece("g7a", [0, 1], [7], 8)
+            weave_w2("G", "g7a")
+            h_piece("c01", [(1, 0, HALF, BANK), (1, 1, HALF, BANK)], 1)
+            scale_h(1, 0, HALF)
+            scale_h(1, 1, HALF)
+            w2_piece("s6b", [2, 3], [6], 7)
+            weave_w2("S", "s6b")
+            for m in range(5):
+                down(1, [m], [2, 3])
+                finish("S", 1, m)
+            w2_piece("s7b", [2, 3], [7], 9)
+            weave_w2("S", "s7b")
             down(0, [5], [2, 3])
             finish("S", 0, 5)
-            quant_h(1, 2)
-            quant_h(1, 3)
-            w2_piece("r6", range(NH), [6], "two")
-            weave_w2("V", "r6")
-            w2_piece("r7", range(NH), [7], "gate_b")
-            weave_w2("V", "r7", 0, 32)
-            quant_w2("r6")
-            weave_w2("V", "r7", 32, P)
-            down(1, range(3), [2])
+            open_tile(1, 5, 3, 0, HALF)
+            down(1, [5], range(NH))
+            finish("S", 1, 5)
+            open_tile(0, 6, 4)
+            open_tile(1, 6, 5, 0, HALF)
+            down(0, [6], [0, 1])
+            down(1, [6], [0, 1])
+            quant_w2("s6b")
+            quant_h("c01")
+            quant_w2("g7a")
+            quant_w2("s7b")
+            h_piece("c23", [(1, 2, HALF, BANK), (1, 3, HALF, BANK)], 2)
+            scale_h(1, 2, HALF)
+            scale_h(1, 3, HALF)
+            down(0, [6], [2, 3])
+            finish("S", 0, 6)
+            down(1, [6], [2, 3])
+            finish("S", 1, 6)
+            for m, b in zip(range(5), [0, 1, 3, 4, 5]):
+                open_tile(1, m, b, HALF, BANK, HALF)
+            down(1, range(2), [0, 1], HALF)
+            open_tile(0, 7, 6)
+            down(0, [7], range(NH))
+            finish("S", 0, 7)
+            open_tile(1, 7, 2, 0, HALF)
+            down(1, [7], range(NH))
+            finish("S", 1, 7)
+            down(1, range(2, 5), [0, 1], HALF)
+            quant_h("c23", 0, HALF)
+            quant_h("c23", HALF, BANK)
+            down(1, range(2), [2], HALF)
             for m in range(5):
-                down(1, [m], [3] if m < 3 else [2, 3])
-                finish("S", 1, m)
-            quant_w2("r7")
-            down(1, [5], [2, 3])
-            finish("V", 1, 5)
-            for n, m, b in [(0, 6, 7), (1, 6, 2)]:
-                open_tile(n, m, b)
-                down(n, [m], range(NH))
-                finish("VS"[n], n, m)
-            for n, first, last, b, e in [(0, 0, 256, 4, "S"), (0, 256, 512, 5, "V"), (1, 0, 256, 6, "S"), (1, 256, 384, 0, "V"), (1, 384, 512, 1, "S")]:
-                open_tile(n, 7, b, first, last)
-                down(n, [7], range(NH), first)
-                finish(e, n, 7, first, nc.scalar if last == BANK and n == 1 else nc.sync)
+                down(1, [m], [3] if m < 2 else [2, 3], HALF)
+                finish("SV"[m % 2], 1, m, HALF)
+            for m, b in [(5, 7), (6, 6)]:
+                open_tile(1, m, b, HALF, BANK, HALF)
+                down(1, [m], range(NH), HALF)
+                finish("SV"[m % 2], 1, m, HALF)
+            for first, b, e, queue in [(HALF, 2, "V", nc.sync), (HALF + P, 0, "S", nc.scalar)]:
+                open_tile(1, 7, b, first, first + P, HALF)
+                down(1, [7], range(NH), first)
+                finish(e, 1, 7, first, queue)

@@ -63,7 +63,11 @@ def tile_rbm_mean_field_reconstruction_s7_kernel(tc, v_bytes, v_scale, w, beta, 
             return slice(n * BANK, (n + 1) * BANK)
 
         def stage(key, slot, shape, dtype=BF16):
-            live[key] = arena.tile([P] + shape, dtype, name="at%d" % slot, align_bytes=64, offset=slot * SLOT)
+            tile = arena.tile([P, shape[0] * shape[1] * (shape[2] if len(shape) == 3 else 1)], dtype, name="at%d" % slot, align_bytes=64, offset=slot * SLOT)
+            if len(shape) == 2:
+                live[key] = tile[:].rearrange("p (a b) -> p a b", b=shape[1])
+            else:
+                live[key] = tile[:].rearrange("p (a b c) -> p a b c", b=shape[1], c=shape[2])
             return live[key]
 
         def new_bank(key, b):
@@ -262,10 +266,11 @@ def tile_rbm_mean_field_reconstruction_s7_kernel(tc, v_bytes, v_scale, w, beta, 
                 load_w(g, 1)
             nc.sync.dma_start(out=beta_bf[:], in_=beta.rearrange("(g p t) o -> p g (t o)", p=P, t=T))
             load_v(0, 1)
+            load_w(2, 0)
+            load_w(2, 1)
             load_v(1, 1)
-            for g in range(2, NH):
-                load_w(g, 0)
-                load_w(g, 1)
+            load_w(3, 0)
+            load_w(3, 1)
             warm_up(BANK, 6)
             warm_up(BANK, 6)
             stage(("vflat", 0, 0), 0, flat)
@@ -294,18 +299,20 @@ def tile_rbm_mean_field_reconstruction_s7_kernel(tc, v_bytes, v_scale, w, beta, 
             empty_turned(1, 0)
             turn(1, 1, [6, 0])
             empty_turned(1, 1)
-            nc.scalar.copy(out=beta32[:], in_=beta_bf[:])
+            nc.vector.tensor_copy(out=beta32[:], in_=beta_bf[:])
             stage(("vflat", 0, 1), 0, flat)
             stage(("vflat", 1, 1), 1, flat)
             stage(("v", 1), 2, [2 * BANK, T])
-            for c in range(NV):
-                for t in range(T):
-                    widen("S" if (c, t) == (1, 3) else "V", c, 1, t)
+            for t in range(T):
+                widen("V", 0, 1, t)
             up(0, 0, [1, 2, 3, 4])
             sigmoids(0, 0)
             beta_to_bank()
             quant_up(1)
             weave_v("V", 0, 1)
+            for t in range(T):
+                widen("VVVS"[t], 1, 1, t)
+            quant_v(1, 0, 1)
             weave_v("V", 1, 1)
             stage(("wt", 2), 4, [2 * KP, T])
             turn(2, 0, [5, 6])
@@ -314,7 +321,6 @@ def tile_rbm_mean_field_reconstruction_s7_kernel(tc, v_bytes, v_scale, w, beta, 
             empty_turned(2, 1)
             up(0, 1, [2, 3, 4, 5])
             sigmoids(0, 1)
-            quant_v(1, 0, 1)
             quant_up(2)
             quant_v(1, 1, 2)
             w2_piece("a", [0, 1], [0, 1, 2], 4)

@@ -22,6 +22,7 @@ NV = V // KP
 NH = H // KP
 BANK = 512
 HALF = 256
+SPLIT = 128
 BETA_BANK = 7
 RUN = 4
 SLOT = 4096
@@ -276,24 +277,24 @@ def tile_rbm_mean_field_reconstruction_s7_kernel(tc, v_bytes, v_scale, w, beta, 
             stage(("vflat", 0, 0), 0, flat)
             stage(("vflat", 1, 0), 1, flat)
             stage(("v", 0), 2, [2 * BANK, T])
-            for c, t, e in [(0, 0, "V"), (0, 1, "S"), (0, 2, "V"), (0, 3, "S"), (1, 0, "V"), (1, 1, "V"), (1, 2, "S"), (1, 3, "S")]:
-                widen(e, c, 0, t)
-            weave_v("V", 0, 0)
-            weave_v("S", 1, 0, 256, 512)
-            weave_v("V", 1, 0, 0, 256)
+            for c in range(NV):
+                for t in range(T):
+                    widen(["VSVS", "VSVV"][c][t], c, 0, t)
+            weave_v("S", 0, 0, SPLIT, BANK)
+            weave_v("V", 0, 0, 0, SPLIT)
+            weave_v("V", 1, 0)
             stage(("wt", 0), 4, [2 * KP, T])
             turn(0, 0, [0, 1])
             empty_turned(0, 0)
             turn(0, 1, [2, 3])
             empty_turned(0, 1)
             warm_up(BANK // 4, 6)
-            quant_v(0, 0, 1)
-            quant_v(0, 1, 2)
             w2_piece("c", [0], [3, 4], 6)
             weave_w2("V", "c")
+            quant_v(0)
             quant_up(0, 0, 1)
-            quant_up(0, 1, 2)
             quant_w2("c")
+            quant_up(0, 1, 2)
             stage(("wt", 1), 7, [2 * KP, T])
             turn(1, 0, [4, 5])
             empty_turned(1, 0)

from contextlib import ExitStack

import concourse.mybir as mybir
from concourse.masks import make_identity

V, H, B = 1024, 2048, 1024
FLOPS = 2 * 2 * H * V * B

F32 = mybir.dt.float32
BF16 = mybir.dt.bfloat16
U32 = mybir.dt.uint32
U8 = mybir.dt.uint8
FP8 = mybir.dt.float8_e4m3fn
FP8X4 = mybir.dt.float8_e4m3fn_x4
ACT = mybir.ActivationFunctionType
ALU = mybir.AluOpType

P = 128
T = 4
KP = P * T
NV = V // KP
NH = H // KP
BANK = 512
HALF = 256
SPLIT = 128
BETA_BANK = 7
RUN = 4
SLOT = 4096
SIG_BUFS = 5
RES_BUFS = 10


def tile_rbm_mean_field_reconstruction_s7_kernel(tc, v_bytes, v_scale, w, beta, out):
    nc = tc.nc
    with ExitStack() as ctx:
        keep = ctx.enter_context(tc.tile_pool(name="keep", bufs=1))
        rot = ctx.enter_context(tc.tile_pool(name="rot", bufs=1))
        arena = ctx.enter_context(tc.tile_pool(name="arena", bufs=1))
        psum = ctx.enter_context(tc.psum_pool(name="psum", bufs=1))

        w_view = w.rearrange("(g p t) v -> g p (t v)", p=P, t=T)
        v_view = v_bytes.rearrange("(c p t) n -> c p t n", p=P, t=T)
        vs = keep.tile([P, NV, T], F32, name="vs")
        beta_bf = keep.tile([P, NH, T], BF16, name="beta_bf")
        beta32 = keep.tile([P, NH, T], F32, name="beta32")
        ident = keep.tile([P, P], F32, name="ident")
        v_codes = keep.tile([P, 2, NV * BANK], U32, name="v_codes", align_bytes=64)
        v_sc = keep.tile([P, 2, NV * BANK], U8, name="v_sc", align_bytes=64)
        wt_codes = keep.tile([P, NH, 2 * KP], U32, name="wt_codes", align_bytes=64)
        wt_sc = keep.tile([P, NH, 2 * KP], U8, name="wt_sc", align_bytes=64)
        w2_codes = keep.tile([P, NH * V], U32, name="w2_codes", align_bytes=64)
        w2_sc = keep.tile([P, NH * V], U8, name="w2_sc", align_bytes=64)
        h_codes = keep.tile([P, 2 * NH * BANK], U32, name="h_codes", align_bytes=64)
        h_sc = keep.tile([P, 2 * NH * BANK], U8, name="h_sc", align_bytes=64)
        w_rows = keep.tile([P, NH * T * V], BF16, name="w_rows", align_bytes=64)
        zeros = keep.tile([P, BANK], F32, name="zeros")
        live = {}
        used = {"w2": 0, "h": 0}
        copy_on = {"V": nc.vector.tensor_copy, "S": nc.scalar.copy}
        w_gtv = w_rows[:].rearrange("p (g t v) -> p g t v", g=NH, t=T)
        w_gvt = w_rows[:].rearrange("p (g t v) -> p g v t", g=NH, t=T)

        def samples(n):
            return slice(n * BANK, (n + 1) * BANK)

        def stage(key, slot, shape, dtype=BF16):
            tile = arena.tile([P, shape[0] * shape[1] * (shape[2] if len(shape) == 3 else 1)], dtype, name="at%d" % slot, align_bytes=64, offset=slot * SLOT)
            if len(shape) == 2:
                live[key] = tile[:].rearrange("p (a b) -> p a b", b=shape[1])
            else:
                live[key] = tile[:].rearrange("p (a b c) -> p a b c", b=shape[1], c=shape[2])
            return live[key]

        def new_bank(key, b):
            live[key] = psum.tile([P, BANK], F32, name="bank%d" % b)
            return live[key]

        def runs_out(dst):
            return dst.rearrange("p (c i) t -> p c t i", i=RUN)

        def runs_in(src):
            return src.rearrange("p t (c i) -> p c t i", i=RUN)

        def quantise(codes, scales, grouped):
            nc.vector.quantize_mx(out=codes.bitcast(FP8X4), scales=scales, in_=grouped.rearrange("p n t -> p (n t)"))

        def load_v(c, n, first=0, last=T):
            raw = keep.tile([P, last - first, BANK], U8, name="v_raw%d_%d_%d" % (c, n, first), align_bytes=64)
            nc.sync.dma_start(out=raw[:], in_=v_view[c][:, first:last, samples(n)])
            for t in range(first, last):
                live["vraw", c, n, t] = raw[:, t - first, :]

        def load_v_rows(c, first, last):
            raw = keep.tile([P, last - first, B], U8, name="v_rows%d_%d" % (c, first), align_bytes=64)
            nc.sync.dma_start(out=raw[:], in_=v_view[c][:, first:last, :])
            for t in range(first, last):
                for n in range(2):
                    live["vraw", c, n, t] = raw[:, t - first, samples(n)]

        def load_w(g, a):
            first = (g * T + 2 * a) * V
            nc.sync.dma_start(out=w_rows[:, first : first + 2 * V], in_=w_view[g][:, 2 * a * V : 2 * (a + 1) * V])

        def widen(e, c, n, t):
            src = live["vraw", c, n, t].bitcast(FP8)
            dst = live["vflat", c, n][:, t, :]
            if e == "V":
                nc.vector.tensor_scalar(out=dst, in0=src, scalar1=vs[:, c, t : t + 1], scalar2=None, op0=ALU.mult)
            else:
                nc.scalar.activation(out=dst, in_=src, func=ACT.Copy, scale=vs[:, c, t : t + 1])

        def weave_v(e, c, n, first=0, last=BANK):
            copy_on[e](out=runs_out(live["v", n][:, c * BANK + first : c * BANK + last, :]), in_=runs_in(live["vflat", c, n][:, :, first:last]))

        def quant_v(n, first=0, last=NV):
            cols = slice(first * BANK, last * BANK)
            quantise(v_codes[:, n, cols], v_sc[:, n, cols], live["v", n][:, cols, :])

        def part_words(g, a, slot):
            parted = stage(("parted", g, a), slot, [2 * NV, 2, P], F32)
            first = (g * T + 2 * a) * V // 2
            nc.vector.tensor_copy(out=parted[:], in_=w_rows[:].bitcast(F32)[:, first : first + V].rearrange("p (k m u) -> p k u m", m=P, u=2))

        def turn(g, a, banks):
            words = w_rows[:].bitcast(F32)
            for c in range(NV):
                bank = new_bank(("tb", g, a, c), banks[c])
                for i in range(2):
                    first = (g * T + 2 * a + i) * V // 2 + c * KP // 2
                    for u in range(2):
                        j = (2 * i + u) * P
                        if ("parted", g, a) in live:
                            rows = live["parted", g, a][:, 2 * i + c, u, :]
                        else:
                            rows = words[:, first + u : first + 2 * P : 2]
                        nc.tensor.transpose(bank[:, j : j + P], rows, ident[:])

        def empty_turned(g, a, engines="SS"):
            dst = live["wt", g][:, a * KP : (a + 1) * KP, :].rearrange("p m t -> p (m t)").bitcast(F32).rearrange("p (c i m u) -> p c i m u", c=NV, i=2, u=2)
            for c in range(NV):
                copy_on[engines[c]](out=dst[:, c], in_=live["tb", g, a, c][:].rearrange("p (i u m) -> p i m u", i=2, u=2))

        def quant_up(g, first=0, last=2):
            cols = slice(first * KP, last * KP)
            quantise(wt_codes[:, g, cols], wt_sc[:, g, cols], live["wt", g][:, cols, :])

        def w2_piece(name, gs, ms, slot):
            stage(("w2", name), slot, [len(gs), len(ms) * P, T])
            live["w2span", name] = (slice(gs[0], gs[-1] + 1), ms[0] * P, used["w2"])
            for g in gs:
                for m in ms:
                    live["w2col", g, m] = used["w2"]
                    used["w2"] = used["w2"] + P

        def weave_w2(e, name, first=0, last=None):
            tile = live["w2", name]
            gs, v0, base = live["w2span", name]
            last = tile.shape[2] if last is None else last
            if e == "G":
                nc.gpsimd.tensor_scalar(out=tile[:, :, first:last, :], in0=w_gvt[:, gs, v0 + first : v0 + last, :],
                                        scalar1=1.0, scalar2=0.0, op0=ALU.mult, op1=ALU.add)
            else:
                copy_on[e](out=tile[:, :, first:last, :].rearrange("p g (c i) t -> p g c t i", i=RUN),
                           in_=w_gtv[:, gs, :, v0 + first : v0 + last].rearrange("p g t (c i) -> p g c t i", i=RUN))

        def quant_w2(name, first=0, last=None):
            words = live["w2", name][:].rearrange("p g v t -> p (g v) t")
            base = live["w2span", name][2]
            last = words.shape[1] // P if last is None else last
            cols = slice(base + first * P, base + last * P)
            quantise(w2_codes[:, cols], w2_sc[:, cols], words[:, first * P : last * P, :])

        def warm_up(cols, b):
            bank = new_bank("warm", b)
            nc.tensor.matmul(out=bank[:, 0:cols], lhsT=zeros[:, 0:P], rhs=zeros[:, 0:cols], start=True, stop=True)

        def beta_to_bank():
            bank = new_bank("factors", BETA_BANK)
            nc.tensor.matmul(out=bank[:, 0 : NH * T], lhsT=ident[:], rhs=beta32[:].rearrange("p g t -> p (g t)"), start=True, stop=True)
            live["beta"] = bank[:, 0 : NH * T].rearrange("p (g t) -> p g t", t=T)

        def up(n, g, banks, ts=range(T)):
            for t, b in zip(ts, banks):
                bank = new_bank(("mb", n, g, t), b)
                for c in range(NV):
                    first = (t // 2) * KP + c * 2 * P + (t % 2) * P
                    m = slice(first, first + P)
                    nc.tensor.matmul_mx(out=bank[:], lhsT=wt_codes[:, g, m].bitcast(FP8X4), lhsT_scale=wt_sc[:, g, m],
                                        rhs=v_codes[:, n, samples(c)].bitcast(FP8X4), rhs_scale=v_sc[:, n, samples(c)],
                                        start=(c == 0), stop=(c == NV - 1))

        def sigmoids(n, g, ts=range(T)):
            if ("sig", n, g) not in live:
                live["sig", n, g] = rot.tile([P, T, BANK], F32, name="sig", align_bytes=64, bufs=SIG_BUFS)
            for t in ts:
                nc.scalar.activation(out=live["sig", n, g][:, t, :], in_=live["mb", n, g, t][:], func=ACT.Sigmoid, scale=beta32[:, g, t : t + 1])

        def h_piece(name, parts, slot):
            tile = stage(("h", name), slot, [sum(last - first for n, g, first, last in parts), T])
            live["hbase", name] = used["h"]
            at = 0
            for n, g, first, last in parts:
                live["h", n, g, first] = tile[:, at : at + last - first, :]
                live["hcol", n, g, first] = used["h"] + at
                at = at + last - first
            used["h"] = used["h"] + at

        def scale_h(n, g, first=0, skip=0, stop=None):
            dst = live["h", n, g, first]
            stop = dst.shape[1] if stop is None else stop
            nc.vector.tensor_tensor(
                out=runs_out(dst[:, skip:stop, :]), in0=runs_in(live["sig", n, g][:, :, first + skip : first + stop]),
                in1=live["beta"][:, g, :].unsqueeze(1).unsqueeze(3).to_broadcast([P, (stop - skip) // RUN, T, RUN]), op=ALU.mult)

        def scale_h_rows(n, g, ts=range(T), first=0, last=BANK):
            for t in ts:
                nc.scalar.activation(out=live["hflat", n, g][:, t, first:last], in_=live["sig", n, g][:, t, first:last],
                                     func=ACT.Copy, scale=beta32[:, g, t : t + 1])

        def weave_h(e, n, g, first=0, skip=0, stop=None):
            dst = live["h", n, g, first]
            stop = dst.shape[1] if stop is None else stop
            copy_on[e](out=runs_out(dst[:, skip:stop, :]), in_=runs_in(live["hflat", n, g][:, :, first + skip : first + stop]))

        def quant_h(name, first=0, last=None):
            tile = live["h", name]
            last = tile.shape[1] if last is None else last
            cols = slice(live["hbase", name] + first, live["hbase", name] + last)
            quantise(h_codes[:, cols], h_sc[:, cols], tile[:, first:last, :])

        def open_tile(n, m, b, first=0, last=BANK, base=0):
            new_bank(("nb", n, m, first), b)
            live["todo", n, m, first] = NH
            live["span", n, m, first] = (last - first, base)

        def down(n, ms, gs, first=0):
            for m in ms:
                width, base = live["span", n, m, first]
                for g in gs:
                    at = live["hcol", n, g, base] + first - base
                    cols = slice(at, at + width)
                    mc = slice(live["w2col", g, m], live["w2col", g, m] + P)
                    left = live["todo", n, m, first]
                    nc.tensor.matmul_mx(out=live["nb", n, m, first][:, 0:width], lhsT=w2_codes[:, mc].bitcast(FP8X4), lhsT_scale=w2_sc[:, mc],
                                        rhs=h_codes[:, cols].bitcast(FP8X4), rhs_scale=h_sc[:, cols],
                                        start=(left == NH), stop=(left == 1))
                    live["todo", n, m, first] = left - 1

        def finish(e, n, m, first=0, queue=nc.sync):
            width = live["span", n, m, first][0]
            res = rot.tile([P, BANK], F32, name="res", align_bytes=64, bufs=RES_BUFS)
            copy_on[e](out=res[:, 0:width], in_=live["nb", n, m, first][:, 0:width])
            queue.dma_start(out=out[m * P : (m + 1) * P, n * BANK + first : n * BANK + first + width], in_=res[:, 0:width])

        flat = [T, BANK]
        with tc.manual_schedule():
            nc.scalar.dma_start(out=vs[:], in_=v_scale.rearrange("(c p t) o -> p c (t o)", p=P, t=T))
            make_identity(nc, ident[:])
            dummy = keep.tile([P, 1], F32, name="dummy")
            nc.vector.memset(zeros[:], 0.0)
            nc.scalar.activation(out=dummy[:], in_=zeros[:, 0:1], func=ACT.Sigmoid)
            load_v(0, 0, 0, 2)
            load_v(0, 0, 2, 4)
            load_v(1, 0)
            for g in range(2):
                load_w(g, 0)
                load_w(g, 1)
            nc.sync.dma_start(out=beta_bf[:], in_=beta.rearrange("(g p t) o -> p g (t o)", p=P, t=T))
            load_v(0, 1)
            load_w(2, 0)
            load_w(2, 1)
            load_v(1, 1)
            load_w(3, 0)
            load_w(3, 1)
            warm_up(BANK, 6)
            warm_up(BANK, 6)
            stage(("vflat", 0, 0), 0, flat)
            stage(("vflat", 1, 0), 1, flat)
            stage(("v", 0), 2, [2 * BANK, T])
            for c in range(NV):
                for t in range(T):
                    widen(["VSVS", "VSVV"][c][t], c, 0, t)
            weave_v("S", 0, 0, SPLIT, BANK)
            weave_v("V", 0, 0, 0, SPLIT)
            weave_v("V", 1, 0)
            stage(("wt", 0), 4, [2 * KP, T])
            turn(0, 0, [0, 1])
            empty_turned(0, 0)
            turn(0, 1, [2, 3])
            empty_turned(0, 1)
            warm_up(BANK // 4, 6)
            w2_piece("c", [0], [3, 4], 6)
            weave_w2("V", "c")
            quant_v(0)
            quant_up(0, 0, 1)
            quant_w2("c")
            quant_up(0, 1, 2)
            stage(("wt", 1), 7, [2 * KP, T])
            turn(1, 0, [4, 5])
            empty_turned(1, 0)
            turn(1, 1, [6, 0])
            empty_turned(1, 1)
            nc.vector.tensor_copy(out=beta32[:], in_=beta_bf[:])
            stage(("vflat", 0, 1), 0, flat)
            stage(("vflat", 1, 1), 1, flat)
            stage(("v", 1), 2, [2 * BANK, T])
            for t in range(T):
                widen("V", 0, 1, t)
            up(0, 0, [1, 2, 3, 4])
            sigmoids(0, 0)
            beta_to_bank()
            quant_up(1)
            weave_v("V", 0, 1)
            for t in range(T):
                widen("VVVS"[t], 1, 1, t)
            quant_v(1, 0, 1)
            weave_v("V", 1, 1)
            stage(("wt", 2), 4, [2 * KP, T])
            turn(2, 0, [5, 6])
            empty_turned(2, 0)
            turn(2, 1, [0, 1])
            empty_turned(2, 1)
            up(0, 1, [2, 3, 4, 5])
            sigmoids(0, 1)
            quant_up(2)
            quant_v(1, 1, 2)
            w2_piece("a", [0, 1], [0, 1, 2], 4)
            weave_w2("G", "a")
            h_piece("p01", [(0, 0, 0, BANK), (0, 1, 0, BANK)], 9)
            scale_h(0, 0)
            scale_h(0, 1)
            stage(("wt", 3), 7, [2 * KP, T])
            turn(3, 0, [6, 0])
            empty_turned(3, 0)
            turn(3, 1, [1, 2])
            empty_turned(3, 1)
            up(0, 2, [3, 4, 5, 6])
            sigmoids(0, 2)
            up(1, 0, [0, 1, 2, 3])
            sigmoids(1, 0)
            quant_up(3)
            quant_w2("a", 0, 4)
            quant_h("p01")
            quant_w2("a", 4, 6)
            w2_piece("b", [2, 3], [0, 1, 2, 3, 4], 9)
            weave_w2("G", "b")
            h_piece("p2", [(0, 2, 0, BANK)], 0)
            h_piece("p3", [(0, 3, 0, BANK)], 1)
            h_piece("b01", [(1, 0, 0, HALF), (1, 1, 0, HALF)], 2)
            scale_h(0, 2)
            scale_h(1, 0)
            up(1, 1, [4, 5, 6, 0])
            sigmoids(1, 1)
            scale_h(1, 1)
            up(0, 3, [1, 2, 3, 4])
            sigmoids(0, 3)
            scale_h(0, 3)
            up(1, 2, [5, 6, 0, 1])
            sigmoids(1, 2)
            up(1, 3, [2, 3, 4, 5])
            sigmoids(1, 3)
            w2_piece("d", [1], [3, 4], 6)
            weave_w2("S", "d")
            w2_piece("e", [0, 1], [5], 7)
            weave_w2("S", "e")
            quant_h("p2")
            quant_w2("b", 0, 4)
            quant_h("p3")
            quant_w2("b", 4, 8)
            quant_h("b01")
            quant_w2("b", 8, 10)
            quant_w2("d")
            w2_piece("g6a", [0, 1], [6], 6)
            weave_w2("G", "g6a")
            h_piece("b23", [(1, 2, 0, HALF), (1, 3, 0, HALF)], 0)
            scale_h(1, 2)
            scale_h(1, 3)
            for m, b in zip(range(5), [6, 0, 1, 2, 3]):
                open_tile(0, m, b)
            down(0, range(3), [0, 1])
            down(0, [3, 4], [0])
            down(0, range(4), [2])
            w2_piece("f", [2, 3], [5], 8)
            for m in range(5):
                down(0, [m], [[3], [3], [3], [3, 1], [1, 2, 3]][m])
                if m == 4:
                    weave_w2("S", "f")
                finish("S", 0, m)
            for m, b in zip(range(5), [4, 5, 6, 0, 1]):
                open_tile(1, m, b, 0, HALF)
            down(1, range(5), [0, 1])
            quant_w2("e")
            open_tile(0, 5, 2)
            down(0, [5], [0, 1])
            quant_h("b23")
            quant_w2("g6a")
            quant_w2("f")
            w2_piece("g7a", [0, 1], [7], 8)
            weave_w2("G", "g7a")
            h_piece("c01", [(1, 0, HALF, BANK), (1, 1, HALF, BANK)], 1)
            scale_h(1, 0, HALF)
            scale_h(1, 1, HALF)
            w2_piece("s6b", [2, 3], [6], 7)
            weave_w2("S", "s6b")
            for m in range(5):
                down(1, [m], [2, 3])
                finish("S", 1, m)
            w2_piece("s7b", [2, 3], [7], 9)
            weave_w2("S", "s7b")
            down(0, [5], [2, 3])
            finish("S", 0, 5)
            open_tile(1, 5, 3, 0, HALF)
            down(1, [5], range(NH))
            finish("S", 1, 5)
            open_tile(0, 6, 4)
            open_tile(1, 6, 5, 0, HALF)
            down(0, [6], [0, 1])
            down(1, [6], [0, 1])
            quant_w2("s6b")
            quant_h("c01")
            quant_w2("g7a")
            quant_w2("s7b")
            h_piece("c23", [(1, 2, HALF, BANK), (1, 3, HALF, BANK)], 2)
            scale_h(1, 2, HALF)
            scale_h(1, 3, HALF)
            down(0, [6], [2, 3])
            finish("S", 0, 6)
            down(1, [6], [2, 3])
            finish("S", 1, 6)
            for m, b in zip(range(5), [0, 1, 3, 4, 5]):
                open_tile(1, m, b, HALF, BANK, HALF)
            down(1, range(2), [0, 1], HALF)
            open_tile(0, 7, 6)
            down(0, [7], range(NH))
            finish("S", 0, 7)
            open_tile(1, 7, 2, 0, HALF)
            down(1, [7], range(NH))
            finish("S", 1, 7)
            down(1, range(2, 5), [0, 1], HALF)
            quant_h("c23", 0, HALF)
            quant_h("c23", HALF, BANK)
            down(1, range(2), [2], HALF)
            for m in range(5):
                down(1, [m], [3] if m < 2 else [2, 3], HALF)
                finish("SV"[m % 2], 1, m, HALF)
            for m, b in [(5, 7), (6, 6)]:
                open_tile(1, m, b, HALF, BANK, HALF)
                down(1, [m], range(NH), HALF)
                finish("SV"[m % 2], 1, m, HALF)
            for first, b, e, queue in [(HALF, 2, "V", nc.sync), (HALF + P, 0, "S", nc.scalar)]:
                open_tile(1, 7, b, first, first + P, HALF)
                down(1, [7], range(NH), first)
                finish(e, 1, 7, first, queue)
